import numpy as np
import ml_dtypes


def mxq(x, axis, fmt="e4m3"):
    dtype, down = {"e4m3": (ml_dtypes.float8_e4m3fn, 7), "e5m2": (ml_dtypes.float8_e5m2, 14)}[fmt]
    v = np.moveaxis(np.asarray(x, np.float32).astype(ml_dtypes.bfloat16).astype(np.float64), axis, -1)
    blocks = v.reshape(v.shape[:-1] + (-1, 32))
    amax = np.abs(blocks).max(-1, keepdims=True)
    byte = np.maximum(np.where(amax > 0, np.frexp(amax)[1] - 1 + 127, 0) - down, 1)
    scale = np.exp2(byte - 127.0)
    codes = (blocks / scale).astype(np.float32).astype(dtype).astype(np.float64)
    return np.moveaxis((codes * scale).reshape(v.shape), -1, axis)


WIDE = False


def mx_kscale(k):
    if not WIDE:
        return np.ones(k)
    levels = np.array([10, -10, 5, -5, 0])
    if k % 512:
        return np.exp2(np.random.permutation(np.resize(levels, k // 32))).repeat(32)
    a = np.empty((k // 512, 16))
    for p in range(k // 512):
        a[p, :8] = np.random.permutation(np.resize(levels, 8))
        for g in range(8):
            far = levels[np.abs(levels - a[p, g]) >= 10]
            a[p, g + 8] = far[np.random.randint(len(far))]
    return np.exp2(a.ravel()).repeat(32)


def f64(x):
    return np.asarray(x).astype(np.float64)


def striped(idx):
    return np.tile(idx.reshape(-1, 16).T, (8, 1)).astype(np.uint16)


def unstriped(offs):
    return offs[:16].T.reshape(-1).astype(np.int64)


E2M1 = np.array([0.0, 0.5, 1.0, 1.5, 2.0, 3.0, 4.0, 6.0, -0.0, -0.5, -1.0, -1.5, -2.0, -3.0, -4.0, -6.0])


def pack_weight(w, fmt):
    k, n = w.shape
    w = f64(np.asarray(w, np.float32).astype(ml_dtypes.bfloat16)).reshape(k // 32, 32, n)
    amax = np.abs(w).max(1)
    if fmt == "e4m3":
        byte = np.frexp(amax)[1] - 1 + 127 - 7
    else:
        mant, ex = np.frexp(amax / 6.0)
        byte = np.where(mant > 0.5, ex, ex - 1) + 127
    byte = np.clip(np.where(amax > 0, byte, 1), 1, 254)
    scaled = (w * np.exp2(127.0 - byte)[:, None, :]).reshape(k, n).astype(np.float32)
    by_word = np.ascontiguousarray(scaled.reshape(k // 512, 128, 4, n).transpose(0, 1, 3, 2))
    if fmt == "e4m3":
        words = by_word.astype(ml_dtypes.float8_e4m3fn).view(np.uint8)
    else:
        c = by_word.astype(ml_dtypes.float4_e2m1fn).view(np.uint8) & 0xF
        words = (c[..., 0::2] | (c[..., 1::2] << 4)).reshape(k // 512, 128, 2 * n)
    return np.ascontiguousarray(words), np.ascontiguousarray(byte.astype(np.uint8).reshape(k // 512, 16, n))


def unpack_weight(words, scales, fmt):
    g, _, n = scales.shape
    words = np.ascontiguousarray(words).reshape(g, 128, n, -1)
    if fmt == "e4m3":
        vals = words.view(ml_dtypes.float8_e4m3fn).astype(np.float64)
    else:
        nib = np.empty((g, 128, n, 4), np.uint8)
        nib[..., 0::2] = words & 0xF
        nib[..., 1::2] = words >> 4
        vals = E2M1[nib]
    vals = vals * np.repeat(np.exp2(scales.astype(np.float64) - 127.0), 8, axis=1)[..., None]
    return vals.transpose(0, 1, 3, 2).reshape(g * 512, n)


def d_relu(v):
    return (v > 0).astype(np.float64)


K, T, E1, C1, E2, C2, H = 512, 512, 2, 256, 4, 128, 512
N = 512


def by_expert(wq, xq, E, C):
    return np.concatenate([wq[e].T @ xq[:, e * C:(e + 1) * C] for e in range(E)], axis=1)


def setup_inputs():
    n = np.random.standard_normal
    v = mx_kscale(N)
    u = mx_kscale(H)
    slots1, slots2 = np.random.permutation(T), np.random.permutation(T)
    dy = pack_weight(n((N, T)) * v[:, None], "e4m3")
    w1t = [pack_weight(m, "e2m1") for m in n((E1, H, K)) / np.sqrt(H) / u[None, :, None]]
    return {
        "dy_words": dy[0],
        "dy_scales": dy[1],
        "w2t": (n((E2, N, H)) / np.sqrt(N) / v[None, :, None] * u).astype(np.float32),
        "w1t_words": np.stack([m[0] for m in w1t]),
        "w1t_scales": np.stack([m[1] for m in w1t]),
        "a": (n((H, T))).astype(np.float32),
        "gate1": (np.tile(np.random.uniform(0.2, 1.0, T), (128, 1))).astype(np.float32),
        "gate2": (np.tile(np.random.uniform(0.2, 1.0, T), (128, 1))).astype(np.float32),
        "offs": striped(slots1),
        "offs2": striped(slots2),
    }


def reference(dy_words, dy_scales, w2t, w1t_words, w1t_scales, a, gate1, gate2, offs, offs2):
    w2tq = mxq(f64(w2t), 1, "e4m3")
    w1t = np.stack([unpack_weight(w1t_words[e], w1t_scales[e], "e2m1") for e in range(E1)])
    idx, idx2 = unstriped(offs), unstriped(offs2)
    gq = unpack_weight(dy_words, dy_scales, "e4m3")[:, idx2]
    dc = np.zeros((H, T))
    dc[:, idx2] = f64(gate2[:1]) * by_expert(w2tq, gq, E2, C2)
    da = f64(gate1[:1]) * dc[:, idx] * d_relu(f64(a))
    out = np.zeros((K, T))
    out[:, idx] = by_expert(w1t, mxq(da, 0, "e4m3"), E1, C1)
    return out

@@ -1,0 +1,236 @@
+from contextlib import ExitStack
+
+import concourse.mybir as mybir
+
+F32 = mybir.dt.float32
+BF16 = mybir.dt.bfloat16
+I32 = mybir.dt.int32
+U32 = mybir.dt.uint32
+U16 = mybir.dt.uint16
+U8 = mybir.dt.uint8
+FP8X4 = mybir.dt.float8_e4m3fn_x4
+FP4X4 = mybir.dt.float4_e2m1fn_x4
+MULT = mybir.AluOpType.mult
+ACT = mybir.ActivationFunctionType
+
+P = 128
+T = 512
+E1, C1 = 2, 256
+E2, C2 = 4, 128
+PACK = 4
+HALF = 256
+FLOPS = 2 * 2 * 512 * 512 * 512
+
+
+def tile_moe_seb_relu_kernel(
+    tc, dy_words, dy_scales, w2t, w1t_words, w1t_scales, a, gate1, gate2, offs, offs2, out
+):
+    nc = tc.nc
+    with ExitStack() as ctx:
+        lists = ctx.enter_context(tc.tile_pool(name="lists", bufs=1))
+        sb = ctx.enter_context(tc.tile_pool(name="sb", bufs=1))
+        psum = ctx.enter_context(tc.psum_pool(name="psum", bufs=8))
+
+        def fresh(name, shape, dtype, tag=None):
+            return sb.tile(shape, dtype, name=name, tag=tag or name, align_bytes=64)
+
+        def entries(lst, first, count):
+            return lst[:, first // 16 : (first + count) // 16]
+
+        list2 = lists.tile([P, T // 16], U16, name="list2")
+        list1 = lists.tile([P, T // 16], U16, name="list1")
+        dy_w = fresh("dy_w", [P, T], I32)
+        dy_s = fresh("dy_s", [P, T], U8)
+        w1_w = fresh("w1_w", [P, E1 * 1024], U8)
+        w1_s = fresh("w1_s", [P, E1 * T], U8)
+        nc.vector.memset(dy_s[:].bitcast(I32), 0)
+        nc.vector.memset(w1_s[:].bitcast(I32), 0)
+
+        nc.sync.dma_start(list2[:], offs2)
+        nc.sync.dma_start(dy_w[:], dy_words[0].rearrange("p t d -> p (t d)").bitcast(I32))
+        for r in range(4):
+            nc.sync.dma_start(dy_s[r:P:32, :].bitcast(I32), dy_scales[0, r:16:4, :].bitcast(I32))
+
+        raw = {}
+
+        def load_w2(f):
+            rows = w2t[f].rearrange("(p j) i -> p j i", j=PACK)
+            for h in range(2):
+                raw[f, h] = fresh(f"raw{f}{h}", [P, PACK, HALF], F32)
+                nc.sync.dma_start(raw[f, h][:], rows[:, :, h * HALF : (h + 1) * HALF])
+
+        load_w2(0)
+        q_first = fresh("q_first", [P, C2], F32)
+        nc.sync.dma_start(q_first[:], gate2[:, 0:C2])
+        load_w2(1)
+        q_rest = fresh("q_rest", [P, T - C2], F32)
+        nc.sync.dma_start(q_rest[:], gate2[:, C2:T])
+        load_w2(2)
+        load_w2(3)
+        a_rows = a.rearrange("(p j) s -> p j s", j=PACK)
+        a_sb = []
+        for e in range(E1):
+            a_sb.append(fresh(f"a{e}", [P, PACK, C1], F32))
+            nc.sync.dma_start(a_sb[e][:], a_rows[:, :, e * C1 : (e + 1) * C1])
+        nc.sync.dma_start(list1[:], offs)
+        g_sb = fresh("g_sb", [P, T], F32)
+        nc.sync.dma_start(g_sb[:], gate1)
+        nc.sync.dma_start(
+            w1_w[:].bitcast(I32).rearrange("p (e c) -> p e c", e=E1),
+            w1t_words[:, 0].bitcast(I32).rearrange("e p c -> p e c"),
+        )
+        for r in range(4):
+            nc.sync.dma_start(
+                w1_s[r:P:32, :].bitcast(I32).rearrange("p (e c) -> p e c", e=E1),
+                w1t_scales[:, 0, r:16:4, :].bitcast(I32).rearrange("e b c -> b e c"),
+            )
+
+        gq_w = fresh("gq_w", [P, T], U32)
+        gq_s = fresh("gq_s", [P, T], U8)
+        for h in range(2):
+            cols = slice(h * HALF, (h + 1) * HALF)
+            nc.vector.tensor_copy(gq_w[:, cols], dy_w[:].bitcast(U32).indirect(entries(list2, h * HALF, HALF)))
+            nc.vector.tensor_copy(gq_s[:, cols], dy_s[:].indirect(entries(list2, h * HALF, HALF)))
+
+        dc = [fresh(f"dc{t}", [P, T], F32) for t in range(PACK)]
+        groups = {0: [[0, 1], [2], [3]], 1: [[0, 1], [2, 3]], 2: [[0, 1], [2, 3]], 3: [[0, 1], [2, 3]]}
+        banks = {}
+
+        def prepare(f):
+            woven = fresh(f"woven{f}", [P, PACK, P, PACK], BF16)
+            for h in range(2):
+                dst = woven[:, :, h * 64 : (h + 1) * 64, :].rearrange("p t m j -> p m t j")
+                src = raw[f, h][:].rearrange("p j (m t) -> p m t j", t=PACK)
+                if f == 0 and h == 1:
+                    nc.vector.tensor_copy(dst, src)
+                else:
+                    nc.scalar.activation(dst, src, ACT.Copy)
+            codes = fresh(f"w2c{f}", [P, T], U32)
+            scales = fresh(f"w2s{f}", [P, T], U8)
+            flat = woven[:].rearrange("p t m j -> p (t m j)")
+            width = HALF if f == 0 else T
+            for c in range(0, T, width):
+                nc.vector.quantize_mx(
+                    out=codes[:, c : c + width].bitcast(FP8X4),
+                    scales=scales[:, c : c + width],
+                    in_=flat[:, PACK * c : PACK * (c + width)],
+                )
+            slots = slice(f * C2, (f + 1) * C2)
+            for n, group in enumerate(groups[f]):
+                bank = psum.tile([P, len(group), C2], F32, name=f"bank{f}{n}", tag="bank")
+                banks[f, n] = bank
+                for u, t in enumerate(group):
+                    cols = slice(t * P, (t + 1) * P)
+                    nc.tensor.matmul_mx(
+                        out=bank[:, u, :],
+                        lhsT=codes[:, cols].bitcast(FP8X4),
+                        lhsT_scale=scales[:, cols],
+                        rhs=gq_w[:, slots].bitcast(FP8X4),
+                        rhs_scale=gq_s[:, slots],
+                        start=True,
+                        stop=True,
+                    )
+
+        def scatter_group(f, n, tag):
+            group = groups[f][n]
+            sums = fresh(f"sums{f}{n}", [P, len(group), C2], F32, tag)
+            nc.scalar.activation(sums[:], banks[f, n][:], ACT.Copy)
+            q = q_first[:] if f == 0 else q_rest[:, (f - 1) * C2 : f * C2]
+            for u, t in enumerate(group):
+                nc.vector.tensor_tensor(dc[t][:].indirect(entries(list2, f * C2, C2)), sums[:, u, :], q, MULT)
+
+        prepare(0)
+        for f in range(E2):
+            last = len(groups[f]) - 1
+            for n in range(last):
+                scatter_group(f, n, None)
+            if f + 1 < E2:
+                prepare(f + 1)
+                scatter_group(f, last, f"raw{f + 1}1")
+            else:
+                scatter_group(f, last, None)
+
+        mask = []
+        for e in range(E1):
+            sign = fresh(f"sign{e}", [P, C1, PACK], BF16)
+            nc.scalar.activation(
+                sign[:].rearrange("p (c i) j -> p c j i", i=4),
+                a_sb[e][:].rearrange("p j (c i) -> p c j i", i=4),
+                ACT.Sign,
+            )
+            mask.append(fresh(f"mask{e}", [P, C1 * PACK], BF16))
+            nc.scalar.activation(mask[e][:], sign[:].rearrange("p s j -> p (s j)"), ACT.Relu)
+
+        banks1 = {}
+        for e in range(E1):
+            for kp in range(2):
+                banks1[e, kp] = psum.tile([P, 2, C1], F32, name=f"bank1_{e}{kp}", tag="bank")
+
+        gathered = {}
+
+        def gather(first, count):
+            gathered[first] = fresh(f"gathered{first}", [P, PACK, count], F32)
+            for t in range(PACK):
+                nc.vector.tensor_tensor(
+                    gathered[first][:, t, :],
+                    dc[t][:].indirect(entries(list1, first, count)),
+                    g_sb[:, first : first + count],
+                    MULT,
+                )
+
+        def multiply(first, count):
+            e, u0 = divmod(first, C1)
+            rounded = fresh(f"rounded{first}", [P, count, PACK], BF16)
+            nc.scalar.activation(
+                rounded[:].rearrange("p (c i) j -> p c j i", i=4),
+                gathered[first][:].rearrange("p j (c i) -> p c j i", i=4),
+                ACT.Copy,
+            )
+            da = fresh(f"da{first}", [P, count * PACK], BF16)
+            nc.vector.tensor_tensor(
+                da[:], rounded[:].rearrange("p s j -> p (s j)"), mask[e][:, PACK * u0 : PACK * (u0 + count)], MULT
+            )
+            codes = fresh(f"dac{first}", [P, count], U32)
+            scales = fresh(f"das{first}", [P, count], U8)
+            nc.vector.quantize_mx(out=codes[:].bitcast(FP8X4), scales=scales[:], in_=da[:])
+            for k in range(4):
+                nc.tensor.matmul_mx(
+                    out=banks1[e, k // 2][:, k % 2, u0 : u0 + count],
+                    lhsT=w1_w[:, e * 1024 + k * 256 : e * 1024 + (k + 1) * 256].bitcast(FP4X4),
+                    lhsT_scale=w1_s[:, e * T + k * P : e * T + (k + 1) * P],
+                    rhs=codes[:].bitcast(FP8X4),
+                    rhs_scale=scales[:],
+                    start=True,
+                    stop=True,
+                )
+
+        sums1 = {}
+
+        def empty(e, kp):
+            sums1[e, kp] = fresh(f"sums1_{e}{kp}", [P, 2, C1], F32)
+            nc.scalar.activation(sums1[e, kp][:], banks1[e, kp][:], ACT.Copy)
+
+        result = {}
+
+        def scatter_out(e, k):
+            nc.vector.tensor_copy(result[k][:].indirect(entries(list1, e * C1, C1)), sums1[e, k // 2][:, k % 2, :])
+
+        gather(0, 128)
+        multiply(0, 128)
+        gather(128, 128)
+        multiply(128, 128)
+        gather(256, 256)
+        empty(0, 0)
+        for k in (0, 1):
+            result[k] = fresh(f"result{k}", [P, T], F32)
+            scatter_out(0, k)
+        multiply(256, 256)
+        empty(0, 1)
+        for k, tag in ((2, "da256"), (3, "rounded256")):
+            result[k] = fresh(f"result{k}", [P, T], F32, tag)
+            scatter_out(0, k)
+        for kp in range(2):
+            empty(1, kp)
+            for k in (2 * kp, 2 * kp + 1):
+                scatter_out(1, k)
+                nc.sync.dma_start(out[k * P : (k + 1) * P, :], result[k][:])

@@ -51,21 +51,19 @@ def tile_moe_seb_relu_kernel(
         for r in range(4):
             nc.sync.dma_start(dy_s[r:P:32, :].bitcast(I32), dy_scales[0, r:16:4, :].bitcast(I32))
 
-        raw = {}
+        raw = []
 
         def load_w2(f):
-            rows = w2t[f].rearrange("(p j) i -> p j i", j=PACK)
-            for h in range(2):
-                raw[f, h] = fresh(f"raw{f}{h}", [P, PACK, HALF], F32)
-                nc.sync.dma_start(raw[f, h][:], rows[:, :, h * HALF : (h + 1) * HALF])
+            raw.append(fresh(f"raw{f}", [P, PACK, T], F32))
+            nc.sync.dma_start(raw[f][:], w2t[f].rearrange("(p j) i -> p j i", j=PACK))
 
         load_w2(0)
         q_first = fresh("q_first", [P, C2], F32)
         nc.sync.dma_start(q_first[:], gate2[:, 0:C2])
         load_w2(1)
+        load_w2(2)
         q_rest = fresh("q_rest", [P, T - C2], F32)
         nc.sync.dma_start(q_rest[:], gate2[:, C2:T])
-        load_w2(2)
         load_w2(3)
         a_rows = a.rearrange("(p j) s -> p j s", j=PACK)
         a_sb = []
@@ -90,75 +88,80 @@ def tile_moe_seb_relu_kernel(
         for h in range(2):
             cols = slice(h * HALF, (h + 1) * HALF)
             nc.vector.tensor_copy(gq_w[:, cols], dy_w[:].bitcast(U32).indirect(entries(list2, h * HALF, HALF)))
+        for h in range(2):
+            cols = slice(h * HALF, (h + 1) * HALF)
             nc.vector.tensor_copy(gq_s[:, cols], dy_s[:].indirect(entries(list2, h * HALF, HALF)))
 
-        dc = [fresh(f"dc{t}", [P, T], F32) for t in range(PACK)]
-        groups = {0: [[0, 1], [2], [3]], 1: [[0, 1], [2, 3]], 2: [[0, 1], [2, 3]], 3: [[0, 1], [2, 3]]}
+        dc = {}
         banks = {}
 
-        def prepare(f):
-            woven = fresh(f"woven{f}", [P, PACK, P, PACK], BF16)
-            for h in range(2):
-                dst = woven[:, :, h * 64 : (h + 1) * 64, :].rearrange("p t m j -> p m t j")
-                src = raw[f, h][:].rearrange("p j (m t) -> p m t j", t=PACK)
-                if f == 0 and h == 1:
-                    nc.vector.tensor_copy(dst, src)
-                else:
-                    nc.scalar.activation(dst, src, ACT.Copy)
-            codes = fresh(f"w2c{f}", [P, T], U32)
-            scales = fresh(f"w2s{f}", [P, T], U8)
-            flat = woven[:].rearrange("p t m j -> p (t m j)")
-            width = HALF if f == 0 else T
-            for c in range(0, T, width):
-                nc.vector.quantize_mx(
-                    out=codes[:, c : c + width].bitcast(FP8X4),
-                    scales=scales[:, c : c + width],
-                    in_=flat[:, PACK * c : PACK * (c + width)],
-                )
-            slots = slice(f * C2, (f + 1) * C2)
-            for n, group in enumerate(groups[f]):
-                bank = psum.tile([P, len(group), C2], F32, name=f"bank{f}{n}", tag="bank")
-                banks[f, n] = bank
-                for u, t in enumerate(group):
-                    cols = slice(t * P, (t + 1) * P)
-                    nc.tensor.matmul_mx(
-                        out=bank[:, u, :],
-                        lhsT=codes[:, cols].bitcast(FP8X4),
-                        lhsT_scale=scales[:, cols],
-                        rhs=gq_w[:, slots].bitcast(FP8X4),
-                        rhs_scale=gq_s[:, slots],
-                        start=True,
-                        stop=True,
-                    )
-
-        def scatter_group(f, n, tag):
-            group = groups[f][n]
-            sums = fresh(f"sums{f}{n}", [P, len(group), C2], F32, tag)
-            nc.scalar.activation(sums[:], banks[f, n][:], ACT.Copy)
-            q = q_first[:] if f == 0 else q_rest[:, (f - 1) * C2 : f * C2]
-            for u, t in enumerate(group):
-                nc.vector.tensor_tensor(dc[t][:].indirect(entries(list2, f * C2, C2)), sums[:, u, :], q, MULT)
-
-        prepare(0)
-        for f in range(E2):
-            last = len(groups[f]) - 1
-            for n in range(last):
-                scatter_group(f, n, None)
-            if f + 1 < E2:
-                prepare(f + 1)
-                scatter_group(f, last, f"raw{f + 1}1")
+        def prepare(f, h):
+            woven = fresh(f"woven{f}{h}", [P, 2, P, PACK], BF16)
+            dst = woven[:].rearrange("p t m j -> p m t j")
+            src = raw[f][:].rearrange("p j (m t) -> p m t j", t=PACK)[:, :, 2 * h : 2 * h + 2, :]
+            if (f, h) == (0, 0):
+                nc.vector.tensor_copy(dst, src)
             else:
-                scatter_group(f, last, None)
+                nc.scalar.activation(dst, src, ACT.Copy)
+            codes = fresh(f"w2c{f}{h}", [P, 2 * P], U32)
+            scales = fresh(f"w2s{f}{h}", [P, 2 * P], U8)
+            nc.vector.quantize_mx(
+                out=codes[:].bitcast(FP8X4), scales=scales[:], in_=woven[:].rearrange("p t m j -> p (t m j)")
+            )
+            slots = slice(f * C2, (f + 1) * C2)
+            banks[f, h] = psum.tile([P, 2, C2], F32, name=f"bank{f}{h}", tag="bank")
+            for u in range(2):
+                cols = slice(u * P, (u + 1) * P)
+                nc.tensor.matmul_mx(
+                    out=banks[f, h][:, u, :],
+                    lhsT=codes[:, cols].bitcast(FP8X4),
+                    lhsT_scale=scales[:, cols],
+                    rhs=gq_w[:, slots].bitcast(FP8X4),
+                    rhs_scale=gq_s[:, slots],
+                    start=True,
+                    stop=True,
+                )
 
-        mask = []
-        for e in range(E1):
-            sign = fresh(f"sign{e}", [P, C1, PACK], BF16)
+        sums = {}
+
+        def empty2(f, h):
+            sums[f, h] = fresh(f"sums{f}{h}", [P, 2, C2], F32)
+            nc.scalar.activation(sums[f, h][:], banks[f, h][:], ACT.Copy)
+
+        def scatter_dc(f, t):
+            if f == 0:
+                dc[t] = fresh(f"dc{t}", [P, T], F32, "woven10" if t == 3 else None)
+            q = q_first[:] if f == 0 else q_rest[:, (f - 1) * C2 : f * C2]
+            nc.vector.tensor_tensor(
+                dc[t][:].indirect(entries(list2, f * C2, C2)), sums[f, t // 2][:, t % 2, :], q, MULT
+            )
+
+        prepare(0, 0)
+        prepare(0, 1)
+        empty2(0, 0)
+        empty2(0, 1)
+        for t in range(3):
+            scatter_dc(0, t)
+        prepare(1, 0)
+        scatter_dc(0, 3)
+        units = [(f, h) for f in range(1, E2) for h in range(2)]
+        for n, (f, h) in enumerate(units):
+            if n + 1 < len(units):
+                prepare(*units[n + 1])
+            empty2(f, h)
+            scatter_dc(f, 2 * h)
+            scatter_dc(f, 2 * h + 1)
+
+        mask = {}
+
+        def make_mask(e, tag):
+            sign = fresh(f"sign{e}", [P, C1, PACK], BF16, tag)
             nc.scalar.activation(
                 sign[:].rearrange("p (c i) j -> p c j i", i=4),
                 a_sb[e][:].rearrange("p j (c i) -> p c j i", i=4),
                 ACT.Sign,
             )
-            mask.append(fresh(f"mask{e}", [P, C1 * PACK], BF16))
+            mask[e] = fresh(f"mask{e}", [P, C1 * PACK], BF16)
             nc.scalar.activation(mask[e][:], sign[:].rearrange("p s j -> p (s j)"), ACT.Relu)
 
         banks1 = {}
@@ -178,21 +181,33 @@ def tile_moe_seb_relu_kernel(
                     MULT,
                 )
 
-        def multiply(first, count):
-            e, u0 = divmod(first, C1)
-            rounded = fresh(f"rounded{first}", [P, count, PACK], BF16)
+        rounded = {}
+
+        def weave(first, count):
+            rounded[first] = fresh(f"rounded{first}", [P, count, PACK], BF16)
             nc.scalar.activation(
-                rounded[:].rearrange("p (c i) j -> p c j i", i=4),
+                rounded[first][:].rearrange("p (c i) j -> p c j i", i=4),
                 gathered[first][:].rearrange("p j (c i) -> p c j i", i=4),
                 ACT.Copy,
             )
-            da = fresh(f"da{first}", [P, count * PACK], BF16)
-            nc.vector.tensor_tensor(
-                da[:], rounded[:].rearrange("p s j -> p (s j)"), mask[e][:, PACK * u0 : PACK * (u0 + count)], MULT
-            )
+
+        def multiply(first, count):
+            e, u0 = divmod(first, C1)
+            flat = rounded[first][:].rearrange("p s j -> p (s j)")
+            da = []
+            for c in range(0, count, P):
+                da.append(fresh(f"da{first + c}", [P, P * PACK], BF16))
+                nc.vector.tensor_tensor(
+                    da[-1][:],
+                    flat[:, PACK * c : PACK * (c + P)],
+                    mask[e][:, PACK * (u0 + c) : PACK * (u0 + c + P)],
+                    MULT,
+                )
             codes = fresh(f"dac{first}", [P, count], U32)
             scales = fresh(f"das{first}", [P, count], U8)
-            nc.vector.quantize_mx(out=codes[:].bitcast(FP8X4), scales=scales[:], in_=da[:])
+            for n, piece in enumerate(da):
+                cols = slice(n * P, (n + 1) * P)
+                nc.vector.quantize_mx(out=codes[:, cols].bitcast(FP8X4), scales=scales[:, cols], in_=piece[:])
             for k in range(4):
                 nc.tensor.matmul_mx(
                     out=banks1[e, k // 2][:, k % 2, u0 : u0 + count],
@@ -215,20 +230,24 @@ def tile_moe_seb_relu_kernel(
         def scatter_out(e, k):
             nc.vector.tensor_copy(result[k][:].indirect(entries(list1, e * C1, C1)), sums1[e, k // 2][:, k % 2, :])
 
+        make_mask(0, None)
         gather(0, 128)
+        weave(0, 128)
         multiply(0, 128)
         gather(128, 128)
+        weave(128, 128)
         multiply(128, 128)
         gather(256, 256)
         empty(0, 0)
-        for k in (0, 1):
+        weave(256, 256)
+        empty(0, 1)
+        make_mask(1, "gathered256")
+        for k in range(3):
             result[k] = fresh(f"result{k}", [P, T], F32)
             scatter_out(0, k)
         multiply(256, 256)
-        empty(0, 1)
-        for k, tag in ((2, "da256"), (3, "rounded256")):
-            result[k] = fresh(f"result{k}", [P, T], F32, tag)
-            scatter_out(0, k)
+        result[3] = fresh("result3", [P, T], F32, "rounded256")
+        scatter_out(0, 3)
         for kp in range(2):
             empty(1, kp)
             for k in (2 * kp, 2 * kp + 1):

@@ -18,7 +18,8 @@ T = 512
 E1, C1 = 2, 256
 E2, C2 = 4, 128
 PACK = 4
-HALF = 256
+WINDOW = 704
+LEAD = 128
 FLOPS = 2 * 2 * 512 * 512 * 512
 
 
@@ -39,17 +40,18 @@ def tile_moe_seb_relu_kernel(
 
         list2 = lists.tile([P, T // 16], U16, name="list2")
         list1 = lists.tile([P, T // 16], U16, name="list1")
-        dy_w = fresh("dy_w", [P, T], I32)
-        dy_s = fresh("dy_s", [P, T], U8)
+        dy_w = fresh("dy_w", [P, WINDOW], I32)
+        dy_s = fresh("dy_s", [P, WINDOW], U8)
         w1_w = fresh("w1_w", [P, E1 * 1024], U8)
         w1_s = fresh("w1_s", [P, E1 * T], U8)
         nc.vector.memset(dy_s[:].bitcast(I32), 0)
+        nc.vector.memset(dy_w[:, T:WINDOW], 0)
         nc.vector.memset(w1_s[:].bitcast(I32), 0)
 
         nc.sync.dma_start(list2[:], offs2)
-        nc.sync.dma_start(dy_w[:], dy_words[0].rearrange("p t d -> p (t d)").bitcast(I32))
+        nc.sync.dma_start(dy_w[:, 0:T], dy_words[0].rearrange("p t d -> p (t d)").bitcast(I32))
         for r in range(4):
-            nc.sync.dma_start(dy_s[r:P:32, :].bitcast(I32), dy_scales[0, r:16:4, :].bitcast(I32))
+            nc.sync.dma_start(dy_s[r:P:32, 0:T].bitcast(I32), dy_scales[0, r:16:4, :].bitcast(I32))
 
         raw = []
 
@@ -66,10 +68,10 @@ def tile_moe_seb_relu_kernel(
         nc.sync.dma_start(q_rest[:], gate2[:, C2:T])
         load_w2(3)
         a_rows = a.rearrange("(p j) s -> p j s", j=PACK)
-        a_sb = []
-        for e in range(E1):
-            a_sb.append(fresh(f"a{e}", [P, PACK, C1], F32))
-            nc.sync.dma_start(a_sb[e][:], a_rows[:, :, e * C1 : (e + 1) * C1])
+        a_sb = {}
+        for first, count in ((0, LEAD), (LEAD, T - LEAD)):
+            a_sb[first] = fresh(f"a{first}", [P, PACK, count], F32)
+            nc.sync.dma_start(a_sb[first][:], a_rows[:, :, first : first + count])
         nc.sync.dma_start(list1[:], offs)
         g_sb = fresh("g_sb", [P, T], F32)
         nc.sync.dma_start(g_sb[:], gate1)
@@ -85,17 +87,12 @@ def tile_moe_seb_relu_kernel(
 
         gq_w = fresh("gq_w", [P, T], U32)
         gq_s = fresh("gq_s", [P, T], U8)
-        for h in range(2):
-            cols = slice(h * HALF, (h + 1) * HALF)
-            nc.vector.tensor_copy(gq_w[:, cols], dy_w[:].bitcast(U32).indirect(entries(list2, h * HALF, HALF)))
-        for h in range(2):
-            cols = slice(h * HALF, (h + 1) * HALF)
-            nc.vector.tensor_copy(gq_s[:, cols], dy_s[:].indirect(entries(list2, h * HALF, HALF)))
+        nc.vector.tensor_copy(gq_w[:], dy_w[:].bitcast(U32).indirect(list2[:]))
+        nc.vector.tensor_copy(gq_s[:], dy_s[:].indirect(list2[:]))
 
-        dc = {}
-        banks = {}
+        dc, banks, sums = {}, {}, {}
 
-        def prepare(f, h):
+        def prepare(f, h, groups):
             woven = fresh(f"woven{f}{h}", [P, 2, P, PACK], BF16)
             dst = woven[:].rearrange("p t m j -> p m t j")
             src = raw[f][:].rearrange("p j (m t) -> p m t j", t=PACK)[:, :, 2 * h : 2 * h + 2, :]
@@ -103,77 +100,80 @@ def tile_moe_seb_relu_kernel(
                 nc.vector.tensor_copy(dst, src)
             else:
                 nc.scalar.activation(dst, src, ACT.Copy)
-            codes = fresh(f"w2c{f}{h}", [P, 2 * P], U32)
-            scales = fresh(f"w2s{f}{h}", [P, 2 * P], U8)
-            nc.vector.quantize_mx(
-                out=codes[:].bitcast(FP8X4), scales=scales[:], in_=woven[:].rearrange("p t m j -> p (t m j)")
-            )
             slots = slice(f * C2, (f + 1) * C2)
-            banks[f, h] = psum.tile([P, 2, C2], F32, name=f"bank{f}{h}", tag="bank")
-            for u in range(2):
-                cols = slice(u * P, (u + 1) * P)
-                nc.tensor.matmul_mx(
-                    out=banks[f, h][:, u, :],
-                    lhsT=codes[:, cols].bitcast(FP8X4),
-                    lhsT_scale=scales[:, cols],
-                    rhs=gq_w[:, slots].bitcast(FP8X4),
-                    rhs_scale=gq_s[:, slots],
-                    start=True,
-                    stop=True,
+            for group in groups:
+                t0, n = group[0], len(group)
+                codes = fresh(f"w2c{f}{t0}", [P, n * P], U32)
+                scales = fresh(f"w2s{f}{t0}", [P, n * P], U8)
+                nc.vector.quantize_mx(
+                    out=codes[:].bitcast(FP8X4),
+                    scales=scales[:],
+                    in_=woven[:, t0 % 2 : t0 % 2 + n].rearrange("p t m j -> p (t m j)"),
                 )
+                banks[f, t0] = psum.tile([P, n, C2], F32, name=f"bank{f}{t0}", tag="bank")
+                for u in range(n):
+                    cols = slice(u * P, (u + 1) * P)
+                    nc.tensor.matmul_mx(
+                        out=banks[f, t0][:, u, :],
+                        lhsT=codes[:, cols].bitcast(FP8X4),
+                        lhsT_scale=scales[:, cols],
+                        rhs=gq_w[:, slots].bitcast(FP8X4),
+                        rhs_scale=gq_s[:, slots],
+                        start=True,
+                        stop=True,
+                    )
 
-        sums = {}
-
-        def empty2(f, h):
-            sums[f, h] = fresh(f"sums{f}{h}", [P, 2, C2], F32)
-            nc.scalar.activation(sums[f, h][:], banks[f, h][:], ACT.Copy)
+        def empty2(f, group):
+            values = fresh(f"sums{f}{group[0]}", [P, len(group), C2], F32)
+            nc.scalar.activation(values[:], banks[f, group[0]][:], ACT.Copy)
+            for u, t in enumerate(group):
+                sums[f, t] = values[:, u, :]
 
         def scatter_dc(f, t):
             if f == 0:
                 dc[t] = fresh(f"dc{t}", [P, T], F32, "woven10" if t == 3 else None)
             q = q_first[:] if f == 0 else q_rest[:, (f - 1) * C2 : f * C2]
-            nc.vector.tensor_tensor(
-                dc[t][:].indirect(entries(list2, f * C2, C2)), sums[f, t // 2][:, t % 2, :], q, MULT
-            )
+            nc.vector.tensor_tensor(dc[t][:].indirect(entries(list2, f * C2, C2)), sums[f, t], q, MULT)
 
-        prepare(0, 0)
-        prepare(0, 1)
-        empty2(0, 0)
-        empty2(0, 1)
+        prepare(0, 0, [[0], [1]])
+        prepare(0, 1, [[2, 3]])
+        for group in ([0], [1], [2, 3]):
+            empty2(0, group)
         for t in range(3):
             scatter_dc(0, t)
-        prepare(1, 0)
+        prepare(1, 0, [[0, 1]])
         scatter_dc(0, 3)
         units = [(f, h) for f in range(1, E2) for h in range(2)]
         for n, (f, h) in enumerate(units):
             if n + 1 < len(units):
-                prepare(*units[n + 1])
-            empty2(f, h)
+                f1, h1 = units[n + 1]
+                prepare(f1, h1, [[2 * h1, 2 * h1 + 1]])
+            empty2(f, [2 * h, 2 * h + 1])
             scatter_dc(f, 2 * h)
             scatter_dc(f, 2 * h + 1)
 
-        mask = {}
+        rest = T - LEAD
+        pieces = {0: LEAD, LEAD: C1 - LEAD, C1: C1}
+        mask, gathered, rounded, da, result = {}, {}, {}, {}, {}
 
-        def make_mask(e, tag):
-            sign = fresh(f"sign{e}", [P, C1, PACK], BF16, tag)
+        def make_mask(first):
+            count = pieces[first]
+            values = a_sb[0][:] if first == 0 else a_sb[LEAD][:, :, first - LEAD : first - LEAD + count]
+            sign = fresh(f"sign{first}", [P, count, PACK], BF16)
             nc.scalar.activation(
-                sign[:].rearrange("p (c i) j -> p c j i", i=4),
-                a_sb[e][:].rearrange("p j (c i) -> p c j i", i=4),
-                ACT.Sign,
+                sign[:].rearrange("p (c i) j -> p c j i", i=4), values.rearrange("p j (c i) -> p c j i", i=4), ACT.Sign
             )
-            mask[e] = fresh(f"mask{e}", [P, C1 * PACK], BF16)
-            nc.scalar.activation(mask[e][:], sign[:].rearrange("p s j -> p (s j)"), ACT.Relu)
+            mask[first] = fresh(f"mask{first}", [P, count * PACK], BF16)
+            nc.scalar.activation(mask[first][:], sign[:].rearrange("p s j -> p (s j)"), ACT.Relu)
 
-        banks1 = {}
-        for e in range(E1):
-            for kp in range(2):
-                banks1[e, kp] = psum.tile([P, 2, C1], F32, name=f"bank1_{e}{kp}", tag="bank")
+        stage = fresh("stage", [P, PACK * rest], F32)
+        gathered[LEAD] = stage[:].rearrange("p (j s) -> p j s", j=PACK)
+        lead_at = 4 * LEAD
+        gathered[0] = stage[:, lead_at : lead_at + PACK * LEAD].rearrange("p (j s) -> p j s", j=PACK)
+        rounded[0] = stage[:, lead_at - PACK * LEAD // 2 : lead_at].bitcast(BF16)
 
-        gathered = {}
-
-        def gather(first, count):
-            gathered[first] = fresh(f"gathered{first}", [P, PACK, count], F32)
-            for t in range(PACK):
+        def gather(first, count, planes):
+            for t in planes:
                 nc.vector.tensor_tensor(
                     gathered[first][:, t, :],
                     dc[t][:].indirect(entries(list1, first, count)),
@@ -181,36 +181,31 @@ def tile_moe_seb_relu_kernel(
                     MULT,
                 )
 
-        rounded = {}
-
-        def weave(first, count):
-            rounded[first] = fresh(f"rounded{first}", [P, count, PACK], BF16)
+        def weave(first):
+            count = pieces[first]
+            if first == 0:
+                values = gathered[0]
+            else:
+                values = gathered[LEAD][:, :, first - LEAD : first - LEAD + count]
+                rounded[first] = fresh(f"rounded{first}", [P, PACK * count], BF16)[:]
             nc.scalar.activation(
-                rounded[first][:].rearrange("p (c i) j -> p c j i", i=4),
-                gathered[first][:].rearrange("p j (c i) -> p c j i", i=4),
+                rounded[first].rearrange("p (c i j) -> p c j i", i=4, j=PACK),
+                values.rearrange("p j (c i) -> p c j i", i=4),
                 ACT.Copy,
             )
 
-        def multiply(first, count):
-            e, u0 = divmod(first, C1)
-            flat = rounded[first][:].rearrange("p s j -> p (s j)")
-            da = []
-            for c in range(0, count, P):
-                da.append(fresh(f"da{first + c}", [P, P * PACK], BF16))
-                nc.vector.tensor_tensor(
-                    da[-1][:],
-                    flat[:, PACK * c : PACK * (c + P)],
-                    mask[e][:, PACK * (u0 + c) : PACK * (u0 + c + P)],
-                    MULT,
-                )
+        def apply_mask(first):
+            da[first] = fresh(f"da{first}", [P, pieces[first] * PACK], BF16)
+            nc.vector.tensor_tensor(da[first][:], rounded[first], mask[first][:], MULT)
+
+        def multiply(first, target):
+            count, e = pieces[first], first // C1
             codes = fresh(f"dac{first}", [P, count], U32)
             scales = fresh(f"das{first}", [P, count], U8)
-            for n, piece in enumerate(da):
-                cols = slice(n * P, (n + 1) * P)
-                nc.vector.quantize_mx(out=codes[:, cols].bitcast(FP8X4), scales=scales[:, cols], in_=piece[:])
+            nc.vector.quantize_mx(out=codes[:].bitcast(FP8X4), scales=scales[:], in_=da[first][:])
             for k in range(4):
                 nc.tensor.matmul_mx(
-                    out=banks1[e, k // 2][:, k % 2, u0 : u0 + count],
+                    out=target(k),
                     lhsT=w1_w[:, e * 1024 + k * 256 : e * 1024 + (k + 1) * 256].bitcast(FP4X4),
                     lhsT_scale=w1_s[:, e * T + k * P : e * T + (k + 1) * P],
                     rhs=codes[:].bitcast(FP8X4),
@@ -219,37 +214,37 @@ def tile_moe_seb_relu_kernel(
                     stop=True,
                 )
 
-        sums1 = {}
+        def scatter_out(k, first, count, values):
+            nc.vector.tensor_copy(result[k][:].indirect(entries(list1, first, count)), values)
 
-        def empty(e, kp):
-            sums1[e, kp] = fresh(f"sums1_{e}{kp}", [P, 2, C1], F32)
-            nc.scalar.activation(sums1[e, kp][:], banks1[e, kp][:], ACT.Copy)
-
-        result = {}
-
-        def scatter_out(e, k):
-            nc.vector.tensor_copy(result[k][:].indirect(entries(list1, e * C1, C1)), sums1[e, k // 2][:, k % 2, :])
-
-        make_mask(0, None)
-        gather(0, 128)
-        weave(0, 128)
-        multiply(0, 128)
-        gather(128, 128)
-        weave(128, 128)
-        multiply(128, 128)
-        gather(256, 256)
-        empty(0, 0)
-        weave(256, 256)
-        empty(0, 1)
-        make_mask(1, "gathered256")
-        for k in range(3):
+        for first in pieces:
+            make_mask(first)
+        gather(0, LEAD, range(PACK))
+        weave(0)
+        gather(LEAD, rest, [3])
+        apply_mask(0)
+        lead_banks = [psum.tile([P, 2, LEAD], F32, name=f"lead_bank{n}", tag="bank") for n in range(2)]
+        multiply(0, lambda k: lead_banks[k // 2][:, k % 2, :])
+        gather(LEAD, rest, [2, 0, 1])
+        lead_sums = []
+        for n in range(2):
+            lead_sums.append(fresh(f"lead_sums{n}", [P, 2, LEAD], F32))
+            nc.scalar.activation(lead_sums[n][:], lead_banks[n][:], ACT.Copy)
+        for k in (0, 1):
             result[k] = fresh(f"result{k}", [P, T], F32)
-            scatter_out(0, k)
-        multiply(256, 256)
-        result[3] = fresh("result3", [P, T], F32, "rounded256")
-        scatter_out(0, 3)
-        for kp in range(2):
-            empty(1, kp)
-            for k in (2 * kp, 2 * kp + 1):
-                scatter_out(1, k)
-                nc.sync.dma_start(out[k * P : (k + 1) * P, :], result[k][:])
+            scatter_out(k, 0, LEAD, lead_sums[0][:, k, :])
+        rest_banks = [psum.tile([P, rest], F32, name=f"rest_bank{k}", tag="bank") for k in range(4)]
+        for first in (C1, LEAD):
+            weave(first)
+        for first in (C1, LEAD):
+            apply_mask(first)
+        for first in (C1, LEAD):
+            multiply(first, lambda k: rest_banks[k][:, first - LEAD : first - LEAD + pieces[first]])
+        for k, tag in ((2, f"rounded{LEAD}"), (3, f"mask{LEAD}")):
+            result[k] = fresh(f"result{k}", [P, T], F32, tag)
+            scatter_out(k, 0, LEAD, lead_sums[1][:, k - 2, :])
+        for k in range(4):
+            rest_sums = fresh(f"rest_sums{k}", [P, rest], F32)
+            nc.scalar.activation(rest_sums[:], rest_banks[k][:], ACT.Copy)
+            scatter_out(k, LEAD, rest, rest_sums[:])
+            nc.sync.dma_start(out[k * P : (k + 1) * P, :], result[k][:])

@@ -53,11 +53,15 @@ def tile_moe_seb_relu_kernel(
         for r in range(4):
             nc.sync.dma_start(dy_s[r:P:32, 0:T].bitcast(I32), dy_scales[0, r:16:4, :].bitcast(I32))
 
-        raw = []
+        raw = {}
 
         def load_w2(f):
-            raw.append(fresh(f"raw{f}", [P, PACK, T], F32))
-            nc.sync.dma_start(raw[f][:], w2t[f].rearrange("(p j) i -> p j i", j=PACK))
+            width = T // 2 if f == 0 else T
+            rows = w2t[f].rearrange("(p j) i -> p j i", j=PACK)
+            raw[f] = []
+            for c in range(0, T, width):
+                raw[f].append(fresh(f"raw{f}_{c}", [P, PACK, width], F32))
+                nc.sync.dma_start(raw[f][-1][:], rows[:, :, c : c + width])
 
         load_w2(0)
         q_first = fresh("q_first", [P, C2], F32)
@@ -94,12 +98,14 @@ def tile_moe_seb_relu_kernel(
 
         def prepare(f, h, groups):
             woven = fresh(f"woven{f}{h}", [P, 2, P, PACK], BF16)
-            dst = woven[:].rearrange("p t m j -> p m t j")
-            src = raw[f][:].rearrange("p j (m t) -> p m t j", t=PACK)[:, :, 2 * h : 2 * h + 2, :]
-            if (f, h) == (0, 0):
-                nc.vector.tensor_copy(dst, src)
-            else:
-                nc.scalar.activation(dst, src, ACT.Copy)
+            for n, part in enumerate(raw[f]):
+                m = P // len(raw[f])
+                dst = woven[:, :, n * m : (n + 1) * m, :].rearrange("p t m j -> p m j t")
+                src = part[:].rearrange("p j (m t) -> p m j t", t=PACK)[:, :, :, 2 * h : 2 * h + 2]
+                if (f, h, n) == (0, 0, 1):
+                    nc.vector.tensor_copy(dst, src)
+                else:
+                    nc.scalar.activation(dst, src, ACT.Copy)
             slots = slice(f * C2, (f + 1) * C2)
             for group in groups:
                 t0, n = group[0], len(group)

@@ -1,6 +1,7 @@
 from contextlib import ExitStack
 
 import concourse.mybir as mybir
+from concourse.masks import make_identity
 
 F32 = mybir.dt.float32
 BF16 = mybir.dt.bfloat16
@@ -19,7 +20,7 @@ E1, C1 = 2, 256
 E2, C2 = 4, 128
 PACK = 4
 WINDOW = 704
-LEAD = 128
+REST = T - P
 FLOPS = 2 * 2 * 512 * 512 * 512
 
 
@@ -30,10 +31,13 @@ def tile_moe_seb_relu_kernel(
     with ExitStack() as ctx:
         lists = ctx.enter_context(tc.tile_pool(name="lists", bufs=1))
         sb = ctx.enter_context(tc.tile_pool(name="sb", bufs=1))
-        psum = ctx.enter_context(tc.psum_pool(name="psum", bufs=8))
+        psum = ctx.enter_context(tc.psum_pool(name="psum", bufs=1))
 
         def fresh(name, shape, dtype, tag=None):
             return sb.tile(shape, dtype, name=name, tag=tag or name, align_bytes=64)
+
+        def bank(name, shape, number):
+            return psum.tile(shape, F32, name=name, tag=f"bank{number}")
 
         def entries(lst, first, count):
             return lst[:, first // 16 : (first + count) // 16]
@@ -41,44 +45,58 @@ def tile_moe_seb_relu_kernel(
         list2 = lists.tile([P, T // 16], U16, name="list2")
         list1 = lists.tile([P, T // 16], U16, name="list1")
         dy_w = fresh("dy_w", [P, WINDOW], I32)
-        dy_s = fresh("dy_s", [P, WINDOW], U8)
+        dy_s = fresh("dy_s", [P, T], U8)
         w1_w = fresh("w1_w", [P, E1 * 1024], U8)
         w1_s = fresh("w1_s", [P, E1 * T], U8)
+        identity = fresh("identity", [P, P], F32)
         nc.vector.memset(dy_s[:].bitcast(I32), 0)
         nc.vector.memset(dy_w[:, T:WINDOW], 0)
-        nc.vector.memset(w1_s[:].bitcast(I32), 0)
+        nc.gpsimd.memset(w1_s[:].bitcast(I32), 0)
+        make_identity(nc, identity[:])
 
         nc.sync.dma_start(list2[:], offs2)
         nc.sync.dma_start(dy_w[:, 0:T], dy_words[0].rearrange("p t d -> p (t d)").bitcast(I32))
-        for r in range(4):
-            nc.sync.dma_start(dy_s[r:P:32, 0:T].bitcast(I32), dy_scales[0, r:16:4, :].bitcast(I32))
 
         raw = {}
 
-        def load_w2(f):
-            width = T // 2 if f == 0 else T
+        def load_w2(f, b0, blocks):
             rows = w2t[f].rearrange("(p j) i -> p j i", j=PACK)
-            raw[f] = []
-            for c in range(0, T, width):
-                raw[f].append(fresh(f"raw{f}_{c}", [P, PACK, width], F32))
-                nc.sync.dma_start(raw[f][-1][:], rows[:, :, c : c + width])
+            flat = fresh(f"raw{f}_{b0}", [P, PACK * blocks * P], F32)
+            piece = flat[:].rearrange("p (j i) -> p j i", j=PACK)
+            nc.sync.dma_start(piece, rows[:, :, b0 * P : (b0 + blocks) * P])
+            for b in range(b0, b0 + blocks):
+                raw[f, b] = (flat, b0, blocks)
 
-        load_w2(0)
-        q_first = fresh("q_first", [P, C2], F32)
-        nc.sync.dma_start(q_first[:], gate2[:, 0:C2])
-        load_w2(1)
-        load_w2(2)
-        q_rest = fresh("q_rest", [P, T - C2], F32)
-        nc.sync.dma_start(q_rest[:], gate2[:, C2:T])
-        load_w2(3)
-        a_rows = a.rearrange("(p j) s -> p j s", j=PACK)
+        def raw_bytes(f, b0, j, columns):
+            flat, first, blocks = raw[f, b0]
+            at = (j * blocks + b0 - first) * P
+            return flat[:, at : at + columns]
+
         a_sb = {}
-        for first, count in ((0, LEAD), (LEAD, T - LEAD)):
-            a_sb[first] = fresh(f"a{first}", [P, PACK, count], F32)
-            nc.sync.dma_start(a_sb[first][:], a_rows[:, :, first : first + count])
+
+        def load_a(b):
+            a_sb[b] = fresh(f"a{b}", [P, T], F32)
+            nc.sync.dma_start(a_sb[b][:], a[b * P : (b + 1) * P, :])
+
+        q_first = fresh("q_first", [P, C2], F32)
+        q_rest = fresh("q_rest", [P, REST], F32)[:]
+        load_w2(0, 0, 1)
+        for r in range(4):
+            nc.sync.dma_start(dy_s[r:P:32, :].bitcast(I32), dy_scales[0, r:16:4, :].bitcast(I32))
+        load_w2(0, 1, 1)
+        nc.sync.dma_start(q_first[:], gate2[:, 0:C2])
+        load_w2(0, 2, 2)
+        load_w2(1, 0, 2)
+        load_w2(1, 2, 2)
+        nc.sync.dma_start(q_rest, gate2[:, C2:T])
+        load_w2(2, 0, 4)
+        load_w2(3, 0, 4)
+        for b in range(4):
+            load_a(b)
         nc.sync.dma_start(list1[:], offs)
-        g_sb = fresh("g_sb", [P, T], F32)
-        nc.sync.dma_start(g_sb[:], gate1)
+        g_col = fresh("g_col", [P, T // P], F32)
+        with nc.allow_non_contiguous_dma(reason="one gate value a partition"):
+            nc.sync.dma_start(g_col[:], gate1[0].rearrange("(c p) -> p c", p=P))
         nc.sync.dma_start(
             w1_w[:].bitcast(I32).rearrange("p (e c) -> p e c", e=E1),
             w1t_words[:, 0].bitcast(I32).rearrange("e p c -> p e c"),
@@ -90,125 +108,136 @@ def tile_moe_seb_relu_kernel(
             )
 
         gq_w = fresh("gq_w", [P, T], U32)
-        gq_s = fresh("gq_s", [P, T], U8)
+        gq_s_first = fresh("gq_s_first", [P, C2], U8)
         nc.vector.tensor_copy(gq_w[:], dy_w[:].bitcast(U32).indirect(list2[:]))
-        nc.vector.tensor_copy(gq_s[:], dy_s[:].indirect(list2[:]))
+        nc.vector.tensor_copy(gq_s_first[:], dy_s[:].indirect(entries(list2, 0, C2)))
+        gq_s = {0: gq_s_first[:]}
 
         dc, banks, sums = {}, {}, {}
 
-        def prepare(f, h, groups):
-            woven = fresh(f"woven{f}{h}", [P, 2, P, PACK], BF16)
-            for n, part in enumerate(raw[f]):
-                m = P // len(raw[f])
-                dst = woven[:, :, n * m : (n + 1) * m, :].rearrange("p t m j -> p m j t")
-                src = part[:].rearrange("p j (m t) -> p m j t", t=PACK)[:, :, :, 2 * h : 2 * h + 2]
-                if (f, h, n) == (0, 0, 1):
-                    nc.vector.tensor_copy(dst, src)
-                else:
-                    nc.scalar.activation(dst, src, ACT.Copy)
-            slots = slice(f * C2, (f + 1) * C2)
-            for group in groups:
-                t0, n = group[0], len(group)
-                codes = fresh(f"w2c{f}{t0}", [P, n * P], U32)
-                scales = fresh(f"w2s{f}{t0}", [P, n * P], U8)
-                nc.vector.quantize_mx(
-                    out=codes[:].bitcast(FP8X4),
-                    scales=scales[:],
-                    in_=woven[:, t0 % 2 : t0 % 2 + n].rearrange("p t m j -> p (t m j)"),
+        def prepare(n, f, b0, blocks):
+            flat, first, loaded = raw[f, b0]
+            woven = fresh(f"woven{n}", [P, blocks * P, PACK], BF16, f"w2c{n - 2}" if n >= 2 else None)
+            values = flat[:].rearrange("p (j i) -> p j i", j=PACK)[:, :, (b0 - first) * P : (b0 - first + blocks) * P]
+            nc.scalar.activation(
+                woven[:].rearrange("p (c i) j -> p c j i", i=4), values.rearrange("p j (c i) -> p c j i", i=4), ACT.Copy
+            )
+            codes = fresh(f"w2c{n}", [P, blocks * P], U32)
+            scales = fresh(f"w2s{f}{b0}", [P, blocks * P], U8)
+            nc.vector.quantize_mx(
+                out=codes[:].bitcast(FP8X4), scales=scales[:], in_=woven[:].rearrange("p i j -> p (i j)")
+            )
+            banks[f, b0] = bank(f"sums_bank{f}{b0}", [P, blocks, C2], n % 4)
+            for u in range(blocks):
+                cols = slice(u * P, (u + 1) * P)
+                nc.tensor.matmul_mx(
+                    out=banks[f, b0][:, u, :],
+                    lhsT=codes[:, cols].bitcast(FP8X4),
+                    lhsT_scale=scales[:, cols],
+                    rhs=gq_w[:, f * C2 : (f + 1) * C2].bitcast(FP8X4),
+                    rhs_scale=gq_s[f],
+                    start=True,
+                    stop=True,
                 )
-                banks[f, t0] = psum.tile([P, n, C2], F32, name=f"bank{f}{t0}", tag="bank")
-                for u in range(n):
-                    cols = slice(u * P, (u + 1) * P)
-                    nc.tensor.matmul_mx(
-                        out=banks[f, t0][:, u, :],
-                        lhsT=codes[:, cols].bitcast(FP8X4),
-                        lhsT_scale=scales[:, cols],
-                        rhs=gq_w[:, slots].bitcast(FP8X4),
-                        rhs_scale=gq_s[:, slots],
-                        start=True,
-                        stop=True,
-                    )
 
-        def empty2(f, group):
-            values = fresh(f"sums{f}{group[0]}", [P, len(group), C2], F32)
-            nc.scalar.activation(values[:], banks[f, group[0]][:], ACT.Copy)
-            for u, t in enumerate(group):
-                sums[f, t] = values[:, u, :]
+        def empty(f, b0, blocks, place):
+            sums[f, b0] = place.rearrange("p (u s) -> p u s", u=blocks)
+            nc.scalar.activation(sums[f, b0], banks[f, b0][:], ACT.Copy)
 
-        def scatter_dc(f, t):
-            if f == 0:
-                dc[t] = fresh(f"dc{t}", [P, T], F32, "woven10" if t == 3 else None)
+        def scatter_dc(f, b0, blocks):
+            values = sums[f, b0]
             q = q_first[:] if f == 0 else q_rest[:, (f - 1) * C2 : f * C2]
-            nc.vector.tensor_tensor(dc[t][:].indirect(entries(list2, f * C2, C2)), sums[f, t], q, MULT)
+            for u in range(blocks):
+                if f == 0:
+                    dc[b0 + u] = fresh(f"dc{b0 + u}", [P, T], F32)
+                nc.vector.tensor_tensor(dc[b0 + u][:].indirect(entries(list2, f * C2, C2)), values[:, u, :], q, MULT)
 
-        prepare(0, 0, [[0], [1]])
-        prepare(0, 1, [[2, 3]])
-        for group in ([0], [1], [2, 3]):
-            empty2(0, group)
-        for t in range(3):
-            scatter_dc(0, t)
-        prepare(1, 0, [[0, 1]])
-        scatter_dc(0, 3)
-        units = [(f, h) for f in range(1, E2) for h in range(2)]
-        for n, (f, h) in enumerate(units):
+        mask = {}
+
+        def sign(b):
+            last_raw = raw[E2 - 1, 0][0]
+            if b == 3:
+                return last_raw[:, 704:1216]
+            at = (256, 1792, 1408)[b]
+            return last_raw[:, at : at + 2 * P].bitcast(BF16)
+
+        def make_sign(b):
+            nc.scalar.activation(sign(b), a_sb[b][:], ACT.Sign)
+
+        def make_mask(b):
+            mask[b] = fresh(f"mask{b}", [P, T], F32)
+            nc.scalar.activation(mask[b][:], sign(b), ACT.Relu)
+
+        units = [(0, b, 1) for b in range(4)] + [(f, b0, 2) for f in range(1, E2) for b0 in (0, 2)]
+        prepare(0, *units[0])
+        gq_s_rest = fresh("gq_s_rest", [P, REST], U8, "woven0")
+        nc.vector.tensor_copy(gq_s_rest[:], dy_s[:].indirect(entries(list2, C2, REST)))
+        for f in range(1, E2):
+            gq_s[f] = gq_s_rest[:, (f - 1) * C2 : f * C2]
+        for n, unit in enumerate(units):
             if n + 1 < len(units):
-                f1, h1 = units[n + 1]
-                prepare(f1, h1, [[2 * h1, 2 * h1 + 1]])
-            empty2(f, [2 * h, 2 * h + 1])
-            scatter_dc(f, 2 * h)
-            scatter_dc(f, 2 * h + 1)
-
-        rest = T - LEAD
-        pieces = {0: LEAD, LEAD: C1 - LEAD, C1: C1}
-        mask, gathered, rounded, da, result = {}, {}, {}, {}, {}
-
-        def make_mask(first):
-            count = pieces[first]
-            values = a_sb[0][:] if first == 0 else a_sb[LEAD][:, :, first - LEAD : first - LEAD + count]
-            sign = fresh(f"sign{first}", [P, count, PACK], BF16)
-            nc.scalar.activation(
-                sign[:].rearrange("p (c i) j -> p c j i", i=4), values.rearrange("p j (c i) -> p c j i", i=4), ACT.Sign
-            )
-            mask[first] = fresh(f"mask{first}", [P, count * PACK], BF16)
-            nc.scalar.activation(mask[first][:], sign[:].rearrange("p s j -> p (s j)"), ACT.Relu)
-
-        stage = fresh("stage", [P, PACK * rest], F32)
-        gathered[LEAD] = stage[:].rearrange("p (j s) -> p j s", j=PACK)
-        lead_at = 4 * LEAD
-        gathered[0] = stage[:, lead_at : lead_at + PACK * LEAD].rearrange("p (j s) -> p j s", j=PACK)
-        rounded[0] = stage[:, lead_at - PACK * LEAD // 2 : lead_at].bitcast(BF16)
-
-        def gather(first, count, planes):
-            for t in planes:
-                nc.vector.tensor_tensor(
-                    gathered[first][:, t, :],
-                    dc[t][:].indirect(entries(list1, first, count)),
-                    g_sb[:, first : first + count],
-                    MULT,
-                )
-
-        def weave(first):
-            count = pieces[first]
-            if first == 0:
-                values = gathered[0]
+                prepare(n + 1, *units[n + 1])
+            f, b0, blocks = unit
+            if n + 2 < len(units):
+                f1, b1 = units[n + 1][:2]
+                empty(*unit, raw_bytes(f1, b1, 0, blocks * C2))
+            elif n + 2 == len(units):
+                make_sign(0)
+                empty(*unit, a_sb[0][:, 0 : blocks * C2])
+                make_mask(0)
+                make_sign(1)
+                make_mask(1)
             else:
-                values = gathered[LEAD][:, :, first - LEAD : first - LEAD + count]
-                rounded[first] = fresh(f"rounded{first}", [P, PACK * count], BF16)[:]
-            nc.scalar.activation(
-                rounded[first].rearrange("p (c i j) -> p c j i", i=4, j=PACK),
-                values.rearrange("p j (c i) -> p c j i", i=4),
-                ACT.Copy,
+                empty(*unit, raw_bytes(f, b0, 3, blocks * C2))
+                for b in (2, 3):
+                    make_sign(b)
+                    make_mask(b)
+            scatter_dc(*unit)
+
+        last_raw = raw[E2 - 1, 0][0]
+        late = fresh("late", [P, 2 * C1], F32)
+        picked = {(b, 0): fresh(f"lead{b}", [P, P], F32)[:] for b in range(4)}
+        picked[3, P] = fresh("second3", [P, P], F32)[:]
+        for b in range(3):
+            picked[b, P] = last_raw[:, 768 + b * P : 768 + (b + 1) * P]
+        picked[0, C1] = last_raw[:, 512:768]
+        picked[1, C1] = last_raw[:, 1152:1408]
+        picked[2, C1] = late[:, 0:C1]
+        picked[3, C1] = late[:, C1 : 2 * C1]
+        turned = [fresh(f"turned{c}", [P, 2, P, 2], BF16) for c in range(4)]
+        result = {}
+
+        def gather(b, first):
+            values = picked[b, first]
+            count = values.shape[1]
+            nc.vector.tensor_tensor(
+                values, dc[b][:].indirect(entries(list1, first, count)), mask[b][:, first : first + count], MULT
             )
 
-        def apply_mask(first):
-            da[first] = fresh(f"da{first}", [P, pieces[first] * PACK], BF16)
-            nc.vector.tensor_tensor(da[first][:], rounded[first], mask[first][:], MULT)
+        def scale_rows(c, b0, values):
+            blocks = values.shape[1] // P
+            nc.scalar.activation(
+                turned[c][:, :, 32 * b0 : 32 * (b0 + blocks), :],
+                values.rearrange("s (p u e) -> s u p e", u=2, e=2),
+                ACT.Copy,
+                scale=g_col[:, c : c + 1],
+            )
 
-        def multiply(first, target):
-            count, e = pieces[first], first // C1
+        def turn_back(cs, number, words):
+            back = bank(f"back{cs[0]}", [P, len(cs), 2, P], number)
+            for n, c in enumerate(cs):
+                pairs = turned[c][:].rearrange("s u p e -> s (u p e)").bitcast(F32)
+                for u in range(2):
+                    nc.tensor.transpose(back[:, n, u, :], pairs[:, u * P : (u + 1) * P], identity[:])
+            nc.scalar.copy(
+                words.rearrange("p (c s u) -> p c s u", c=len(cs), u=2), back[:].rearrange("p c u s -> p c s u")
+            )
+
+        def multiply(first, count, words, target):
+            e = first // C1
             codes = fresh(f"dac{first}", [P, count], U32)
             scales = fresh(f"das{first}", [P, count], U8)
-            nc.vector.quantize_mx(out=codes[:].bitcast(FP8X4), scales=scales[:], in_=da[first][:])
+            nc.vector.quantize_mx(out=codes[:].bitcast(FP8X4), scales=scales[:], in_=words.bitcast(BF16))
             for k in range(4):
                 nc.tensor.matmul_mx(
                     out=target(k),
@@ -223,34 +252,53 @@ def tile_moe_seb_relu_kernel(
         def scatter_out(k, first, count, values):
             nc.vector.tensor_copy(result[k][:].indirect(entries(list1, first, count)), values)
 
-        for first in pieces:
-            make_mask(first)
-        gather(0, LEAD, range(PACK))
-        weave(0)
-        gather(LEAD, rest, [3])
-        apply_mask(0)
-        lead_banks = [psum.tile([P, 2, LEAD], F32, name=f"lead_bank{n}", tag="bank") for n in range(2)]
-        multiply(0, lambda k: lead_banks[k // 2][:, k % 2, :])
-        gather(LEAD, rest, [2, 0, 1])
-        lead_sums = []
-        for n in range(2):
-            lead_sums.append(fresh(f"lead_sums{n}", [P, 2, LEAD], F32))
-            nc.scalar.activation(lead_sums[n][:], lead_banks[n][:], ACT.Copy)
-        for k in (0, 1):
+        def turn(c, blocks, number):
+            first = min(c * P, C1)
+            rows = bank(f"rows{c}_{blocks[0]}", [P, len(blocks), P], number)
+            for n, b in enumerate(blocks):
+                nc.tensor.transpose(rows[:, n, :], picked[b, first][:, c * P - first : (c + 1) * P - first], identity[:])
+            scale_rows(c, blocks[0], rows[:].rearrange("s b i -> s (b i)"))
+
+        def product(first, count, words, numbers):
+            halves = [bank(f"out_bank{first}_{n}", [P, 2, count], numbers[n]) for n in range(2)]
+            multiply(first, count, words, lambda k: halves[k // 2][:, k % 2, :])
+            values = []
+            for n in range(2):
+                values.append(fresh(f"out_sums{first}_{n}", [P, 2, count], F32))
+                nc.scalar.activation(values[n][:], halves[n][:], ACT.Copy)
+            return [values[k // 2][:, k % 2, :] for k in range(4)]
+
+        for b in range(4):
+            gather(b, 0)
+        for b in range(4):
+            gather(b, P)
+        for b in range(2):
+            gather(b, C1)
+        turn(0, [0, 1, 2], 4)
+        turn(0, [3], 5)
+        turn_back([0], 6, late[:, P : 3 * P])
+        sums0 = product(0, P, late[:, P : 3 * P], (2, 3))
+        for b in (2, 3):
+            gather(b, C1)
+        turn(1, [0, 1, 2, 3], 5)
+        for k in (0, 2):
             result[k] = fresh(f"result{k}", [P, T], F32)
-            scatter_out(k, 0, LEAD, lead_sums[0][:, k, :])
-        rest_banks = [psum.tile([P, rest], F32, name=f"rest_bank{k}", tag="bank") for k in range(4)]
-        for first in (C1, LEAD):
-            weave(first)
-        for first in (C1, LEAD):
-            apply_mask(first)
-        for first in (C1, LEAD):
-            multiply(first, lambda k: rest_banks[k][:, first - LEAD : first - LEAD + pieces[first]])
-        for k, tag in ((2, f"rounded{LEAD}"), (3, f"mask{LEAD}")):
-            result[k] = fresh(f"result{k}", [P, T], F32, tag)
-            scatter_out(k, 0, LEAD, lead_sums[1][:, k - 2, :])
+            scatter_out(k, 0, P, sums0[k])
+        da1 = fresh("da1", [P, 2 * P], F32)
+        turn_back([1], 7, da1[:])
+        sums1 = product(P, P, da1[:], (0, 1))
+        result[1] = fresh("result1", [P, T], F32, "da1")
+        scatter_out(1, 0, P, sums0[1])
+        turn(2, [0, 1, 2, 3], 6)
+        turn(3, [0, 1, 2, 3], 7)
+        for k in range(3):
+            scatter_out(k, P, P, sums1[k])
+        da23 = fresh("da23", [P, 2 * C1], F32)
+        turn_back([2, 3], 4, da23[:])
+        sums23 = product(C1, C1, da23[:], (2, 3))
+        result[3] = fresh("result3", [P, T], F32, "da23")
+        scatter_out(3, 0, P, sums0[3])
+        scatter_out(3, P, P, sums1[3])
         for k in range(4):
-            rest_sums = fresh(f"rest_sums{k}", [P, rest], F32)
-            nc.scalar.activation(rest_sums[:], rest_banks[k][:], ACT.Copy)
-            scatter_out(k, LEAD, rest, rest_sums[:])
+            scatter_out(k, C1, C1, sums23[k])
             nc.sync.dma_start(out[k * P : (k + 1) * P, :], result[k][:])

@@ -54,8 +54,8 @@ def tile_moe_seb_relu_kernel(
         nc.gpsimd.memset(w1_s[:].bitcast(I32), 0)
         make_identity(nc, identity[:])
 
-        nc.sync.dma_start(list2[:], offs2)
         nc.sync.dma_start(dy_w[:, 0:T], dy_words[0].rearrange("p t d -> p (t d)").bitcast(I32))
+        nc.sync.dma_start(list2[:], offs2)
 
         raw = {}
 
@@ -91,8 +91,10 @@ def tile_moe_seb_relu_kernel(
         nc.sync.dma_start(q_rest, gate2[:, C2:T])
         load_w2(2, 0, 4)
         load_w2(3, 0, 4)
-        for b in range(4):
-            load_a(b)
+        load_a(0)
+        load_a(1)
+        a23 = fresh("a23", [P, 2, T], F32)
+        nc.sync.dma_start(a23[:], a[2 * P : 4 * P, :].rearrange("(b p) s -> p b s", p=P))
         nc.sync.dma_start(list1[:], offs)
         g_col = fresh("g_col", [P, T // P], F32)
         with nc.allow_non_contiguous_dma(reason="one gate value a partition"):
@@ -153,24 +155,19 @@ def tile_moe_seb_relu_kernel(
                 nc.vector.tensor_tensor(dc[b0 + u][:].indirect(entries(list2, f * C2, C2)), values[:, u, :], q, MULT)
 
         mask = {}
+        last_raw = raw[E2 - 1, 0][0]
 
-        def sign(b):
-            last_raw = raw[E2 - 1, 0][0]
-            if b == 3:
-                return last_raw[:, 704:1216]
-            at = (256, 1792, 1408)[b]
-            return last_raw[:, at : at + 2 * P].bitcast(BF16)
-
-        def make_sign(b):
-            nc.scalar.activation(sign(b), a_sb[b][:], ACT.Sign)
-
-        def make_mask(b):
-            mask[b] = fresh(f"mask{b}", [P, T], F32)
-            nc.scalar.activation(mask[b][:], sign(b), ACT.Relu)
+        def keep_positive(name, signs, blocks, first, tag=None):
+            count = signs.shape[-1]
+            made = fresh(name, [P, len(blocks), count], F32, tag)
+            nc.scalar.activation(made[:], signs, ACT.Relu)
+            for n, b in enumerate(blocks):
+                for at in range(0, count, C1):
+                    mask[b, first + at] = made[:, n, at : at + C1]
 
         units = [(0, b, 1) for b in range(4)] + [(f, b0, 2) for f in range(1, E2) for b0 in (0, 2)]
         prepare(0, *units[0])
-        gq_s_rest = fresh("gq_s_rest", [P, REST], U8, "woven0")
+        gq_s_rest = fresh("gq_s_rest", [P, REST], U8, "raw0_0")
         nc.vector.tensor_copy(gq_s_rest[:], dy_s[:].indirect(entries(list2, C2, REST)))
         for f in range(1, E2):
             gq_s[f] = gq_s_rest[:, (f - 1) * C2 : f * C2]
@@ -178,32 +175,34 @@ def tile_moe_seb_relu_kernel(
             if n + 1 < len(units):
                 prepare(n + 1, *units[n + 1])
             f, b0, blocks = unit
-            if n + 2 < len(units):
+            if n == len(units) - 2:
+                sign0 = raw_bytes(E2 - 1, 2, 0, 2 * P).bitcast(BF16).rearrange("p (b s) -> p b s", b=1)
+                nc.scalar.activation(sign0[:, 0, :], a_sb[0][:], ACT.Sign)
+                empty(*unit, a_sb[0][:, 0 : blocks * C2])
+                keep_positive("mask0", sign0, [0], 0)
+            elif n + 1 < len(units):
                 f1, b1 = units[n + 1][:2]
                 empty(*unit, raw_bytes(f1, b1, 0, blocks * C2))
-            elif n + 2 == len(units):
-                make_sign(0)
-                empty(*unit, a_sb[0][:, 0 : blocks * C2])
-                make_mask(0)
-                make_sign(1)
-                make_mask(1)
             else:
-                empty(*unit, raw_bytes(f, b0, 3, blocks * C2))
-                for b in (2, 3):
-                    make_sign(b)
-                    make_mask(b)
+                sign1 = last_raw[:, 1792:2048].bitcast(BF16).rearrange("p (b s) -> p b s", b=1)
+                nc.scalar.activation(sign1[:, 0, :], a_sb[1][:], ACT.Sign)
+                keep_positive("mask1", sign1, [1], 0)
+                empty(*unit, last_raw[:, 1792:2048])
+                early = last_raw[:, 704:1216].rearrange("p (b s) -> p b s", b=2)
+                nc.scalar.activation(early, a23[:, :, 0:C1], ACT.Sign)
+                keep_positive("mask23", early, [2, 3], 0)
+                sign_late = last_raw[:, 1408:1664].bitcast(BF16).rearrange("p (b s) -> p b s", b=2)
+                nc.scalar.activation(sign_late, a23[:, :, C1:T], ACT.Sign)
             scatter_dc(*unit)
 
-        last_raw = raw[E2 - 1, 0][0]
-        late = fresh("late", [P, 2 * C1], F32)
         picked = {(b, 0): fresh(f"lead{b}", [P, P], F32)[:] for b in range(4)}
         picked[3, P] = fresh("second3", [P, P], F32)[:]
         for b in range(3):
             picked[b, P] = last_raw[:, 768 + b * P : 768 + (b + 1) * P]
         picked[0, C1] = last_raw[:, 512:768]
         picked[1, C1] = last_raw[:, 1152:1408]
-        picked[2, C1] = late[:, 0:C1]
-        picked[3, C1] = late[:, C1 : 2 * C1]
+        for b in (2, 3):
+            picked[b, C1] = fresh(f"third{b}", [P, C1], F32)[:]
         turned = [fresh(f"turned{c}", [P, 2, P, 2], BF16) for c in range(4)]
         result = {}
 
@@ -211,7 +210,7 @@ def tile_moe_seb_relu_kernel(
             values = picked[b, first]
             count = values.shape[1]
             nc.vector.tensor_tensor(
-                values, dc[b][:].indirect(entries(list1, first, count)), mask[b][:, first : first + count], MULT
+                values, dc[b][:].indirect(entries(list1, first, count)), mask[b, first // C1 * C1][:, first % C1 : first % C1 + count], MULT
             )
 
         def scale_rows(c, b0, values):
@@ -262,11 +261,19 @@ def tile_moe_seb_relu_kernel(
         def product(first, count, words, numbers):
             halves = [bank(f"out_bank{first}_{n}", [P, 2, count], numbers[n]) for n in range(2)]
             multiply(first, count, words, lambda k: halves[k // 2][:, k % 2, :])
-            values = []
-            for n in range(2):
-                values.append(fresh(f"out_sums{first}_{n}", [P, 2, count], F32))
-                nc.scalar.activation(values[n][:], halves[n][:], ACT.Copy)
-            return [values[k // 2][:, k % 2, :] for k in range(4)]
+            return halves
+
+        def send(first, half, sums_bank, tag=None):
+            count = sums_bank.shape[-1]
+            values = fresh(f"out_sums{first}_{half}", [P, 2, count], F32, tag)
+            nc.scalar.activation(values[:], sums_bank[:], ACT.Copy)
+            for u in range(2):
+                k = 2 * half + u
+                if first == 0:
+                    result[k] = fresh(f"result{k}", [P, T], F32)
+                scatter_out(k, first, count, values[:, u, :])
+                if first == C1:
+                    nc.sync.dma_start(out[k * P : (k + 1) * P, :], result[k][:])
 
         for b in range(4):
             gather(b, 0)
@@ -276,29 +283,24 @@ def tile_moe_seb_relu_kernel(
             gather(b, C1)
         turn(0, [0, 1, 2], 4)
         turn(0, [3], 5)
-        turn_back([0], 6, late[:, P : 3 * P])
-        sums0 = product(0, P, late[:, P : 3 * P], (2, 3))
+        da0 = fresh("da0", [P, 2 * P], F32)
+        turn_back([0], 6, da0[:])
+        keep_positive("mask_late", sign_late, [2, 3], C1, "turned0")
+        sums0 = product(0, P, da0[:], (2, 3))
         for b in (2, 3):
             gather(b, C1)
         turn(1, [0, 1, 2, 3], 5)
-        for k in (0, 2):
-            result[k] = fresh(f"result{k}", [P, T], F32)
-            scatter_out(k, 0, P, sums0[k])
+        send(0, 0, sums0[0])
         da1 = fresh("da1", [P, 2 * P], F32)
         turn_back([1], 7, da1[:])
         sums1 = product(P, P, da1[:], (0, 1))
-        result[1] = fresh("result1", [P, T], F32, "da1")
-        scatter_out(1, 0, P, sums0[1])
+        send(0, 1, sums0[1], "turned1")
         turn(2, [0, 1, 2, 3], 6)
         turn(3, [0, 1, 2, 3], 7)
-        for k in range(3):
-            scatter_out(k, P, P, sums1[k])
+        send(P, 0, sums1[0])
         da23 = fresh("da23", [P, 2 * C1], F32)
         turn_back([2, 3], 4, da23[:])
         sums23 = product(C1, C1, da23[:], (2, 3))
-        result[3] = fresh("result3", [P, T], F32, "da23")
-        scatter_out(3, 0, P, sums0[3])
-        scatter_out(3, P, P, sums1[3])
-        for k in range(4):
-            scatter_out(k, C1, C1, sums23[k])
-            nc.sync.dma_start(out[k * P : (k + 1) * P, :], result[k][:])
+        send(P, 1, sums1[1], "turned3")
+        for half in range(2):
+            send(C1, half, sums23[half])

@@ -89,8 +89,15 @@ def tile_moe_seb_relu_kernel(
         load_w2(1, 0, 2)
         load_w2(1, 2, 2)
         nc.sync.dma_start(q_rest, gate2[:, C2:T])
-        load_w2(2, 0, 4)
-        load_w2(3, 0, 4)
+        load_w2(2, 0, 2)
+        load_w2(2, 2, 2)
+        load_w2(3, 0, 2)
+        last_raw = fresh("last_raw", [P, PACK * T], F32)
+        nc.sync.dma_start(
+            last_raw[:].rearrange("p (j i) -> p j i", j=PACK)[:, :, C1:T],
+            w2t[3].rearrange("(p j) i -> p j i", j=PACK)[:, :, C1:T],
+        )
+        raw[3, 2] = (last_raw, 0, 4)
         load_a(0)
         load_a(1)
         a23 = fresh("a23", [P, 2, T], F32)
@@ -155,7 +162,6 @@ def tile_moe_seb_relu_kernel(
                 nc.vector.tensor_tensor(dc[b0 + u][:].indirect(entries(list2, f * C2, C2)), values[:, u, :], q, MULT)
 
         mask = {}
-        last_raw = raw[E2 - 1, 0][0]
 
         def keep_positive(name, signs, blocks, first, tag=None):
             count = signs.shape[-1]
@@ -266,9 +272,13 @@ def tile_moe_seb_relu_kernel(
         def send(first, half, sums_bank, tag=None):
             count = sums_bank.shape[-1]
             values = fresh(f"out_sums{first}_{half}", [P, 2, count], F32, tag)
-            nc.scalar.activation(values[:], sums_bank[:], ACT.Copy)
+            alone = (first, half) == (0, 0)
+            if not alone:
+                nc.scalar.activation(values[:], sums_bank[:], ACT.Copy)
             for u in range(2):
                 k = 2 * half + u
+                if alone:
+                    nc.scalar.activation(values[:, u, :], sums_bank[:, u, :], ACT.Copy)
                 if first == 0:
                     result[k] = fresh(f"result{k}", [P, T], F32)
                 scatter_out(k, first, count, values[:, u, :])

@@ -21,6 +21,8 @@ E2, C2 = 4, 128
 PACK = 4
 WINDOW = 704
 REST = T - P
+PAD = 256
+SINGLES = 6
 FLOPS = 2 * 2 * 512 * 512 * 512
 
 
@@ -57,12 +59,13 @@ def tile_moe_seb_relu_kernel(
         nc.sync.dma_start(dy_w[:, 0:T], dy_words[0].rearrange("p t d -> p (t d)").bitcast(I32))
         nc.sync.dma_start(list2[:], offs2)
 
-        raw = {}
+        raw, padded = {}, {}
 
         def load_w2(f, b0, blocks):
             rows = w2t[f].rearrange("(p j) i -> p j i", j=PACK)
-            flat = fresh(f"raw{f}_{b0}", [P, PACK * blocks * P], F32)
-            piece = flat[:].rearrange("p (j i) -> p j i", j=PACK)
+            padded[f, b0] = fresh(f"raw{f}_{b0}", [P, PAD + PACK * blocks * P], F32)
+            flat = padded[f, b0][:, PAD:]
+            piece = flat.rearrange("p (j i) -> p j i", j=PACK)
             nc.sync.dma_start(piece, rows[:, :, b0 * P : (b0 + blocks) * P])
             for b in range(b0, b0 + blocks):
                 raw[f, b] = (flat, b0, blocks)
@@ -97,7 +100,7 @@ def tile_moe_seb_relu_kernel(
             last_raw[:].rearrange("p (j i) -> p j i", j=PACK)[:, :, C1:T],
             w2t[3].rearrange("(p j) i -> p j i", j=PACK)[:, :, C1:T],
         )
-        raw[3, 2] = (last_raw, 0, 4)
+        raw[3, 2] = (last_raw[:], 0, 4)
         load_a(0)
         load_a(1)
         a23 = fresh("a23", [P, 2, T], F32)
@@ -124,13 +127,25 @@ def tile_moe_seb_relu_kernel(
 
         dc, banks, sums = {}, {}, {}
 
+        def ahead(n):
+            return 2 if 3 <= n <= SINGLES else 1
+
+        def held_by(n):
+            if n == 3:
+                return "w2s00"
+            return f"w2c{n - ahead(n) - 1}" if n >= 2 else None
+
         def prepare(n, f, b0, blocks):
             flat, first, loaded = raw[f, b0]
-            woven = fresh(f"woven{n}", [P, blocks * P, PACK], BF16, f"w2c{n - 2}" if n >= 2 else None)
-            values = flat[:].rearrange("p (j i) -> p j i", j=PACK)[:, :, (b0 - first) * P : (b0 - first + blocks) * P]
-            nc.scalar.activation(
-                woven[:].rearrange("p (c i) j -> p c j i", i=4), values.rearrange("p j (c i) -> p c j i", i=4), ACT.Copy
-            )
+            woven = fresh(f"woven{n}", [P, blocks * P, PACK], BF16, held_by(n))
+            values = flat.rearrange("p (j i) -> p j i", j=PACK)[:, :, (b0 - first) * P : (b0 - first + blocks) * P]
+            half = blocks * P // 2 if n > 0 else P
+            for at in range(0, blocks * P, half):
+                nc.scalar.activation(
+                    woven[:, at : at + half, :].rearrange("p (c i) j -> p c j i", i=4),
+                    values[:, :, at : at + half].rearrange("p j (c i) -> p c j i", i=4),
+                    ACT.Copy,
+                )
             codes = fresh(f"w2c{n}", [P, blocks * P], U32)
             scales = fresh(f"w2s{f}{b0}", [P, blocks * P], U8)
             nc.vector.quantize_mx(
@@ -171,15 +186,17 @@ def tile_moe_seb_relu_kernel(
                 for at in range(0, count, C1):
                     mask[b, first + at] = made[:, n, at : at + C1]
 
-        units = [(0, b, 1) for b in range(4)] + [(f, b0, 2) for f in range(1, E2) for b0 in (0, 2)]
+        units = [(n // 4, n % 4, 1) for n in range(SINGLES)] + [(n // 4, n % 4, 2) for n in range(SINGLES, 16, 2)]
         prepare(0, *units[0])
         gq_s_rest = fresh("gq_s_rest", [P, REST], U8, "raw0_0")
         nc.vector.tensor_copy(gq_s_rest[:], dy_s[:].indirect(entries(list2, C2, REST)))
         for f in range(1, E2):
             gq_s[f] = gq_s_rest[:, (f - 1) * C2 : f * C2]
+        prepared = 1
         for n, unit in enumerate(units):
-            if n + 1 < len(units):
-                prepare(n + 1, *units[n + 1])
+            while prepared < len(units) and prepared - ahead(prepared) <= n:
+                prepare(prepared, *units[prepared])
+                prepared = prepared + 1
             f, b0, blocks = unit
             if n == len(units) - 2:
                 sign0 = raw_bytes(E2 - 1, 2, 0, 2 * P).bitcast(BF16).rearrange("p (b s) -> p b s", b=1)
@@ -187,8 +204,13 @@ def tile_moe_seb_relu_kernel(
                 empty(*unit, a_sb[0][:, 0 : blocks * C2])
                 keep_positive("mask0", sign0, [0], 0)
             elif n + 1 < len(units):
-                f1, b1 = units[n + 1][:2]
-                empty(*unit, raw_bytes(f1, b1, 0, blocks * C2))
+                f1, b1 = units[prepared - 1][:2]
+                first = raw[f1, b1][1]
+                end = PAD + 16 + (b1 - first) * 3 * P
+                if n == SINGLES - 1:
+                    empty(*unit, raw_bytes(f1, b1, 1, blocks * C2))
+                else:
+                    empty(*unit, padded[f1, first][:, end - blocks * C2 : end])
             else:
                 sign1 = last_raw[:, 1792:2048].bitcast(BF16).rearrange("p (b s) -> p b s", b=1)
                 nc.scalar.activation(sign1[:, 0, :], a_sb[1][:], ACT.Sign)
@@ -197,8 +219,6 @@ def tile_moe_seb_relu_kernel(
                 early = last_raw[:, 704:1216].rearrange("p (b s) -> p b s", b=2)
                 nc.scalar.activation(early, a23[:, :, 0:C1], ACT.Sign)
                 keep_positive("mask23", early, [2, 3], 0)
-                sign_late = last_raw[:, 1408:1664].bitcast(BF16).rearrange("p (b s) -> p b s", b=2)
-                nc.scalar.activation(sign_late, a23[:, :, C1:T], ACT.Sign)
             scatter_dc(*unit)
 
         picked = {(b, 0): fresh(f"lead{b}", [P, P], F32)[:] for b in range(4)}
@@ -207,8 +227,9 @@ def tile_moe_seb_relu_kernel(
             picked[b, P] = last_raw[:, 768 + b * P : 768 + (b + 1) * P]
         picked[0, C1] = last_raw[:, 512:768]
         picked[1, C1] = last_raw[:, 1152:1408]
+        late = fresh("late", [P, 2 * C1], F32)
         for b in (2, 3):
-            picked[b, C1] = fresh(f"third{b}", [P, C1], F32)[:]
+            picked[b, C1] = late[:, (b - 2) * C1 : (b - 1) * C1]
         turned = [fresh(f"turned{c}", [P, 2, P, 2], BF16) for c in range(4)]
         result = {}
 
@@ -293,10 +314,13 @@ def tile_moe_seb_relu_kernel(
             gather(b, C1)
         turn(0, [0, 1, 2], 4)
         turn(0, [3], 5)
-        da0 = fresh("da0", [P, 2 * P], F32)
-        turn_back([0], 6, da0[:])
-        keep_positive("mask_late", sign_late, [2, 3], C1, "turned0")
-        sums0 = product(0, P, da0[:], (2, 3))
+        da0 = late[:, P : 3 * P]
+        turn_back([0], 6, da0)
+        mask_late = fresh("mask_late", [P, 2, C1], F32, "turned0")
+        nc.vector.tensor_scalar(mask_late[:], a23[:, :, C1:T], 0.0, None, mybir.AluOpType.is_gt)
+        for b in (2, 3):
+            mask[b, C1] = mask_late[:, b - 2, :]
+        sums0 = product(0, P, da0, (2, 3))
         for b in (2, 3):
             gather(b, C1)
         turn(1, [0, 1, 2, 3], 5)

@@ -12,18 +12,21 @@ U8 = mybir.dt.uint8
 FP8X4 = mybir.dt.float8_e4m3fn_x4
 FP4X4 = mybir.dt.float4_e2m1fn_x4
 MULT = mybir.AluOpType.mult
+IS_GT = mybir.AluOpType.is_gt
 ACT = mybir.ActivationFunctionType
 
 P = 128
 T = 512
+BLOCKS = T // P
 E1, C1 = 2, 256
 E2, C2 = 4, 128
 PACK = 4
+LINE = 4
 WINDOW = 704
-REST = T - P
-PAD = 256
 SINGLES = 6
-FLOPS = 2 * 2 * 512 * 512 * 512
+OVERLAP = 16
+SUM_BANKS = 4
+FLOPS = 2 * 2 * T * T * T
 
 
 def tile_moe_seb_relu_kernel(
@@ -44,11 +47,14 @@ def tile_moe_seb_relu_kernel(
         def entries(lst, first, count):
             return lst[:, first // 16 : (first + count) // 16]
 
+        def by_block(columns):
+            return columns.rearrange("p (b s) -> p b s", b=2)
+
         list2 = lists.tile([P, T // 16], U16, name="list2")
         list1 = lists.tile([P, T // 16], U16, name="list1")
         dy_w = fresh("dy_w", [P, WINDOW], I32)
         dy_s = fresh("dy_s", [P, T], U8)
-        w1_w = fresh("w1_w", [P, E1 * 1024], U8)
+        w1_w = fresh("w1_w", [P, E1 * 2 * T], U8)
         w1_s = fresh("w1_s", [P, E1 * T], U8)
         identity = fresh("identity", [P, P], F32)
         nc.vector.memset(dy_s[:].bitcast(I32), 0)
@@ -56,55 +62,48 @@ def tile_moe_seb_relu_kernel(
         nc.gpsimd.memset(w1_s[:].bitcast(I32), 0)
         make_identity(nc, identity[:])
 
+        raw = {}
+
+        def raw_rows(f, b):
+            tile, spare = raw[f, b][:2]
+            return tile[:, spare:].rearrange("p (j i) -> p j i", j=PACK)
+
+        def load_w2(f, b0, blocks, spare):
+            tile = fresh(f"raw{f}_{b0}", [P, spare + PACK * blocks * P], F32)
+            for b in range(b0, b0 + blocks):
+                raw[f, b] = (tile, spare, b0, blocks)
+            rows = w2t[f].rearrange("(p j) i -> p j i", j=PACK)
+            nc.sync.dma_start(raw_rows(f, b0), rows[:, :, b0 * P : (b0 + blocks) * P])
+
+        def load_gate2(first, experts):
+            tile = fresh(f"q{first}", [P, experts * C2], F32)
+            nc.sync.dma_start(tile[:], gate2[:, first * C2 : (first + experts) * C2])
+            return [tile[:, n * C2 : (n + 1) * C2] for n in range(experts)]
+
+        def load_a(b0, spare):
+            tile = fresh(f"a{b0}", [P, 2 * T + spare], F32)
+            rows = a[b0 * P : (b0 + 2) * P, :].rearrange("(b p) s -> p b s", p=P)
+            nc.sync.dma_start(by_block(tile[:, 0 : 2 * T]), rows)
+            return tile
+
         nc.sync.dma_start(dy_w[:, 0:T], dy_words[0].rearrange("p t d -> p (t d)").bitcast(I32))
         nc.sync.dma_start(list2[:], offs2)
-
-        raw, padded = {}, {}
-
-        def load_w2(f, b0, blocks):
-            rows = w2t[f].rearrange("(p j) i -> p j i", j=PACK)
-            padded[f, b0] = fresh(f"raw{f}_{b0}", [P, PAD + PACK * blocks * P], F32)
-            flat = padded[f, b0][:, PAD:]
-            piece = flat.rearrange("p (j i) -> p j i", j=PACK)
-            nc.sync.dma_start(piece, rows[:, :, b0 * P : (b0 + blocks) * P])
-            for b in range(b0, b0 + blocks):
-                raw[f, b] = (flat, b0, blocks)
-
-        def raw_bytes(f, b0, j, columns):
-            flat, first, blocks = raw[f, b0]
-            at = (j * blocks + b0 - first) * P
-            return flat[:, at : at + columns]
-
-        a_sb = {}
-
-        def load_a(b):
-            a_sb[b] = fresh(f"a{b}", [P, T], F32)
-            nc.sync.dma_start(a_sb[b][:], a[b * P : (b + 1) * P, :])
-
-        q_first = fresh("q_first", [P, C2], F32)
-        q_rest = fresh("q_rest", [P, REST], F32)[:]
-        load_w2(0, 0, 1)
+        load_w2(0, 0, 1, 0)
         for r in range(4):
             nc.sync.dma_start(dy_s[r:P:32, :].bitcast(I32), dy_scales[0, r:16:4, :].bitcast(I32))
-        load_w2(0, 1, 1)
-        nc.sync.dma_start(q_first[:], gate2[:, 0:C2])
-        load_w2(0, 2, 2)
-        load_w2(1, 0, 2)
-        load_w2(1, 2, 2)
-        nc.sync.dma_start(q_rest, gate2[:, C2:T])
-        load_w2(2, 0, 2)
-        load_w2(2, 2, 2)
-        load_w2(3, 0, 2)
-        last_raw = fresh("last_raw", [P, PACK * T], F32)
-        nc.sync.dma_start(
-            last_raw[:].rearrange("p (j i) -> p j i", j=PACK)[:, :, C1:T],
-            w2t[3].rearrange("(p j) i -> p j i", j=PACK)[:, :, C1:T],
-        )
-        raw[3, 2] = (last_raw[:], 0, 4)
-        load_a(0)
-        load_a(1)
-        a23 = fresh("a23", [P, 2, T], F32)
-        nc.sync.dma_start(a23[:], a[2 * P : 4 * P, :].rearrange("(b p) s -> p b s", p=P))
+        load_w2(0, 1, 1, C2)
+        q = load_gate2(0, 1)
+        load_w2(0, 2, 2, 0)
+        load_w2(1, 0, 2, C2)
+        load_w2(1, 2, 2, C2)
+        q = q + load_gate2(1, 1)
+        load_w2(2, 0, 2, 0)
+        load_w2(2, 2, 2, 0)
+        q = q + load_gate2(2, 2)
+        load_w2(3, 0, 2, 0)
+        load_w2(3, 2, 2, T)
+        a01 = load_a(0, 3 * P + C1)
+        a23 = by_block(load_a(2, 0)[:])
         nc.sync.dma_start(list1[:], offs)
         g_col = fresh("g_col", [P, T // P], F32)
         with nc.allow_non_contiguous_dma(reason="one gate value a partition"):
@@ -123,39 +122,42 @@ def tile_moe_seb_relu_kernel(
         gq_s_first = fresh("gq_s_first", [P, C2], U8)
         nc.vector.tensor_copy(gq_w[:], dy_w[:].bitcast(U32).indirect(list2[:]))
         nc.vector.tensor_copy(gq_s_first[:], dy_s[:].indirect(entries(list2, 0, C2)))
-        gq_s = {0: gq_s_first[:]}
+        gq_s = [gq_s_first[:]]
 
-        dc, banks, sums = {}, {}, {}
+        units = [(n // BLOCKS, n % BLOCKS, 1) for n in range(SINGLES)]
+        units = units + [(n // BLOCKS, n % BLOCKS, 2) for n in range(SINGLES, E2 * BLOCKS, 2)]
+        dc, banks, mask = {}, {}, {}
 
         def ahead(n):
             return 2 if 3 <= n <= SINGLES else 1
 
-        def held_by(n):
-            if n == 3:
-                return "w2s00"
-            return f"w2c{n - ahead(n) - 1}" if n >= 2 else None
+        def woven_tag(n):
+            if n < 2:
+                return None
+            return "scales0" if n == 3 else f"codes{n - ahead(n) - 1}"
 
-        def prepare(n, f, b0, blocks):
-            flat, first, loaded = raw[f, b0]
-            woven = fresh(f"woven{n}", [P, blocks * P, PACK], BF16, held_by(n))
-            values = flat.rearrange("p (j i) -> p j i", j=PACK)[:, :, (b0 - first) * P : (b0 - first + blocks) * P]
-            half = blocks * P // 2 if n > 0 else P
-            for at in range(0, blocks * P, half):
+        def prepare(n):
+            f, b0, blocks = units[n]
+            at = (b0 - raw[f, b0][2]) * P
+            values = raw_rows(f, b0)[:, :, at : at + blocks * P]
+            woven = fresh(f"woven{n}", [P, blocks * P, PACK], BF16, woven_tag(n))
+            part = blocks * P // 2 if n > 0 else P
+            for c0 in range(0, blocks * P, part):
                 nc.scalar.activation(
-                    woven[:, at : at + half, :].rearrange("p (c i) j -> p c j i", i=4),
-                    values[:, :, at : at + half].rearrange("p j (c i) -> p c j i", i=4),
+                    woven[:, c0 : c0 + part, :].rearrange("p (c i) j -> p c j i", i=LINE),
+                    values[:, :, c0 : c0 + part].rearrange("p j (c i) -> p c j i", i=LINE),
                     ACT.Copy,
                 )
-            codes = fresh(f"w2c{n}", [P, blocks * P], U32)
-            scales = fresh(f"w2s{f}{b0}", [P, blocks * P], U8)
+            codes = fresh(f"codes{n}", [P, blocks * P], U32)
+            scales = fresh(f"scales{n}", [P, blocks * P], U8)
             nc.vector.quantize_mx(
                 out=codes[:].bitcast(FP8X4), scales=scales[:], in_=woven[:].rearrange("p i j -> p (i j)")
             )
-            banks[f, b0] = bank(f"sums_bank{f}{b0}", [P, blocks, C2], n % 4)
+            banks[n] = bank(f"sums_bank{n}", [P, blocks, C2], n % SUM_BANKS)
             for u in range(blocks):
                 cols = slice(u * P, (u + 1) * P)
                 nc.tensor.matmul_mx(
-                    out=banks[f, b0][:, u, :],
+                    out=banks[n][:, u, :],
                     lhsT=codes[:, cols].bitcast(FP8X4),
                     lhsT_scale=scales[:, cols],
                     rhs=gq_w[:, f * C2 : (f + 1) * C2].bitcast(FP8X4),
@@ -164,87 +166,89 @@ def tile_moe_seb_relu_kernel(
                     stop=True,
                 )
 
-        def empty(f, b0, blocks, place):
-            sums[f, b0] = place.rearrange("p (u s) -> p u s", u=blocks)
-            nc.scalar.activation(sums[f, b0], banks[f, b0][:], ACT.Copy)
+        def behind_weave(n, later):
+            f, b0, blocks = units[later]
+            tile, spare, first, loaded = raw[f, b0]
+            if units[n][2] == 2:
+                return [raw_rows(f, b0)[:, j, 0:C2] for j in range(2)]
+            if n == SINGLES - 1:
+                return [raw_rows(f, b0)[:, 1, 0:C2]]
+            end = spare + (b0 - first) * (loaded * P + P) + OVERLAP
+            return [tile[:, end - C2 : end]]
 
-        def scatter_dc(f, b0, blocks):
-            values = sums[f, b0]
-            q = q_first[:] if f == 0 else q_rest[:, (f - 1) * C2 : f * C2]
-            for u in range(blocks):
+        def empty(n, places):
+            for u, place in enumerate(places):
+                nc.scalar.activation(place, banks[n][:, u, :], ACT.Copy)
+
+        def scatter_dc(n, places):
+            f, b0 = units[n][:2]
+            for u, place in enumerate(places):
                 if f == 0:
                     dc[b0 + u] = fresh(f"dc{b0 + u}", [P, T], F32)
-                nc.vector.tensor_tensor(dc[b0 + u][:].indirect(entries(list2, f * C2, C2)), values[:, u, :], q, MULT)
+                nc.vector.tensor_tensor(dc[b0 + u][:].indirect(entries(list2, f * C2, C2)), place, q[f], MULT)
 
-        mask = {}
-
-        def keep_positive(name, signs, blocks, first, tag=None):
-            count = signs.shape[-1]
-            made = fresh(name, [P, len(blocks), count], F32, tag)
+        def keep_positive(b0, signs):
+            made = fresh(f"mask{b0}", list(signs.shape), F32)
             nc.scalar.activation(made[:], signs, ACT.Relu)
-            for n, b in enumerate(blocks):
-                for at in range(0, count, C1):
-                    mask[b, first + at] = made[:, n, at : at + C1]
+            for u in range(2):
+                for e in range(signs.shape[2] // C1):
+                    mask[b0 + u, e] = made[:, u, e * C1 : (e + 1) * C1]
 
-        units = [(n // 4, n % 4, 1) for n in range(SINGLES)] + [(n // 4, n % 4, 2) for n in range(SINGLES, 16, 2)]
-        prepare(0, *units[0])
-        gq_s_rest = fresh("gq_s_rest", [P, REST], U8, "raw0_0")
-        nc.vector.tensor_copy(gq_s_rest[:], dy_s[:].indirect(entries(list2, C2, REST)))
-        for f in range(1, E2):
-            gq_s[f] = gq_s_rest[:, (f - 1) * C2 : f * C2]
+        prepare(0)
+        gq_s_rest = fresh("gq_s_rest", [P, T - C2], U8, "raw0_0")
+        nc.vector.tensor_copy(gq_s_rest[:], dy_s[:].indirect(entries(list2, C2, T - C2)))
+        gq_s = gq_s + [gq_s_rest[:, (f - 1) * C2 : f * C2] for f in range(1, E2)]
         prepared = 1
-        for n, unit in enumerate(units):
-            while prepared < len(units) and prepared - ahead(prepared) <= n:
-                prepare(prepared, *units[prepared])
+        for n in range(len(units) - 2):
+            while prepared - ahead(prepared) <= n:
+                prepare(prepared)
                 prepared = prepared + 1
-            f, b0, blocks = unit
-            if n == len(units) - 2:
-                sign0 = raw_bytes(E2 - 1, 2, 0, 2 * P).bitcast(BF16).rearrange("p (b s) -> p b s", b=1)
-                nc.scalar.activation(sign0[:, 0, :], a_sb[0][:], ACT.Sign)
-                empty(*unit, a_sb[0][:, 0 : blocks * C2])
-                keep_positive("mask0", sign0, [0], 0)
-            elif n + 1 < len(units):
-                f1, b1 = units[prepared - 1][:2]
-                first = raw[f1, b1][1]
-                end = PAD + 16 + (b1 - first) * 3 * P
-                if n == SINGLES - 1:
-                    empty(*unit, raw_bytes(f1, b1, 1, blocks * C2))
-                else:
-                    empty(*unit, padded[f1, first][:, end - blocks * C2 : end])
-            else:
-                sign1 = last_raw[:, 1792:2048].bitcast(BF16).rearrange("p (b s) -> p b s", b=1)
-                nc.scalar.activation(sign1[:, 0, :], a_sb[1][:], ACT.Sign)
-                keep_positive("mask1", sign1, [1], 0)
-                empty(*unit, last_raw[:, 1792:2048])
-                early = last_raw[:, 704:1216].rearrange("p (b s) -> p b s", b=2)
-                nc.scalar.activation(early, a23[:, :, 0:C1], ACT.Sign)
-                keep_positive("mask23", early, [2, 3], 0)
-            scatter_dc(*unit)
+            places = behind_weave(n, prepared - 1)
+            empty(n, places)
+            scatter_dc(n, places)
 
-        picked = {(b, 0): fresh(f"lead{b}", [P, P], F32)[:] for b in range(4)}
+        last = len(units) - 1
+        prepare(last)
+        signs01 = by_block(raw[E2 - 1, 2][0][:, OVERLAP : T + OVERLAP].bitcast(BF16))
+        nc.scalar.activation(signs01, by_block(a01[:, 0 : 2 * T]), ACT.Sign)
+        places = [a01[:, u * C2 : (u + 1) * C2] for u in range(2)]
+        empty(last - 1, places)
+        keep_positive(0, signs01)
+        signs23 = by_block(a01[:, 2 * T - P // 2 : 3 * T - P // 2])
+        nc.scalar.activation(signs23, a23[:, :, 0:C1], ACT.Sign)
+        scatter_dc(last - 1, places)
+        places = [a23[:, u, 0:C2] for u in range(2)]
+        empty(last, places)
+        keep_positive(2, signs23)
+        scatter_dc(last, places)
+
+        picked = {(b, 0): fresh(f"first{b}", [P, P], F32)[:] for b in range(BLOCKS)}
         picked[3, P] = fresh("second3", [P, P], F32)[:]
         for b in range(3):
-            picked[b, P] = last_raw[:, 768 + b * P : 768 + (b + 1) * P]
-        picked[0, C1] = last_raw[:, 512:768]
-        picked[1, C1] = last_raw[:, 1152:1408]
+            picked[b, P] = a01[:, 2 * T + b * P : 2 * T + (b + 1) * P]
+        picked[0, C1] = a01[:, 2 * T - C1 : 2 * T]
+        picked[1, C1] = a01[:, 2 * T + 3 * P : 2 * T + 3 * P + C1]
         late = fresh("late", [P, 2 * C1], F32)
         for b in (2, 3):
             picked[b, C1] = late[:, (b - 2) * C1 : (b - 1) * C1]
-        turned = [fresh(f"turned{c}", [P, 2, P, 2], BF16) for c in range(4)]
+        turned = [fresh(f"turned{c}", [P, 2, P, 2], BF16) for c in range(T // P)]
         result = {}
 
         def gather(b, first):
             values = picked[b, first]
             count = values.shape[1]
-            nc.vector.tensor_tensor(
-                values, dc[b][:].indirect(entries(list1, first, count)), mask[b, first // C1 * C1][:, first % C1 : first % C1 + count], MULT
-            )
+            kept = mask[b, first // C1][:, first % C1 : first % C1 + count]
+            nc.vector.tensor_tensor(values, dc[b][:].indirect(entries(list1, first, count)), kept, MULT)
 
-        def scale_rows(c, b0, values):
-            blocks = values.shape[1] // P
+        def turn(c, b0, blocks, number):
+            first = min(c * P, C1)
+            rows = bank(f"rows{c}_{b0}", [P, blocks, P], number)
+            for u in range(blocks):
+                slots = picked[b0 + u, first][:, c * P - first : (c + 1) * P - first]
+                nc.tensor.transpose(rows[:, u, :], slots, identity[:])
             nc.scalar.activation(
-                turned[c][:, :, 32 * b0 : 32 * (b0 + blocks), :],
-                values.rearrange("s (p u e) -> s u p e", u=2, e=2),
+                turned[c][:, :, P // PACK * b0 : P // PACK * (b0 + blocks), :],
+                rows[:].rearrange("s b (p u e) -> s u (b p) e", u=2, e=2),
                 ACT.Copy,
                 scale=g_col[:, c : c + 1],
             )
@@ -259,82 +263,67 @@ def tile_moe_seb_relu_kernel(
                 words.rearrange("p (c s u) -> p c s u", c=len(cs), u=2), back[:].rearrange("p c u s -> p c s u")
             )
 
-        def multiply(first, count, words, target):
-            e = first // C1
-            codes = fresh(f"dac{first}", [P, count], U32)
-            scales = fresh(f"das{first}", [P, count], U8)
+        def product(first, words, numbers):
+            count, e = words.shape[1] // 2, first // C1
+            halves = [bank(f"out_bank{first}_{n}", [P, 2, count], numbers[n]) for n in range(2)]
+            codes = fresh(f"da_codes{first}", [P, count], U32)
+            scales = fresh(f"da_scales{first}", [P, count], U8)
             nc.vector.quantize_mx(out=codes[:].bitcast(FP8X4), scales=scales[:], in_=words.bitcast(BF16))
-            for k in range(4):
+            for k in range(BLOCKS):
+                column = e * T + k * P
                 nc.tensor.matmul_mx(
-                    out=target(k),
-                    lhsT=w1_w[:, e * 1024 + k * 256 : e * 1024 + (k + 1) * 256].bitcast(FP4X4),
-                    lhsT_scale=w1_s[:, e * T + k * P : e * T + (k + 1) * P],
+                    out=halves[k // 2][:, k % 2, :],
+                    lhsT=w1_w[:, 2 * column : 2 * (column + P)].bitcast(FP4X4),
+                    lhsT_scale=w1_s[:, column : column + P],
                     rhs=codes[:].bitcast(FP8X4),
                     rhs_scale=scales[:],
                     start=True,
                     stop=True,
                 )
-
-        def scatter_out(k, first, count, values):
-            nc.vector.tensor_copy(result[k][:].indirect(entries(list1, first, count)), values)
-
-        def turn(c, blocks, number):
-            first = min(c * P, C1)
-            rows = bank(f"rows{c}_{blocks[0]}", [P, len(blocks), P], number)
-            for n, b in enumerate(blocks):
-                nc.tensor.transpose(rows[:, n, :], picked[b, first][:, c * P - first : (c + 1) * P - first], identity[:])
-            scale_rows(c, blocks[0], rows[:].rearrange("s b i -> s (b i)"))
-
-        def product(first, count, words, numbers):
-            halves = [bank(f"out_bank{first}_{n}", [P, 2, count], numbers[n]) for n in range(2)]
-            multiply(first, count, words, lambda k: halves[k // 2][:, k % 2, :])
             return halves
 
         def send(first, half, sums_bank, tag=None):
             count = sums_bank.shape[-1]
             values = fresh(f"out_sums{first}_{half}", [P, 2, count], F32, tag)
-            alone = (first, half) == (0, 0)
-            if not alone:
+            one_by_one = (first, half) == (0, 0)
+            if not one_by_one:
                 nc.scalar.activation(values[:], sums_bank[:], ACT.Copy)
             for u in range(2):
                 k = 2 * half + u
-                if alone:
+                if one_by_one:
                     nc.scalar.activation(values[:, u, :], sums_bank[:, u, :], ACT.Copy)
                 if first == 0:
                     result[k] = fresh(f"result{k}", [P, T], F32)
-                scatter_out(k, first, count, values[:, u, :])
+                nc.vector.tensor_copy(result[k][:].indirect(entries(list1, first, count)), values[:, u, :])
                 if first == C1:
                     nc.sync.dma_start(out[k * P : (k + 1) * P, :], result[k][:])
 
-        for b in range(4):
-            gather(b, 0)
-        for b in range(4):
-            gather(b, P)
-        for b in range(2):
-            gather(b, C1)
-        turn(0, [0, 1, 2], 4)
-        turn(0, [3], 5)
+        for first, blocks in ((0, BLOCKS), (P, BLOCKS), (C1, 2)):
+            for b in range(blocks):
+                gather(b, first)
+        turn(0, 0, 2, 4)
+        turn(0, 2, 2, 5)
         da0 = late[:, P : 3 * P]
         turn_back([0], 6, da0)
         mask_late = fresh("mask_late", [P, 2, C1], F32, "turned0")
-        nc.vector.tensor_scalar(mask_late[:], a23[:, :, C1:T], 0.0, None, mybir.AluOpType.is_gt)
+        nc.vector.tensor_scalar(mask_late[:], a23[:, :, C1:T], 0.0, None, IS_GT)
         for b in (2, 3):
-            mask[b, C1] = mask_late[:, b - 2, :]
-        sums0 = product(0, P, da0, (2, 3))
+            mask[b, 1] = mask_late[:, b - 2, :]
+        sums0 = product(0, da0, (2, 3))
         for b in (2, 3):
             gather(b, C1)
-        turn(1, [0, 1, 2, 3], 5)
+        turn(1, 0, BLOCKS, 5)
         send(0, 0, sums0[0])
         da1 = fresh("da1", [P, 2 * P], F32)
         turn_back([1], 7, da1[:])
-        sums1 = product(P, P, da1[:], (0, 1))
+        sums1 = product(P, da1[:], (0, 1))
         send(0, 1, sums0[1], "turned1")
-        turn(2, [0, 1, 2, 3], 6)
-        turn(3, [0, 1, 2, 3], 7)
+        turn(2, 0, BLOCKS, 6)
+        turn(3, 0, BLOCKS, 7)
         send(P, 0, sums1[0])
         da23 = fresh("da23", [P, 2 * C1], F32)
         turn_back([2, 3], 4, da23[:])
-        sums23 = product(C1, C1, da23[:], (2, 3))
+        sums23 = product(C1, da23[:], (2, 3))
         send(P, 1, sums1[1], "turned3")
         for half in range(2):
             send(C1, half, sums23[half])

@@ -1,7 +1,6 @@
 from contextlib import ExitStack
 
 import concourse.mybir as mybir
-from concourse.masks import make_identity
 
 F32 = mybir.dt.float32
 BF16 = mybir.dt.bfloat16
@@ -13,19 +12,14 @@ FP8X4 = mybir.dt.float8_e4m3fn_x4
 FP4X4 = mybir.dt.float4_e2m1fn_x4
 MULT = mybir.AluOpType.mult
 IS_GT = mybir.AluOpType.is_gt
-ACT = mybir.ActivationFunctionType
+COPY = mybir.ActivationFunctionType.Copy
 
 P = 128
 T = 512
-BLOCKS = T // P
 E1, C1 = 2, 256
 E2, C2 = 4, 128
 PACK = 4
-LINE = 4
-WINDOW = 704
-SINGLES = 6
-OVERLAP = 16
-SUM_BANKS = 4
+HALF = P // 2
 FLOPS = 2 * 2 * T * T * T
 
 
@@ -47,67 +41,49 @@ def tile_moe_seb_relu_kernel(
         def entries(lst, first, count):
             return lst[:, first // 16 : (first + count) // 16]
 
-        def by_block(columns):
-            return columns.rearrange("p (b s) -> p b s", b=2)
+        def copy(on_vector, dst, src):
+            if on_vector:
+                nc.vector.tensor_copy(dst, src)
+            else:
+                nc.scalar.activation(dst, src, COPY)
 
         list2 = lists.tile([P, T // 16], U16, name="list2")
         list1 = lists.tile([P, T // 16], U16, name="list1")
-        dy_w = fresh("dy_w", [P, WINDOW], I32)
+        dy_w = fresh("dy_w", [P, T], I32)
         dy_s = fresh("dy_s", [P, T], U8)
         w1_w = fresh("w1_w", [P, E1 * 2 * T], U8)
         w1_s = fresh("w1_s", [P, E1 * T], U8)
-        identity = fresh("identity", [P, P], F32)
         nc.vector.memset(dy_s[:].bitcast(I32), 0)
-        nc.vector.memset(dy_w[:, T:WINDOW], 0)
         nc.gpsimd.memset(w1_s[:].bitcast(I32), 0)
-        make_identity(nc, identity[:])
 
         raw = {}
 
-        def raw_rows(f, b):
-            tile, spare = raw[f, b][:2]
-            return tile[:, spare:].rearrange("p (j i) -> p j i", j=PACK)
-
-        def load_w2(f, b0, blocks, spare):
-            tile = fresh(f"raw{f}_{b0}", [P, spare + PACK * blocks * P], F32)
-            for b in range(b0, b0 + blocks):
-                raw[f, b] = (tile, spare, b0, blocks)
+        def load_w2(f, h):
+            raw[f, h] = fresh(f"raw{f}_{h}", [P, PACK, T // 2], F32)
             rows = w2t[f].rearrange("(p j) i -> p j i", j=PACK)
-            nc.sync.dma_start(raw_rows(f, b0), rows[:, :, b0 * P : (b0 + blocks) * P])
+            nc.sync.dma_start(raw[f, h][:], rows[:, :, h * (T // 2) : (h + 1) * (T // 2)])
 
-        def load_gate2(first, experts):
-            tile = fresh(f"q{first}", [P, experts * C2], F32)
-            nc.sync.dma_start(tile[:], gate2[:, first * C2 : (first + experts) * C2])
-            return [tile[:, n * C2 : (n + 1) * C2] for n in range(experts)]
-
-        def load_a(b0, spare):
-            tile = fresh(f"a{b0}", [P, 2 * T + spare], F32)
-            rows = a[b0 * P : (b0 + 2) * P, :].rearrange("(b p) s -> p b s", p=P)
-            nc.sync.dma_start(by_block(tile[:, 0 : 2 * T]), rows)
-            return tile
-
-        nc.sync.dma_start(dy_w[:, 0:T], dy_words[0].rearrange("p t d -> p (t d)").bitcast(I32))
+        nc.sync.dma_start(dy_w[:], dy_words[0].rearrange("p t d -> p (t d)").bitcast(I32))
         nc.sync.dma_start(list2[:], offs2)
-        load_w2(0, 0, 1, 0)
+        load_w2(0, 0)
         for r in range(4):
             nc.sync.dma_start(dy_s[r:P:32, :].bitcast(I32), dy_scales[0, r:16:4, :].bitcast(I32))
-        load_w2(0, 1, 1, C2)
-        q = load_gate2(0, 1)
-        load_w2(0, 2, 2, 0)
-        load_w2(1, 0, 2, C2)
-        load_w2(1, 2, 2, C2)
-        q = q + load_gate2(1, 1)
-        load_w2(2, 0, 2, 0)
-        load_w2(2, 2, 2, 0)
-        q = q + load_gate2(2, 2)
-        load_w2(3, 0, 2, 0)
-        load_w2(3, 2, 2, T)
-        a01 = load_a(0, 3 * P + C1)
-        a23 = by_block(load_a(2, 0)[:])
+        load_w2(0, 1)
+        q_first = fresh("q_first", [P, C2], F32)
+        nc.sync.dma_start(q_first[:], gate2[:, 0:C2])
+        load_w2(1, 0)
+        load_w2(1, 1)
+        q_rest = fresh("q_rest", [P, T - C2], F32)
+        nc.sync.dma_start(q_rest[:], gate2[:, C2:T])
+        q = [q_first[:]] + [q_rest[:, n * C2 : (n + 1) * C2] for n in range(E2 - 1)]
+        for f in (2, 3):
+            for h in range(2):
+                load_w2(f, h)
+        g = fresh("g", [P, T], F32)
+        nc.sync.dma_start(g[:], gate1)
+        a_sb = fresh("a_sb", [P, PACK, T], F32)
+        nc.sync.dma_start(a_sb[:], a.rearrange("(p t) s -> p t s", t=PACK))
         nc.sync.dma_start(list1[:], offs)
-        g_col = fresh("g_col", [P, T // P], F32)
-        with nc.allow_non_contiguous_dma(reason="one gate value a partition"):
-            nc.sync.dma_start(g_col[:], gate1[0].rearrange("(c p) -> p c", p=P))
         nc.sync.dma_start(
             w1_w[:].bitcast(I32).rearrange("p (e c) -> p e c", e=E1),
             w1t_words[:, 0].bitcast(I32).rearrange("e p c -> p e c"),
@@ -119,211 +95,117 @@ def tile_moe_seb_relu_kernel(
             )
 
         gq_w = fresh("gq_w", [P, T], U32)
-        gq_s_first = fresh("gq_s_first", [P, C2], U8)
-        nc.vector.tensor_copy(gq_w[:], dy_w[:].bitcast(U32).indirect(list2[:]))
-        nc.vector.tensor_copy(gq_s_first[:], dy_s[:].indirect(entries(list2, 0, C2)))
-        gq_s = [gq_s_first[:]]
+        gq_s = fresh("gq_s", [P, T], U8)
+        for first, count in ((0, C2), (C2, T - C2)):
+            cols = slice(first, first + count)
+            nc.vector.tensor_copy(gq_w[:, cols], dy_w[:].bitcast(U32).indirect(entries(list2, first, count)))
+        for first, count in ((0, C2), (C2, T - C2)):
+            cols = slice(first, first + count)
+            nc.vector.tensor_copy(gq_s[:, cols], dy_s[:].indirect(entries(list2, first, count)))
 
-        units = [(n // BLOCKS, n % BLOCKS, 1) for n in range(SINGLES)]
-        units = units + [(n // BLOCKS, n % BLOCKS, 2) for n in range(SINGLES, E2 * BLOCKS, 2)]
-        dc, banks, mask = {}, {}, {}
+        dc = [fresh(f"dc{t}", [P, T], F32) for t in range(PACK)]
+        sums = [fresh(f"sums{n}", [P, PACK, 2, C2], F32) for n in range(E2 // 2)]
 
-        def ahead(n):
-            return 2 if 3 <= n <= SINGLES else 1
+        def weave(f, woven, m0, m1, on_vector):
+            h = m0 // HALF
+            src = raw[f, h][:].rearrange("p j (m t) -> p m j t", t=PACK)[:, m0 - h * HALF : m1 - h * HALF]
+            copy(on_vector, woven[:].rearrange("p t m j -> p m j t")[:, m0:m1], src)
 
-        def woven_tag(n):
-            if n < 2:
-                return None
-            return "scales0" if n == 3 else f"codes{n - ahead(n) - 1}"
-
-        def prepare(n):
-            f, b0, blocks = units[n]
-            at = (b0 - raw[f, b0][2]) * P
-            values = raw_rows(f, b0)[:, :, at : at + blocks * P]
-            woven = fresh(f"woven{n}", [P, blocks * P, PACK], BF16, woven_tag(n))
-            part = blocks * P // 2 if n > 0 else P
-            for c0 in range(0, blocks * P, part):
-                nc.scalar.activation(
-                    woven[:, c0 : c0 + part, :].rearrange("p (c i) j -> p c j i", i=LINE),
-                    values[:, :, c0 : c0 + part].rearrange("p j (c i) -> p c j i", i=LINE),
-                    ACT.Copy,
-                )
-            codes = fresh(f"codes{n}", [P, blocks * P], U32)
-            scales = fresh(f"scales{n}", [P, blocks * P], U8)
+        def multiply(f, t0, t1, woven, codes, scales, number):
+            cols = slice(t0 * P, t1 * P)
             nc.vector.quantize_mx(
-                out=codes[:].bitcast(FP8X4), scales=scales[:], in_=woven[:].rearrange("p i j -> p (i j)")
+                out=codes[:, cols].bitcast(FP8X4),
+                scales=scales[:, cols],
+                in_=woven[:, t0:t1].rearrange("p t m j -> p (t m j)"),
             )
-            banks[n] = bank(f"sums_bank{n}", [P, blocks, C2], n % SUM_BANKS)
-            for u in range(blocks):
-                cols = slice(u * P, (u + 1) * P)
+            acc = bank(f"acc{f}_{t0}", [P, t1 - t0, C2], number)
+            for t in range(t0, t1):
+                cols = slice(t * P, (t + 1) * P)
                 nc.tensor.matmul_mx(
-                    out=banks[n][:, u, :],
+                    out=acc[:, t - t0, :],
                     lhsT=codes[:, cols].bitcast(FP8X4),
                     lhsT_scale=scales[:, cols],
                     rhs=gq_w[:, f * C2 : (f + 1) * C2].bitcast(FP8X4),
-                    rhs_scale=gq_s[f],
+                    rhs_scale=gq_s[:, f * C2 : (f + 1) * C2],
                     start=True,
                     stop=True,
                 )
-
-        def behind_weave(n, later):
-            f, b0, blocks = units[later]
-            tile, spare, first, loaded = raw[f, b0]
-            if units[n][2] == 2:
-                return [raw_rows(f, b0)[:, j, 0:C2] for j in range(2)]
-            if n == SINGLES - 1:
-                return [raw_rows(f, b0)[:, 1, 0:C2]]
-            end = spare + (b0 - first) * (loaded * P + P) + OVERLAP
-            return [tile[:, end - C2 : end]]
-
-        def empty(n, places):
-            for u, place in enumerate(places):
-                nc.scalar.activation(place, banks[n][:, u, :], ACT.Copy)
-
-        def scatter_dc(n, places):
-            f, b0 = units[n][:2]
-            for u, place in enumerate(places):
-                if f == 0:
-                    dc[b0 + u] = fresh(f"dc{b0 + u}", [P, T], F32)
-                nc.vector.tensor_tensor(dc[b0 + u][:].indirect(entries(list2, f * C2, C2)), place, q[f], MULT)
-
-        def keep_positive(b0, signs):
-            made = fresh(f"mask{b0}", list(signs.shape), F32)
-            nc.scalar.activation(made[:], signs, ACT.Relu)
-            for u in range(2):
-                for e in range(signs.shape[2] // C1):
-                    mask[b0 + u, e] = made[:, u, e * C1 : (e + 1) * C1]
-
-        prepare(0)
-        gq_s_rest = fresh("gq_s_rest", [P, T - C2], U8, "raw0_0")
-        nc.vector.tensor_copy(gq_s_rest[:], dy_s[:].indirect(entries(list2, C2, T - C2)))
-        gq_s = gq_s + [gq_s_rest[:, (f - 1) * C2 : f * C2] for f in range(1, E2)]
-        prepared = 1
-        for n in range(len(units) - 2):
-            while prepared - ahead(prepared) <= n:
-                prepare(prepared)
-                prepared = prepared + 1
-            places = behind_weave(n, prepared - 1)
-            empty(n, places)
-            scatter_dc(n, places)
-
-        last = len(units) - 1
-        prepare(last)
-        signs01 = by_block(raw[E2 - 1, 2][0][:, OVERLAP : T + OVERLAP].bitcast(BF16))
-        nc.scalar.activation(signs01, by_block(a01[:, 0 : 2 * T]), ACT.Sign)
-        places = [a01[:, u * C2 : (u + 1) * C2] for u in range(2)]
-        empty(last - 1, places)
-        keep_positive(0, signs01)
-        signs23 = by_block(a01[:, 2 * T - P // 2 : 3 * T - P // 2])
-        nc.scalar.activation(signs23, a23[:, :, 0:C1], ACT.Sign)
-        scatter_dc(last - 1, places)
-        places = [a23[:, u, 0:C2] for u in range(2)]
-        empty(last, places)
-        keep_positive(2, signs23)
-        scatter_dc(last, places)
-
-        picked = {(b, 0): fresh(f"first{b}", [P, P], F32)[:] for b in range(BLOCKS)}
-        picked[3, P] = fresh("second3", [P, P], F32)[:]
-        for b in range(3):
-            picked[b, P] = a01[:, 2 * T + b * P : 2 * T + (b + 1) * P]
-        picked[0, C1] = a01[:, 2 * T - C1 : 2 * T]
-        picked[1, C1] = a01[:, 2 * T + 3 * P : 2 * T + 3 * P + C1]
-        late = fresh("late", [P, 2 * C1], F32)
-        for b in (2, 3):
-            picked[b, C1] = late[:, (b - 2) * C1 : (b - 1) * C1]
-        turned = [fresh(f"turned{c}", [P, 2, P, 2], BF16) for c in range(T // P)]
-        result = {}
-
-        def gather(b, first):
-            values = picked[b, first]
-            count = values.shape[1]
-            kept = mask[b, first // C1][:, first % C1 : first % C1 + count]
-            nc.vector.tensor_tensor(values, dc[b][:].indirect(entries(list1, first, count)), kept, MULT)
-
-        def turn(c, b0, blocks, number):
-            first = min(c * P, C1)
-            rows = bank(f"rows{c}_{b0}", [P, blocks, P], number)
-            for u in range(blocks):
-                slots = picked[b0 + u, first][:, c * P - first : (c + 1) * P - first]
-                nc.tensor.transpose(rows[:, u, :], slots, identity[:])
-            nc.scalar.activation(
-                turned[c][:, :, P // PACK * b0 : P // PACK * (b0 + blocks), :],
-                rows[:].rearrange("s b (p u e) -> s u (b p) e", u=2, e=2),
-                ACT.Copy,
-                scale=g_col[:, c : c + 1],
+            nc.vector.tensor_tensor(
+                sums[f // 2][:, t0:t1, f % 2, :], acc[:], q[f].unsqueeze(1).to_broadcast([P, t1 - t0, C2]), MULT
             )
 
-        def turn_back(cs, number, words):
-            back = bank(f"back{cs[0]}", [P, len(cs), 2, P], number)
-            for n, c in enumerate(cs):
-                pairs = turned[c][:].rearrange("s u p e -> s (u p e)").bitcast(F32)
+        def scatter_dc(t, f, experts):
+            values = sums[f // 2][:, t, f % 2 : f % 2 + experts, :].rearrange("p f s -> p (f s)")
+            nc.scalar.activation(dc[t][:].indirect(entries(list2, f * C2, experts * C2)), values, COPY)
+
+        for f in range(E2):
+            woven = fresh(f"woven{f}", [P, PACK, P, PACK], BF16)
+            codes = fresh(f"codes{f}", [P, T], U32)
+            scales = fresh(f"scales{f}", [P, T], U8)
+            if f == 0:
+                weave(f, woven, 0, HALF, False)
+                weave(f, woven, HALF, HALF + 44, True)
+                weave(f, woven, HALF + 44, P, False)
+                multiply(f, 0, 1, woven, codes, scales, 4)
+                multiply(f, 1, PACK, woven, codes, scales, 0)
+            else:
+                weave(f, woven, 0, HALF, True)
+                weave(f, woven, HALF, P, True)
+                multiply(f, 0, PACK, woven, codes, scales, f)
+            for t in range(PACK if f < 2 else 2):
+                scatter_dc(t, f, 1)
+        for t in (2, 3):
+            scatter_dc(t, 2, 2)
+
+        keep = fresh("keep", [P, PACK, T], F32)
+        for t in range(PACK):
+            nc.vector.scalar_tensor_tensor(keep[:, t, :], a_sb[:, t, :], 0.0, g[:], IS_GT, MULT)
+        picked = fresh("picked", [P, PACK, T], F32)
+
+        def gather(t, first, count):
+            cols = slice(first, first + count)
+            nc.vector.tensor_tensor(
+                picked[:, t, cols], dc[t][:].indirect(entries(list1, first, count)), keep[:, t, cols], MULT
+            )
+
+        pieces = ((0, P), (P, P), (C1, C1))
+        for t in range(PACK - 1):
+            for e in range(E1):
+                gather(t, e * C1, C1)
+        for first, count in pieces:
+            gather(PACK - 1, first, count)
+
+        result = [fresh(f"result{k}", [P, T], F32) for k in range(T // P)]
+        for n, (first, count) in enumerate(pieces):
+            e = first // C1
+            da = fresh(f"da{n}", [P, count, PACK], BF16)
+            copy(
+                n == 2,
+                da[:].rearrange("p (c i) t -> p c t i", i=4),
+                picked[:, :, first : first + count].rearrange("p t (c i) -> p c t i", i=4),
+            )
+            codes = fresh(f"da_codes{n}", [P, count], U32)
+            scales = fresh(f"da_scales{n}", [P, count], U8)
+            nc.vector.quantize_mx(
+                out=codes[:].bitcast(FP8X4), scales=scales[:], in_=da[:].rearrange("p s t -> p (s t)")
+            )
+            for half in range(2):
+                acc = bank(f"out_acc{n}_{half}", [P, 2, count], (5 + 2 * n + half) % 8)
                 for u in range(2):
-                    nc.tensor.transpose(back[:, n, u, :], pairs[:, u * P : (u + 1) * P], identity[:])
-            nc.scalar.copy(
-                words.rearrange("p (c s u) -> p c s u", c=len(cs), u=2), back[:].rearrange("p c u s -> p c s u")
-            )
-
-        def product(first, words, numbers):
-            count, e = words.shape[1] // 2, first // C1
-            halves = [bank(f"out_bank{first}_{n}", [P, 2, count], numbers[n]) for n in range(2)]
-            codes = fresh(f"da_codes{first}", [P, count], U32)
-            scales = fresh(f"da_scales{first}", [P, count], U8)
-            nc.vector.quantize_mx(out=codes[:].bitcast(FP8X4), scales=scales[:], in_=words.bitcast(BF16))
-            for k in range(BLOCKS):
-                column = e * T + k * P
-                nc.tensor.matmul_mx(
-                    out=halves[k // 2][:, k % 2, :],
-                    lhsT=w1_w[:, 2 * column : 2 * (column + P)].bitcast(FP4X4),
-                    lhsT_scale=w1_s[:, column : column + P],
-                    rhs=codes[:].bitcast(FP8X4),
-                    rhs_scale=scales[:],
-                    start=True,
-                    stop=True,
-                )
-            return halves
-
-        def send(first, half, sums_bank, tag=None):
-            count = sums_bank.shape[-1]
-            values = fresh(f"out_sums{first}_{half}", [P, 2, count], F32, tag)
-            one_by_one = (first, half) == (0, 0)
-            if not one_by_one:
-                nc.scalar.activation(values[:], sums_bank[:], ACT.Copy)
-            for u in range(2):
-                k = 2 * half + u
-                if one_by_one:
-                    nc.scalar.activation(values[:, u, :], sums_bank[:, u, :], ACT.Copy)
-                if first == 0:
-                    result[k] = fresh(f"result{k}", [P, T], F32)
-                nc.vector.tensor_copy(result[k][:].indirect(entries(list1, first, count)), values[:, u, :])
-                if first == C1:
-                    nc.sync.dma_start(out[k * P : (k + 1) * P, :], result[k][:])
-
-        for first, blocks in ((0, BLOCKS), (P, BLOCKS), (C1, 2)):
-            for b in range(blocks):
-                gather(b, first)
-        turn(0, 0, 2, 4)
-        turn(0, 2, 2, 5)
-        da0 = late[:, P : 3 * P]
-        turn_back([0], 6, da0)
-        mask_late = fresh("mask_late", [P, 2, C1], F32, "turned0")
-        nc.vector.tensor_scalar(mask_late[:], a23[:, :, C1:T], 0.0, None, IS_GT)
-        for b in (2, 3):
-            mask[b, 1] = mask_late[:, b - 2, :]
-        sums0 = product(0, da0, (2, 3))
-        for b in (2, 3):
-            gather(b, C1)
-        turn(1, 0, BLOCKS, 5)
-        send(0, 0, sums0[0])
-        da1 = fresh("da1", [P, 2 * P], F32)
-        turn_back([1], 7, da1[:])
-        sums1 = product(P, da1[:], (0, 1))
-        send(0, 1, sums0[1], "turned1")
-        turn(2, 0, BLOCKS, 6)
-        turn(3, 0, BLOCKS, 7)
-        send(P, 0, sums1[0])
-        da23 = fresh("da23", [P, 2 * C1], F32)
-        turn_back([2, 3], 4, da23[:])
-        sums23 = product(C1, da23[:], (2, 3))
-        send(P, 1, sums1[1], "turned3")
-        for half in range(2):
-            send(C1, half, sums23[half])
+                    column = e * T + (2 * half + u) * P
+                    nc.tensor.matmul_mx(
+                        out=acc[:, u, :],
+                        lhsT=w1_w[:, 2 * column : 2 * (column + P)].bitcast(FP4X4),
+                        lhsT_scale=w1_s[:, column : column + P],
+                        rhs=codes[:].bitcast(FP8X4),
+                        rhs_scale=scales[:],
+                        start=True,
+                        stop=True,
+                    )
+                values = fresh(f"out_sums{n}_{half}", [P, 2, count], F32)
+                copy(half == 1, values[:], acc[:])
+                for u in range(2):
+                    k = 2 * half + u
+                    copy(half == 1, result[k][:].indirect(entries(list1, first, count)), values[:, u, :])
+                    if n == len(pieces) - 1:
+                        nc.sync.dma_start(out[k * P : (k + 1) * P, :], result[k][:])

@@ -53,15 +53,15 @@ def tile_moe_seb_relu_kernel(
         dy_s = fresh("dy_s", [P, T], U8)
         w1_w = fresh("w1_w", [P, E1 * 2 * T], U8)
         w1_s = fresh("w1_s", [P, E1 * T], U8)
-        nc.vector.memset(dy_s[:].bitcast(I32), 0)
-        nc.gpsimd.memset(w1_s[:].bitcast(I32), 0)
+        nc.gpsimd.memset(dy_s[:].bitcast(I32), 0)
+        nc.vector.memset(w1_s[:].bitcast(I32), 0)
 
         raw = {}
 
-        def load_w2(f, h):
-            raw[f, h] = fresh(f"raw{f}_{h}", [P, PACK, T // 2], F32)
+        def load_w2(f, h, width=T // 2):
+            raw[f, h] = fresh(f"raw{f}_{h}", [P, PACK, width], F32)
             rows = w2t[f].rearrange("(p j) i -> p j i", j=PACK)
-            nc.sync.dma_start(raw[f, h][:], rows[:, :, h * (T // 2) : (h + 1) * (T // 2)])
+            nc.sync.dma_start(raw[f, h][:], rows[:, :, h * width : (h + 1) * width])
 
         nc.sync.dma_start(dy_w[:], dy_words[0].rearrange("p t d -> p (t d)").bitcast(I32))
         nc.sync.dma_start(list2[:], offs2)
@@ -77,12 +77,14 @@ def tile_moe_seb_relu_kernel(
         nc.sync.dma_start(q_rest[:], gate2[:, C2:T])
         q = [q_first[:]] + [q_rest[:, n * C2 : (n + 1) * C2] for n in range(E2 - 1)]
         for f in (2, 3):
-            for h in range(2):
-                load_w2(f, h)
+            load_w2(f, 0, T)
         g = fresh("g", [P, T], F32)
         nc.sync.dma_start(g[:], gate1)
-        a_sb = fresh("a_sb", [P, PACK, T], F32)
-        nc.sync.dma_start(a_sb[:], a.rearrange("(p t) s -> p t s", t=PACK))
+        a_rows = a.rearrange("(p t) s -> p t s", t=PACK)
+        a_first = fresh("a_first", [P, 1, T], F32)
+        a_rest = fresh("a_rest", [P, PACK - 1, T], F32)
+        nc.sync.dma_start(a_first[:], a_rows[:, 0:1, :])
+        nc.sync.dma_start(a_rest[:], a_rows[:, 1:PACK, :])
         nc.sync.dma_start(list1[:], offs)
         nc.sync.dma_start(
             w1_w[:].bitcast(I32).rearrange("p (e c) -> p e c", e=E1),
@@ -103,96 +105,139 @@ def tile_moe_seb_relu_kernel(
             cols = slice(first, first + count)
             nc.vector.tensor_copy(gq_s[:, cols], dy_s[:].indirect(entries(list2, first, count)))
 
+        made = {}
         dc = [fresh(f"dc{t}", [P, T], F32) for t in range(PACK)]
-        sums = [fresh(f"sums{n}", [P, PACK, 2, C2], F32) for n in range(E2 // 2)]
 
-        def weave(f, woven, m0, m1, on_vector):
-            h = m0 // HALF
-            src = raw[f, h][:].rearrange("p j (m t) -> p m j t", t=PACK)[:, m0 - h * HALF : m1 - h * HALF]
-            copy(on_vector, woven[:].rearrange("p t m j -> p m j t")[:, m0:m1], src)
+        def weave(source, m0, woven, t0, on_vector):
+            planes = woven.shape[1]
+            src = source[:].rearrange("p j (m t) -> p m j t", t=PACK)[:, :, :, t0 : t0 + planes]
+            copy(on_vector, woven[:].rearrange("p t m j -> p m j t")[:, m0 : m0 + src.shape[1]], src)
 
-        def multiply(f, t0, t1, woven, codes, scales, number):
-            cols = slice(t0 * P, t1 * P)
+        def quantise(f, t0, woven):
+            width = woven.shape[1] * P
+            codes = fresh(f"codes{f}_{t0}", [P, width], U32)
+            scales = fresh(f"scales{f}_{t0}", [P, width], U8)
+            made[f, t0] = scales
             nc.vector.quantize_mx(
-                out=codes[:, cols].bitcast(FP8X4),
-                scales=scales[:, cols],
-                in_=woven[:, t0:t1].rearrange("p t m j -> p (t m j)"),
+                out=codes[:].bitcast(FP8X4), scales=scales[:], in_=woven[:].rearrange("p t m j -> p (t m j)")
             )
-            acc = bank(f"acc{f}_{t0}", [P, t1 - t0, C2], number)
-            for t in range(t0, t1):
-                cols = slice(t * P, (t + 1) * P)
+            return [(codes[:, c : c + P], scales[:, c : c + P]) for c in range(0, width, P)]
+
+        def multiply(f, acc, operands):
+            for u, (codes, scales) in enumerate(operands):
                 nc.tensor.matmul_mx(
-                    out=acc[:, t - t0, :],
-                    lhsT=codes[:, cols].bitcast(FP8X4),
-                    lhsT_scale=scales[:, cols],
+                    out=acc[:, u, :],
+                    lhsT=codes.bitcast(FP8X4),
+                    lhsT_scale=scales,
                     rhs=gq_w[:, f * C2 : (f + 1) * C2].bitcast(FP8X4),
                     rhs_scale=gq_s[:, f * C2 : (f + 1) * C2],
                     start=True,
                     stop=True,
                 )
-            nc.vector.tensor_tensor(
-                sums[f // 2][:, t0:t1, f % 2, :], acc[:], q[f].unsqueeze(1).to_broadcast([P, t1 - t0, C2]), MULT
-            )
 
-        def scatter_dc(t, f, experts):
-            values = sums[f // 2][:, t, f % 2 : f % 2 + experts, :].rearrange("p f s -> p (f s)")
-            nc.scalar.activation(dc[t][:].indirect(entries(list2, f * C2, experts * C2)), values, COPY)
+        def gated(f, place, acc):
+            nc.vector.tensor_tensor(place, acc, q[f].unsqueeze(1).to_broadcast(list(place.shape)), MULT)
 
-        for f in range(E2):
-            woven = fresh(f"woven{f}", [P, PACK, P, PACK], BF16)
-            codes = fresh(f"codes{f}", [P, T], U32)
-            scales = fresh(f"scales{f}", [P, T], U8)
-            if f == 0:
-                weave(f, woven, 0, HALF, False)
-                weave(f, woven, HALF, HALF + 44, True)
-                weave(f, woven, HALF + 44, P, False)
-                multiply(f, 0, 1, woven, codes, scales, 4)
-                multiply(f, 1, PACK, woven, codes, scales, 0)
-            else:
-                weave(f, woven, 0, HALF, True)
-                weave(f, woven, HALF, P, True)
-                multiply(f, 0, PACK, woven, codes, scales, f)
-            for t in range(PACK if f < 2 else 2):
-                scatter_dc(t, f, 1)
+        def scatter_dc(t, f, values):
+            nc.scalar.activation(dc[t][:].indirect(entries(list2, f * C2, values.shape[-1])), values, COPY)
+
+        sums = [fresh(f"sums{f}", [P, PACK, C2], F32) for f in range(E2)]
+        pair = fresh("pair", [P, 2, 2, C2], F32)
+        low = fresh("woven0_0", [P, 2, P, PACK], BF16)
+        high = fresh("woven0_2", [P, 2, P, PACK], BF16)
+        weave(raw[0, 0], 0, low, 0, False)
+        weave(raw[0, 0], 0, high, 2, False)
+        weave(raw[0, 1], HALF, low, 0, True)
+        weave(raw[0, 1], HALF, high, 2, False)
+        operands = quantise(0, 0, low)
+        first_acc = bank("acc_first", [P, 1, C2], 7)
+        multiply(0, first_acc, operands[0:1])
+        operands = operands + quantise(0, 2, high)
+        acc = bank("acc0", [P, PACK - 1, C2], 0)
+        multiply(0, acc, operands[1:])
+        first_sums = fresh("first_sums", [P, 1, C2], F32)
+        gated(0, first_sums[:], first_acc[:])
+        gated(0, sums[0][:, 1:PACK, :], acc[:])
+        scatter_dc(0, 0, first_sums[:, 0, :])
+        for t in range(1, PACK):
+            scatter_dc(t, 0, sums[0][:, t, :])
+
+        tags = {(2, 0): "codes1_0", (2, 2): "codes1_2", (3, 0): "codes1_0", (3, 2): "codes2_0"}
+        for f in range(1, E2):
+            woven = {}
+            for t0 in (0, 2):
+                woven[t0] = fresh(f"woven{f}_{t0}", [P, 2, P, PACK], BF16, tags.get((f, t0)))
+                weave(raw[f, 0], 0, woven[t0], t0, True)
+            if f == 1:
+                for t0 in (0, 2):
+                    weave(raw[f, 1], HALF, woven[t0], t0, True)
+            for t0 in (0, 2):
+                acc = bank(f"acc{f}_{t0}", [P, 2, C2], (2 * f - 1 + t0 // 2) % 8)
+                multiply(f, acc, quantise(f, t0, woven[t0]))
+                paired = f > 1 and t0 == 2
+                place = pair[:, :, f - 2, :] if paired else sums[f][:, t0 : t0 + 2, :]
+                gated(f, place, acc[:])
+                if not paired:
+                    for u in range(2):
+                        scatter_dc(t0 + u, f, place[:, u, :])
         for t in (2, 3):
-            scatter_dc(t, 2, 2)
+            scatter_dc(t, 2, pair[:, t - 2].rearrange("p f s -> p (f s)"))
 
-        keep = fresh("keep", [P, PACK, T], F32)
-        for t in range(PACK):
-            nc.vector.scalar_tensor_tensor(keep[:, t, :], a_sb[:, t, :], 0.0, g[:], IS_GT, MULT)
-        picked = fresh("picked", [P, PACK, T], F32)
+        keep = {}
+
+        def make_keep(values, t0, tag):
+            planes = values.shape[1]
+            kept = fresh(f"keep{t0}", [P, planes, T], F32, tag)
+            nc.vector.scalar_tensor_tensor(
+                kept[:], values[:], 0.0, g[:].unsqueeze(1).to_broadcast([P, planes, T]), IS_GT, MULT
+            )
+            for u in range(planes):
+                keep[t0 + u] = kept[:, u, :]
+
+        make_keep(a_first, 0, "codes1_0")
+        make_keep(a_rest, 1, f"codes{E2 - 1}_2")
+        lead = fresh("lead", [P, PACK, P], F32)
+        rest = fresh("rest", [P, PACK, T - P], F32)
+
+        def picked(first, count):
+            return lead[:] if first == 0 else rest[:, :, first - P : first - P + count]
 
         def gather(t, first, count):
-            cols = slice(first, first + count)
             nc.vector.tensor_tensor(
-                picked[:, t, cols], dc[t][:].indirect(entries(list1, first, count)), keep[:, t, cols], MULT
+                picked(first, count)[:, t, :],
+                dc[t][:].indirect(entries(list1, first, count)),
+                keep[t][:, first : first + count],
+                MULT,
             )
 
         pieces = ((0, P), (P, P), (C1, C1))
         for t in range(PACK - 1):
-            for e in range(E1):
-                gather(t, e * C1, C1)
+            gather(t, 0, P)
+            gather(t, P, T - P)
         for first, count in pieces:
             gather(PACK - 1, first, count)
 
-        result = [fresh(f"result{k}", [P, T], F32) for k in range(T // P)]
+        lead_sums = [fresh(f"lead_sums{n}", [P, blocks, P], F32) for n, blocks in enumerate((1, 1, 2))]
+        lead_of = [lead_sums[0][:, 0, :], lead_sums[2][:, 0, :], lead_sums[1][:, 0, :], lead_sums[2][:, 1, :]]
+        rest_sums = [fresh(f"rest_sums{half}", [P, 2, T - P], F32) for half in range(2)]
         for n, (first, count) in enumerate(pieces):
             e = first // C1
-            da = fresh(f"da{n}", [P, count, PACK], BF16)
+            da = fresh(f"da{n}", [P, count, PACK], BF16, "lead" if n == 2 else None)
             copy(
                 n == 2,
                 da[:].rearrange("p (c i) t -> p c t i", i=4),
-                picked[:, :, first : first + count].rearrange("p t (c i) -> p c t i", i=4),
+                picked(first, count).rearrange("p t (c i) -> p c t i", i=4),
             )
             codes = fresh(f"da_codes{n}", [P, count], U32)
             scales = fresh(f"da_scales{n}", [P, count], U8)
             nc.vector.quantize_mx(
                 out=codes[:].bitcast(FP8X4), scales=scales[:], in_=da[:].rearrange("p s t -> p (s t)")
             )
-            for half in range(2):
-                acc = bank(f"out_acc{n}_{half}", [P, 2, count], (5 + 2 * n + half) % 8)
-                for u in range(2):
-                    column = e * T + (2 * half + u) * P
+            groups = ((0,), (2,), (1, 3)) if n == 0 else ((0, 1), (2, 3))
+            for half, blocks in enumerate(groups):
+                acc = bank(f"out_acc{n}_{half}", [P, len(blocks), count], (0, 3, 5)[n] + half)
+                for u, k in enumerate(blocks):
+                    column = e * T + k * P
                     nc.tensor.matmul_mx(
                         out=acc[:, u, :],
                         lhsT=w1_w[:, 2 * column : 2 * (column + P)].bitcast(FP4X4),
@@ -202,10 +247,14 @@ def tile_moe_seb_relu_kernel(
                         start=True,
                         stop=True,
                     )
-                values = fresh(f"out_sums{n}_{half}", [P, 2, count], F32)
-                copy(half == 1, values[:], acc[:])
-                for u in range(2):
-                    k = 2 * half + u
-                    copy(half == 1, result[k][:].indirect(entries(list1, first, count)), values[:, u, :])
-                    if n == len(pieces) - 1:
-                        nc.sync.dma_start(out[k * P : (k + 1) * P, :], result[k][:])
+                if n == 0:
+                    copy(False, lead_sums[half][:], acc[:])
+                else:
+                    copy(half == 1, rest_sums[half][:, :, first - P : first - P + count], acc[:])
+        tags = {1: "da_scales2", 3: "da_codes2"}
+        result = [fresh(f"result{k}", [P, T], F32, tags.get(k)) for k in range(T // P)]
+        for k in range(T // P):
+            copy(k >= 2, result[k][:].indirect(entries(list1, 0, P)), lead_of[k])
+        for k in range(T // P):
+            copy(k >= 2, result[k][:].indirect(entries(list1, P, T - P)), rest_sums[k // 2][:, k % 2, :])
+            nc.sync.dma_start(out[k * P : (k + 1) * P, :], result[k][:])

@@ -19,7 +19,6 @@ T = 512
 E1, C1 = 2, 256
 E2, C2 = 4, 128
 PACK = 4
-HALF = P // 2
 FLOPS = 2 * 2 * T * T * T
 
 
@@ -58,26 +57,27 @@ def tile_moe_seb_relu_kernel(
 
         raw = {}
 
-        def load_w2(f, h, width=T // 2):
-            raw[f, h] = fresh(f"raw{f}_{h}", [P, PACK, width], F32)
-            rows = w2t[f].rearrange("(p j) i -> p j i", j=PACK)
-            nc.sync.dma_start(raw[f, h][:], rows[:, :, h * width : (h + 1) * width])
+        def load_w2(f):
+            raw[f] = fresh(f"raw{f}", [P, PACK, T], F32)
+            nc.sync.dma_start(raw[f][:], w2t[f].rearrange("(p j) i -> p j i", j=PACK))
 
         nc.sync.dma_start(dy_w[:], dy_words[0].rearrange("p t d -> p (t d)").bitcast(I32))
         nc.sync.dma_start(list2[:], offs2)
-        load_w2(0, 0)
         for r in range(4):
             nc.sync.dma_start(dy_s[r:P:32, :].bitcast(I32), dy_scales[0, r:16:4, :].bitcast(I32))
-        load_w2(0, 1)
-        q_first = fresh("q_first", [P, C2], F32)
-        nc.sync.dma_start(q_first[:], gate2[:, 0:C2])
-        load_w2(1, 0)
-        load_w2(1, 1)
-        q_rest = fresh("q_rest", [P, T - C2], F32)
-        nc.sync.dma_start(q_rest[:], gate2[:, C2:T])
-        q = [q_first[:]] + [q_rest[:, n * C2 : (n + 1) * C2] for n in range(E2 - 1)]
-        for f in (2, 3):
-            load_w2(f, 0, T)
+        q = []
+
+        def load_gate2(first):
+            tile = fresh(f"q{first}", [P, 2 * C2], F32)
+            nc.sync.dma_start(tile[:], gate2[:, first * C2 : (first + 2) * C2])
+            q.extend([tile[:, 0:C2], tile[:, C2 : 2 * C2]])
+
+        load_w2(0)
+        load_gate2(0)
+        load_w2(1)
+        load_w2(2)
+        load_gate2(2)
+        load_w2(3)
         g = fresh("g", [P, T], F32)
         nc.sync.dma_start(g[:], gate1)
         a_rows = a.rearrange("(p t) s -> p t s", t=PACK)
@@ -105,19 +105,17 @@ def tile_moe_seb_relu_kernel(
             cols = slice(first, first + count)
             nc.vector.tensor_copy(gq_s[:, cols], dy_s[:].indirect(entries(list2, first, count)))
 
-        made = {}
         dc = [fresh(f"dc{t}", [P, T], F32) for t in range(PACK)]
 
-        def weave(source, m0, woven, t0, on_vector):
+        def weave(source, woven, t0, on_vector):
             planes = woven.shape[1]
             src = source[:].rearrange("p j (m t) -> p m j t", t=PACK)[:, :, :, t0 : t0 + planes]
-            copy(on_vector, woven[:].rearrange("p t m j -> p m j t")[:, m0 : m0 + src.shape[1]], src)
+            copy(on_vector, woven[:].rearrange("p t m j -> p m j t"), src)
 
         def quantise(f, t0, woven):
             width = woven.shape[1] * P
             codes = fresh(f"codes{f}_{t0}", [P, width], U32)
             scales = fresh(f"scales{f}_{t0}", [P, width], U8)
-            made[f, t0] = scales
             nc.vector.quantize_mx(
                 out=codes[:].bitcast(FP8X4), scales=scales[:], in_=woven[:].rearrange("p t m j -> p (t m j)")
             )
@@ -145,10 +143,8 @@ def tile_moe_seb_relu_kernel(
         pair = fresh("pair", [P, 2, 2, C2], F32)
         low = fresh("woven0_0", [P, 2, P, PACK], BF16)
         high = fresh("woven0_2", [P, 2, P, PACK], BF16)
-        weave(raw[0, 0], 0, low, 0, False)
-        weave(raw[0, 0], 0, high, 2, False)
-        weave(raw[0, 1], HALF, low, 0, True)
-        weave(raw[0, 1], HALF, high, 2, False)
+        weave(raw[0], low, 0, True)
+        weave(raw[0], high, 2, False)
         operands = quantise(0, 0, low)
         first_acc = bank("acc_first", [P, 1, C2], 7)
         multiply(0, first_acc, operands[0:1])
@@ -167,10 +163,7 @@ def tile_moe_seb_relu_kernel(
             woven = {}
             for t0 in (0, 2):
                 woven[t0] = fresh(f"woven{f}_{t0}", [P, 2, P, PACK], BF16, tags.get((f, t0)))
-                weave(raw[f, 0], 0, woven[t0], t0, True)
-            if f == 1:
-                for t0 in (0, 2):
-                    weave(raw[f, 1], HALF, woven[t0], t0, True)
+                weave(raw[f], woven[t0], t0, True)
             for t0 in (0, 2):
                 acc = bank(f"acc{f}_{t0}", [P, 2, C2], (2 * f - 1 + t0 // 2) % 8)
                 multiply(f, acc, quantise(f, t0, woven[t0]))
@@ -217,44 +210,64 @@ def tile_moe_seb_relu_kernel(
         for first, count in pieces:
             gather(PACK - 1, first, count)
 
-        lead_sums = [fresh(f"lead_sums{n}", [P, blocks, P], F32) for n, blocks in enumerate((1, 1, 2))]
-        lead_of = [lead_sums[0][:, 0, :], lead_sums[2][:, 0, :], lead_sums[1][:, 0, :], lead_sums[2][:, 1, :]]
-        rest_sums = [fresh(f"rest_sums{half}", [P, 2, T - P], F32) for half in range(2)]
-        for n, (first, count) in enumerate(pieces):
-            e = first // C1
+        codes = [fresh(f"da_codes{e}", [P, C1], U32) for e in range(E1)]
+        scales = [fresh(f"da_scales{e}", [P, C1], U8) for e in range(E1)]
+        result = {}
+
+        def quantise_da(n):
+            first, count = pieces[n]
             da = fresh(f"da{n}", [P, count, PACK], BF16, "lead" if n == 2 else None)
             copy(
                 n == 2,
                 da[:].rearrange("p (c i) t -> p c t i", i=4),
                 picked(first, count).rearrange("p t (c i) -> p c t i", i=4),
             )
-            codes = fresh(f"da_codes{n}", [P, count], U32)
-            scales = fresh(f"da_scales{n}", [P, count], U8)
+            cols = slice(first % C1, first % C1 + count)
             nc.vector.quantize_mx(
-                out=codes[:].bitcast(FP8X4), scales=scales[:], in_=da[:].rearrange("p s t -> p (s t)")
+                out=codes[first // C1][:, cols].bitcast(FP8X4),
+                scales=scales[first // C1][:, cols],
+                in_=da[:].rearrange("p s t -> p (s t)"),
             )
-            groups = ((0,), (2,), (1, 3)) if n == 0 else ((0, 1), (2, 3))
-            for half, blocks in enumerate(groups):
-                acc = bank(f"out_acc{n}_{half}", [P, len(blocks), count], (0, 3, 5)[n] + half)
-                for u, k in enumerate(blocks):
-                    column = e * T + k * P
-                    nc.tensor.matmul_mx(
-                        out=acc[:, u, :],
-                        lhsT=w1_w[:, 2 * column : 2 * (column + P)].bitcast(FP4X4),
-                        lhsT_scale=w1_s[:, column : column + P],
-                        rhs=codes[:].bitcast(FP8X4),
-                        rhs_scale=scales[:],
-                        start=True,
-                        stop=True,
-                    )
-                if n == 0:
-                    copy(False, lead_sums[half][:], acc[:])
-                else:
-                    copy(half == 1, rest_sums[half][:, :, first - P : first - P + count], acc[:])
-        tags = {1: "da_scales2", 3: "da_codes2"}
-        result = [fresh(f"result{k}", [P, T], F32, tags.get(k)) for k in range(T // P)]
+
+        def product(first, count, blocks, number, on_vector):
+            e, cols = first // C1, slice(first % C1, first % C1 + count)
+            acc = bank(f"out_acc{number}", [P, len(blocks), count], number)
+            for u, k in enumerate(blocks):
+                column = e * T + k * P
+                nc.tensor.matmul_mx(
+                    out=acc[:, u, :],
+                    lhsT=w1_w[:, 2 * column : 2 * (column + P)].bitcast(FP4X4),
+                    lhsT_scale=w1_s[:, column : column + P],
+                    rhs=codes[e][:, cols].bitcast(FP8X4),
+                    rhs_scale=scales[e][:, cols],
+                    start=True,
+                    stop=True,
+                )
+            values = fresh(f"out_sums{number}", [P, len(blocks), count], F32)
+            copy(on_vector, values[:], acc[:])
+            return {(k, first): values[:, u, :] for u, k in enumerate(blocks)}
+
+        def send(k, first, values, tag=None):
+            if first == 0:
+                result[k] = fresh(f"result{k}", [P, T], F32, tag)
+            copy(k >= 2, result[k][:].indirect(entries(list1, first, values.shape[1])), values)
+            if first == C1:
+                nc.sync.dma_start(out[k * P : (k + 1) * P, :], result[k][:])
+
+        quantise_da(0)
+        done = product(0, P, (0,), 0, False)
+        done.update(product(0, P, (2,), 1, False))
+        quantise_da(1)
+        quantise_da(2)
+        done.update(product(P, P, (0, 2), 2, False))
+        done.update(product(0, C1, (1,), 3, False))
+        done.update(product(0, C1, (3,), 4, True))
+        done.update(product(C1, C1, (2, 3), 5, True))
+        done.update(product(C1, C1, (0, 1), 6, False))
+        for k in (0, 2):
+            send(k, 0, done[k, 0])
+            send(k, P, done[k, P])
+        send(1, 0, done[1, 0], "da_scales1")
+        send(3, 0, done[3, 0], "da_codes1")
         for k in range(T // P):
-            copy(k >= 2, result[k][:].indirect(entries(list1, 0, P)), lead_of[k])
-        for k in range(T // P):
-            copy(k >= 2, result[k][:].indirect(entries(list1, P, T - P)), rest_sums[k // 2][:, k % 2, :])
-            nc.sync.dma_start(out[k * P : (k + 1) * P, :], result[k][:])
+            send(k, C1, done[k, C1])

@@ -63,16 +63,19 @@ def tile_moe_seb_relu_kernel(
 
         nc.sync.dma_start(dy_w[:], dy_words[0].rearrange("p t d -> p (t d)").bitcast(I32))
         nc.sync.dma_start(list2[:], offs2)
+        q = []
+        halves = [fresh(f"raw0_{h}", [P, PACK, T // 2], F32) for h in range(2)]
+        rows0 = w2t[0].rearrange("(p j) i -> p j i", j=PACK)
+        nc.sync.dma_start(halves[0][:], rows0[:, :, 0 : T // 2])
         for r in range(4):
             nc.sync.dma_start(dy_s[r:P:32, :].bitcast(I32), dy_scales[0, r:16:4, :].bitcast(I32))
-        q = []
+        nc.sync.dma_start(halves[1][:], rows0[:, :, T // 2 : T])
 
         def load_gate2(first):
             tile = fresh(f"q{first}", [P, 2 * C2], F32)
             nc.sync.dma_start(tile[:], gate2[:, first * C2 : (first + 2) * C2])
             q.extend([tile[:, 0:C2], tile[:, C2 : 2 * C2]])
 
-        load_w2(0)
         load_gate2(0)
         load_w2(1)
         load_w2(2)
@@ -107,10 +110,10 @@ def tile_moe_seb_relu_kernel(
 
         dc = [fresh(f"dc{t}", [P, T], F32) for t in range(PACK)]
 
-        def weave(source, woven, t0, on_vector):
+        def weave(source, woven, t0, on_vector, m0=0):
             planes = woven.shape[1]
             src = source[:].rearrange("p j (m t) -> p m j t", t=PACK)[:, :, :, t0 : t0 + planes]
-            copy(on_vector, woven[:].rearrange("p t m j -> p m j t"), src)
+            copy(on_vector, woven[:].rearrange("p t m j -> p m j t")[:, m0 : m0 + src.shape[1]], src)
 
         def quantise(f, t0, woven):
             width = woven.shape[1] * P
@@ -143,8 +146,10 @@ def tile_moe_seb_relu_kernel(
         pair = fresh("pair", [P, 2, 2, C2], F32)
         low = fresh("woven0_0", [P, 2, P, PACK], BF16)
         high = fresh("woven0_2", [P, 2, P, PACK], BF16)
-        weave(raw[0], low, 0, True)
-        weave(raw[0], high, 2, False)
+        weave(halves[0], low, 0, False)
+        weave(halves[0], high, 2, False)
+        weave(halves[1], low, 0, True, P // 2)
+        weave(halves[1], high, 2, False, P // 2)
         operands = quantise(0, 0, low)
         first_acc = bank("acc_first", [P, 1, C2], 7)
         multiply(0, first_acc, operands[0:1])

@@ -64,23 +64,30 @@ def tile_moe_seb_relu_kernel(
         nc.sync.dma_start(dy_w[:], dy_words[0].rearrange("p t d -> p (t d)").bitcast(I32))
         nc.sync.dma_start(list2[:], offs2)
         q = []
-        halves = [fresh(f"raw0_{h}", [P, PACK, T // 2], F32) for h in range(2)]
-        rows0 = w2t[0].rearrange("(p j) i -> p j i", j=PACK)
-        nc.sync.dma_start(halves[0][:], rows0[:, :, 0 : T // 2])
+        halves = {}
+
+        def load_half(f, h):
+            halves[f, h] = fresh(f"raw{f}_{h}", [P, PACK, T // 2], F32)
+            rows = w2t[f].rearrange("(p j) i -> p j i", j=PACK)
+            nc.sync.dma_start(halves[f, h][:], rows[:, :, h * (T // 2) : (h + 1) * (T // 2)])
+
+        load_half(0, 0)
         for r in range(4):
             nc.sync.dma_start(dy_s[r:P:32, :].bitcast(I32), dy_scales[0, r:16:4, :].bitcast(I32))
-        nc.sync.dma_start(halves[1][:], rows0[:, :, T // 2 : T])
+        load_half(0, 1)
 
-        def load_gate2(first):
-            tile = fresh(f"q{first}", [P, 2 * C2], F32)
-            nc.sync.dma_start(tile[:], gate2[:, first * C2 : (first + 2) * C2])
-            q.extend([tile[:, 0:C2], tile[:, C2 : 2 * C2]])
+        def load_gate2(first, experts):
+            tile = fresh(f"q{first}", [P, experts * C2], F32)
+            nc.sync.dma_start(tile[:], gate2[:, first * C2 : (first + experts) * C2])
+            q.extend([tile[:, n * C2 : (n + 1) * C2] for n in range(experts)])
 
-        load_gate2(0)
-        load_w2(1)
+        load_gate2(0, 1)
+        load_half(1, 0)
+        load_half(1, 1)
         load_w2(2)
-        load_gate2(2)
+        load_gate2(1, 1)
         load_w2(3)
+        load_gate2(2, 2)
         g = fresh("g", [P, T], F32)
         nc.sync.dma_start(g[:], gate1)
         a_rows = a.rearrange("(p t) s -> p t s", t=PACK)
@@ -146,10 +153,10 @@ def tile_moe_seb_relu_kernel(
         pair = fresh("pair", [P, 2, 2, C2], F32)
         low = fresh("woven0_0", [P, 2, P, PACK], BF16)
         high = fresh("woven0_2", [P, 2, P, PACK], BF16)
-        weave(halves[0], low, 0, False)
-        weave(halves[0], high, 2, False)
-        weave(halves[1], low, 0, True, P // 2)
-        weave(halves[1], high, 2, False, P // 2)
+        weave(halves[0, 0], low, 0, False)
+        weave(halves[0, 0], high, 2, False)
+        weave(halves[0, 1], low, 0, True, P // 2)
+        weave(halves[0, 1], high, 2, False, P // 2)
         operands = quantise(0, 0, low)
         first_acc = bank("acc_first", [P, 1, C2], 7)
         multiply(0, first_acc, operands[0:1])
@@ -163,12 +170,15 @@ def tile_moe_seb_relu_kernel(
         for t in range(1, PACK):
             scatter_dc(t, 0, sums[0][:, t, :])
 
-        tags = {(2, 0): "codes1_0", (2, 2): "codes1_2", (3, 0): "codes1_0", (3, 2): "codes2_0"}
+        tags = {(2, 0): "woven1_0", (2, 2): "codes1_2", (3, 0): "woven1_0", (3, 2): "codes2_0"}
         for f in range(1, E2):
             woven = {}
             for t0 in (0, 2):
                 woven[t0] = fresh(f"woven{f}_{t0}", [P, 2, P, PACK], BF16, tags.get((f, t0)))
-                weave(raw[f], woven[t0], t0, True)
+                weave(halves[f, 0] if f == 1 else raw[f], woven[t0], t0, True)
+            if f == 1:
+                for t0 in (0, 2):
+                    weave(halves[f, 1], woven[t0], t0, True, P // 2)
             for t0 in (0, 2):
                 acc = bank(f"acc{f}_{t0}", [P, 2, C2], (2 * f - 1 + t0 // 2) % 8)
                 multiply(f, acc, quantise(f, t0, woven[t0]))
@@ -192,7 +202,7 @@ def tile_moe_seb_relu_kernel(
             for u in range(planes):
                 keep[t0 + u] = kept[:, u, :]
 
-        make_keep(a_first, 0, "codes1_0")
+        make_keep(a_first, 0, "woven1_0")
         make_keep(a_rest, 1, f"codes{E2 - 1}_2")
         lead = fresh("lead", [P, PACK, P], F32)
         rest = fresh("rest", [P, PACK, T - P], F32)

@@ -55,12 +55,6 @@ def tile_moe_seb_relu_kernel(
         nc.gpsimd.memset(dy_s[:].bitcast(I32), 0)
         nc.vector.memset(w1_s[:].bitcast(I32), 0)
 
-        raw = {}
-
-        def load_w2(f):
-            raw[f] = fresh(f"raw{f}", [P, PACK, T], F32)
-            nc.sync.dma_start(raw[f][:], w2t[f].rearrange("(p j) i -> p j i", j=PACK))
-
         nc.sync.dma_start(dy_w[:], dy_words[0].rearrange("p t d -> p (t d)").bitcast(I32))
         nc.sync.dma_start(list2[:], offs2)
         q = []
@@ -84,17 +78,18 @@ def tile_moe_seb_relu_kernel(
         load_gate2(0, 1)
         load_half(1, 0)
         load_half(1, 1)
-        load_w2(2)
+        load_half(2, 0)
+        load_half(2, 1)
         load_gate2(1, 1)
-        load_w2(3)
+        load_half(3, 0)
+        load_half(3, 1)
         load_gate2(2, 2)
         g = fresh("g", [P, T], F32)
         nc.sync.dma_start(g[:], gate1)
         a_rows = a.rearrange("(p t) s -> p t s", t=PACK)
-        a_first = fresh("a_first", [P, 1, T], F32)
-        a_rest = fresh("a_rest", [P, PACK - 1, T], F32)
-        nc.sync.dma_start(a_first[:], a_rows[:, 0:1, :])
-        nc.sync.dma_start(a_rest[:], a_rows[:, 1:PACK, :])
+        a_of = [fresh(f"a{e}", [P, PACK, C1], F32) for e in range(E1)]
+        for e in (1, 0):
+            nc.sync.dma_start(a_of[e][:], a_rows[:, :, e * C1 : (e + 1) * C1])
         nc.sync.dma_start(list1[:], offs)
         nc.sync.dma_start(
             w1_w[:].bitcast(I32).rearrange("p (e c) -> p e c", e=E1),
@@ -146,11 +141,10 @@ def tile_moe_seb_relu_kernel(
         def gated(f, place, acc):
             nc.vector.tensor_tensor(place, acc, q[f].unsqueeze(1).to_broadcast(list(place.shape)), MULT)
 
-        def scatter_dc(t, f, values):
-            nc.scalar.activation(dc[t][:].indirect(entries(list2, f * C2, values.shape[-1])), values, COPY)
+        def scatter_dc(t, f, values, on_vector=False):
+            copy(on_vector, dc[t][:].indirect(entries(list2, f * C2, values.shape[-1])), values)
 
         sums = [fresh(f"sums{f}", [P, PACK, C2], F32) for f in range(E2)]
-        pair = fresh("pair", [P, 2, 2, C2], F32)
         low = fresh("woven0_0", [P, 2, P, PACK], BF16)
         high = fresh("woven0_2", [P, 2, P, PACK], BF16)
         weave(halves[0, 0], low, 0, False)
@@ -170,81 +164,68 @@ def tile_moe_seb_relu_kernel(
         for t in range(1, PACK):
             scatter_dc(t, 0, sums[0][:, t, :])
 
-        tags = {(2, 0): "woven1_0", (2, 2): "codes1_2", (3, 0): "woven1_0", (3, 2): "codes2_0"}
+        acc2 = None
+        tags = {(2, 0): "woven1_0", (2, 2): "woven1_2", (3, 0): "woven1_0", (3, 2): "woven1_2"}
         for f in range(1, E2):
             woven = {}
             for t0 in (0, 2):
                 woven[t0] = fresh(f"woven{f}_{t0}", [P, 2, P, PACK], BF16, tags.get((f, t0)))
-                weave(halves[f, 0] if f == 1 else raw[f], woven[t0], t0, True)
-            if f == 1:
-                for t0 in (0, 2):
-                    weave(halves[f, 1], woven[t0], t0, True, P // 2)
+                weave(halves[f, 0], woven[t0], t0, True)
             for t0 in (0, 2):
+                weave(halves[f, 1], woven[t0], t0, True, P // 2)
+            for t0 in (0, 2):
+                if (f, t0) == (3, 2):
+                    kept_back = fresh("kept_back", [P, 1, C2], F32, "raw3_1")
+                    gated(2, kept_back[:], acc2[:, 0:1, :])
                 acc = bank(f"acc{f}_{t0}", [P, 2, C2], (2 * f - 1 + t0 // 2) % 8)
                 multiply(f, acc, quantise(f, t0, woven[t0]))
-                paired = f > 1 and t0 == 2
-                place = pair[:, :, f - 2, :] if paired else sums[f][:, t0 : t0 + 2, :]
-                gated(f, place, acc[:])
-                if not paired:
-                    for u in range(2):
-                        scatter_dc(t0 + u, f, place[:, u, :])
-        for t in (2, 3):
-            scatter_dc(t, 2, pair[:, t - 2].rearrange("p f s -> p (f s)"))
+                if (f, t0) == (3, 2):
+                    scatter_dc(2, 2, kept_back[:, 0, :], True)
+                skip = 1 if (f, t0) == (2, 2) else 0
+                acc2 = acc if skip else acc2
+                gated(f, sums[f][:, t0 + skip : t0 + 2, :], acc[:, skip:2, :])
+                for t in range(t0 + skip, t0 + 2):
+                    scatter_dc(t, f, sums[f][:, t, :])
 
-        keep = {}
+        def make_keep(e, t0, planes, tag):
+            kept = fresh(f"keep{e}_{t0}", [P, planes, C1], F32, tag)
+            gate = g[:, e * C1 : (e + 1) * C1].unsqueeze(1).to_broadcast([P, planes, C1])
+            nc.vector.scalar_tensor_tensor(kept[:], a_of[e][:, t0 : t0 + planes, :], 0.0, gate, IS_GT, MULT)
+            return kept
 
-        def make_keep(values, t0, tag):
-            planes = values.shape[1]
-            kept = fresh(f"keep{t0}", [P, planes, T], F32, tag)
-            nc.vector.scalar_tensor_tensor(
-                kept[:], values[:], 0.0, g[:].unsqueeze(1).to_broadcast([P, planes, T]), IS_GT, MULT
-            )
-            for u in range(planes):
-                keep[t0 + u] = kept[:, u, :]
+        keep1 = make_keep(1, 0, PACK, f"codes{E2 - 1}_2")
+        keep0 = make_keep(0, 0, PACK, f"scales{E2 - 1}_2")
+        picked = [fresh(f"picked{e}", [P, PACK, C1], F32, f"a{e}") for e in range(E1)]
 
-        make_keep(a_first, 0, "woven1_0")
-        make_keep(a_rest, 1, f"codes{E2 - 1}_2")
-        lead = fresh("lead", [P, PACK, P], F32)
-        rest = fresh("rest", [P, PACK, T - P], F32)
+        def window(t, first, count):
+            return dc[t][:].indirect(entries(list1, first, count))
 
-        def picked(first, count):
-            return lead[:] if first == 0 else rest[:, :, first - P : first - P + count]
-
-        def gather(t, first, count):
-            nc.vector.tensor_tensor(
-                picked(first, count)[:, t, :],
-                dc[t][:].indirect(entries(list1, first, count)),
-                keep[t][:, first : first + count],
-                MULT,
-            )
-
-        pieces = ((0, P), (P, P), (C1, C1))
-        for t in range(PACK - 1):
-            gather(t, 0, P)
-            gather(t, P, T - P)
-        for first, count in pieces:
-            gather(PACK - 1, first, count)
+        for t in range(PACK):
+            copy(t < 1, picked[1][:, t, :], window(t, C1, C1))
+        for t, first, count in ((0, 0, C1), (1, 0, C1), (2, 0, C1), (3, 0, P), (3, P, P)):
+            cols = slice(first, first + count)
+            nc.vector.tensor_tensor(picked[0][:, t, cols], window(t, first, count), keep0[:, t, cols], MULT)
 
         codes = [fresh(f"da_codes{e}", [P, C1], U32) for e in range(E1)]
         scales = [fresh(f"da_scales{e}", [P, C1], U8) for e in range(E1)]
         result = {}
 
-        def quantise_da(n):
-            first, count = pieces[n]
-            da = fresh(f"da{n}", [P, count, PACK], BF16, "lead" if n == 2 else None)
-            copy(
-                n == 2,
-                da[:].rearrange("p (c i) t -> p c t i", i=4),
-                picked(first, count).rearrange("p t (c i) -> p c t i", i=4),
-            )
-            cols = slice(first % C1, first % C1 + count)
+        def by_line(planes):
+            return planes.rearrange("p t (c i) -> p c t i", i=4)
+
+        def woven_da(name, count, tag=None):
+            da = fresh(name, [P, count, PACK], BF16, tag)
+            return da, da[:].rearrange("p (c i) t -> p c t i", i=4)
+
+        def quantise_da(da, first):
+            cols = slice(first % C1, first % C1 + da.shape[1])
             nc.vector.quantize_mx(
                 out=codes[first // C1][:, cols].bitcast(FP8X4),
                 scales=scales[first // C1][:, cols],
                 in_=da[:].rearrange("p s t -> p (s t)"),
             )
 
-        def product(first, count, blocks, number, on_vector):
+        def product(first, count, blocks, number):
             e, cols = first // C1, slice(first % C1, first % C1 + count)
             acc = bank(f"out_acc{number}", [P, len(blocks), count], number)
             for u, k in enumerate(blocks):
@@ -258,7 +239,11 @@ def tile_moe_seb_relu_kernel(
                     start=True,
                     stop=True,
                 )
-            values = fresh(f"out_sums{number}", [P, len(blocks), count], F32)
+            return acc, first, blocks, number
+
+        def empty(made, on_vector):
+            acc, first, blocks, number = made
+            values = fresh(f"out_sums{number}", list(acc.shape), F32)
             copy(on_vector, values[:], acc[:])
             return {(k, first): values[:, u, :] for u, k in enumerate(blocks)}
 
@@ -269,20 +254,29 @@ def tile_moe_seb_relu_kernel(
             if first == C1:
                 nc.sync.dma_start(out[k * P : (k + 1) * P, :], result[k][:])
 
-        quantise_da(0)
-        done = product(0, P, (0,), 0, False)
-        done.update(product(0, P, (2,), 1, False))
-        quantise_da(1)
-        quantise_da(2)
-        done.update(product(P, P, (0, 2), 2, False))
-        done.update(product(0, C1, (1,), 3, False))
-        done.update(product(0, C1, (3,), 4, True))
-        done.update(product(C1, C1, (2, 3), 5, True))
-        done.update(product(C1, C1, (0, 1), 6, False))
+        lead = []
+        for n in range(2):
+            da, view = woven_da(f"da{n}", P)
+            nc.vector.tensor_copy(view, by_line(picked[0][:, :, n * P : (n + 1) * P]))
+            lead.append(da)
+        for n in range(2):
+            quantise_da(lead[n], n * P)
+        done = empty(product(0, P, (0,), 0), False)
+        done.update(empty(product(0, P, (2,), 1), False))
+        third = product(0, C1, (3,), 2)
+        done.update(empty(product(P, P, (0, 2), 3), False))
+        done.update(empty(product(0, C1, (1,), 4), False))
+        da, view = woven_da("da2", C1, "da0")
+        nc.vector.tensor_tensor(view, by_line(picked[1][:]), by_line(keep1[:]), MULT)
+        done.update(empty(third, True))
+        quantise_da(da, C1)
+        done.update(empty(product(C1, C1, (0, 1), 5), False))
+        done.update(empty(product(C1, C1, (2, 3), 6), False))
+        send(0, 0, done[0, 0])
+        send(2, 0, done[2, 0], "a1")
         for k in (0, 2):
-            send(k, 0, done[k, 0])
             send(k, P, done[k, P])
         send(1, 0, done[1, 0], "da_scales1")
-        send(3, 0, done[3, 0], "da_codes1")
+        send(3, 0, done[3, 0])
         for k in range(T // P):
             send(k, C1, done[k, C1])

@@ -1,6 +1,7 @@
 from contextlib import ExitStack
 
 import concourse.mybir as mybir
+from concourse.masks import make_identity
 
 F32 = mybir.dt.float32
 BF16 = mybir.dt.bfloat16
@@ -54,6 +55,10 @@ def tile_moe_seb_relu_kernel(
         w1_s = fresh("w1_s", [P, E1 * T], U8)
         nc.gpsimd.memset(dy_s[:].bitcast(I32), 0)
         nc.vector.memset(w1_s[:].bitcast(I32), 0)
+        g_rows = fresh("g_rows", [P, P], F32)
+        identity = fresh("identity", [P, P], F32)
+        nc.vector.memset(g_rows[:], 0.0)
+        make_identity(nc, identity[:])
 
         nc.sync.dma_start(dy_w[:], dy_words[0].rearrange("p t d -> p (t d)").bitcast(I32))
         nc.sync.dma_start(list2[:], offs2)
@@ -78,19 +83,18 @@ def tile_moe_seb_relu_kernel(
         load_gate2(0, 1)
         load_half(1, 0)
         load_half(1, 1)
+        nc.sync.dma_start(g_rows[0:PACK, :], gate1[0].rearrange("(c p) -> c p", p=P))
         load_half(2, 0)
         load_half(2, 1)
         load_gate2(1, 1)
         load_half(3, 0)
         load_half(3, 1)
         load_gate2(2, 2)
-        g = fresh("g", [P, T], F32)
-        nc.sync.dma_start(g[:], gate1)
-        a_rows = a.rearrange("(p t) s -> p t s", t=PACK)
-        a_of = [fresh(f"a{e}", [P, PACK, C1], F32) for e in range(E1)]
-        for e in (1, 0):
-            nc.sync.dma_start(a_of[e][:], a_rows[:, :, e * C1 : (e + 1) * C1])
         nc.sync.dma_start(list1[:], offs)
+        a_rows = a.rearrange("(p t) s -> p t s", t=PACK)
+        a_of = [fresh(f"a{n}", [P, 2, T], F32) for n in range(2)]
+        for n in range(2):
+            nc.sync.dma_start(a_of[n][:], a_rows[:, 2 * n : 2 * n + 2, :])
         nc.sync.dma_start(
             w1_w[:].bitcast(I32).rearrange("p (e c) -> p e c", e=E1),
             w1t_words[:, 0].bitcast(I32).rearrange("e p c -> p e c"),
@@ -122,7 +126,7 @@ def tile_moe_seb_relu_kernel(
             codes = fresh(f"codes{f}_{t0}", [P, width], U32)
             scales = fresh(f"scales{f}_{t0}", [P, width], U8)
             nc.vector.quantize_mx(
-                out=codes[:].bitcast(FP8X4), scales=scales[:], in_=woven[:].rearrange("p t m j -> p (t m j)")
+                out=codes[:].bitcast(FP8X4), scales=scales[:], in_=woven.rearrange("p t m j -> p (t m j)")
             )
             return [(codes[:, c : c + P], scales[:, c : c + P]) for c in range(0, width, P)]
 
@@ -145,63 +149,75 @@ def tile_moe_seb_relu_kernel(
             copy(on_vector, dc[t][:].indirect(entries(list2, f * C2, values.shape[-1])), values)
 
         sums = [fresh(f"sums{f}", [P, PACK, C2], F32) for f in range(E2)]
-        low = fresh("woven0_0", [P, 2, P, PACK], BF16)
+        low = fresh("woven0_low", [P, 2, P, PACK], BF16)
         high = fresh("woven0_2", [P, 2, P, PACK], BF16)
         weave(halves[0, 0], low, 0, False)
         weave(halves[0, 0], high, 2, False)
         weave(halves[0, 1], low, 0, True, P // 2)
-        weave(halves[0, 1], high, 2, False, P // 2)
-        operands = quantise(0, 0, low)
+        weave(halves[0, 1], high, 2, True, P // 2)
+        operands = quantise(0, 0, low[:, 0:1])
         first_acc = bank("acc_first", [P, 1, C2], 7)
         multiply(0, first_acc, operands[0:1])
-        operands = operands + quantise(0, 2, high)
+        operands = operands + quantise(0, 1, low[:, 1:2]) + quantise(0, 2, high[:])
         acc = bank("acc0", [P, PACK - 1, C2], 0)
         multiply(0, acc, operands[1:])
         first_sums = fresh("first_sums", [P, 1, C2], F32)
         gated(0, first_sums[:], first_acc[:])
         gated(0, sums[0][:, 1:PACK, :], acc[:])
+        turned = bank("g_turned", [P, P], 5)
+        nc.tensor.transpose(turned[:], g_rows[:], identity[:])
+        g_cols = fresh("g_cols", [P, PACK], F32)
+        copy(False, g_cols[:], turned[:, 0:PACK])
         scatter_dc(0, 0, first_sums[:, 0, :])
         for t in range(1, PACK):
             scatter_dc(t, 0, sums[0][:, t, :])
 
-        acc2 = None
-        tags = {(2, 0): "woven1_0", (2, 2): "woven1_2", (3, 0): "woven1_0", (3, 2): "woven1_2"}
+        waiting = None
         for f in range(1, E2):
-            woven = {}
-            for t0 in (0, 2):
-                woven[t0] = fresh(f"woven{f}_{t0}", [P, 2, P, PACK], BF16, tags.get((f, t0)))
-                weave(halves[f, 0], woven[t0], t0, True)
-            for t0 in (0, 2):
-                weave(halves[f, 1], woven[t0], t0, True, P // 2)
-            for t0 in (0, 2):
-                if (f, t0) == (3, 2):
-                    kept_back = fresh("kept_back", [P, 1, C2], F32, "raw3_1")
-                    gated(2, kept_back[:], acc2[:, 0:1, :])
-                acc = bank(f"acc{f}_{t0}", [P, 2, C2], (2 * f - 1 + t0 // 2) % 8)
-                multiply(f, acc, quantise(f, t0, woven[t0]))
-                if (f, t0) == (3, 2):
-                    scatter_dc(2, 2, kept_back[:, 0, :], True)
-                skip = 1 if (f, t0) == (2, 2) else 0
-                acc2 = acc if skip else acc2
-                gated(f, sums[f][:, t0 + skip : t0 + 2, :], acc[:, skip:2, :])
-                for t in range(t0 + skip, t0 + 2):
-                    scatter_dc(t, f, sums[f][:, t, :])
+            woven = fresh(f"woven{f}", [P, PACK, P, PACK], BF16)
+            for h in range(2):
+                weave(halves[f, h], woven, 0, True, h * (P // 2))
+            if waiting is not None:
+                late = fresh(f"late{f}", [P, 2, C2], F32, f"raw{f}_1")
+                gated(f - 1, late[:], waiting[:])
+                for u in range(2):
+                    if (f, u) != (3, 0):
+                        scatter_dc(2 + u, f - 1, late[:, u, :])
+            operands = [quantise(f, t0, woven[:, t0 : t0 + 2]) for t0 in (0, 2)]
+            if f == 3:
+                scatter_dc(2, 2, late[:, 0, :], True)
+            acc = bank(f"acc{f}_0", [P, 2, C2], 2 * f - 1)
+            waiting = bank(f"acc{f}_2", [P, 2, C2], 2 * f)
+            multiply(f, acc, operands[0])
+            multiply(f, waiting, operands[1])
+            gated(f, sums[f][:, 0:2, :], acc[:])
+            for t in range(2):
+                scatter_dc(t, f, sums[f][:, t, :])
+            if f == 1:
+                g = bank("g", [P, T], 1)
+                for c in range(T // P):
+                    column = g_cols[:, c : c + 1].to_broadcast([P, P])
+                    nc.tensor.transpose(g[:, c * P : (c + 1) * P], column, identity[:])
+        gated(E2 - 1, sums[E2 - 1][:, 2:PACK, :], waiting[:])
+        for t in (2, 3):
+            scatter_dc(t, E2 - 1, sums[E2 - 1][:, t, :])
 
-        def make_keep(e, t0, planes, tag):
-            kept = fresh(f"keep{e}_{t0}", [P, planes, C1], F32, tag)
-            gate = g[:, e * C1 : (e + 1) * C1].unsqueeze(1).to_broadcast([P, planes, C1])
-            nc.vector.scalar_tensor_tensor(kept[:], a_of[e][:, t0 : t0 + planes, :], 0.0, gate, IS_GT, MULT)
+        def make_keep(first, count, tag):
+            kept = fresh(f"keep{first}", [P, PACK, count], F32, tag)
+            gate = g[:, first : first + count].unsqueeze(1).to_broadcast([P, 2, count])
+            for n in range(2):
+                values = a_of[n][:, :, first : first + count]
+                nc.vector.scalar_tensor_tensor(kept[:, 2 * n : 2 * n + 2, :], values, 0.0, gate, IS_GT, MULT)
             return kept
 
-        keep1 = make_keep(1, 0, PACK, f"codes{E2 - 1}_2")
-        keep0 = make_keep(0, 0, PACK, f"scales{E2 - 1}_2")
-        picked = [fresh(f"picked{e}", [P, PACK, C1], F32, f"a{e}") for e in range(E1)]
+        keep0 = make_keep(0, T, f"codes{E2 - 1}_2")
+        picked = [fresh(f"picked{e}", [P, PACK, C1], F32, "a0" if e else None) for e in range(E1)]
 
         def window(t, first, count):
             return dc[t][:].indirect(entries(list1, first, count))
 
         for t in range(PACK):
-            copy(t < 1, picked[1][:, t, :], window(t, C1, C1))
+            copy(t == 0, picked[1][:, t, :], window(t, C1, C1))
         for t, first, count in ((0, 0, C1), (1, 0, C1), (2, 0, C1), (3, 0, P), (3, P, P)):
             cols = slice(first, first + count)
             nc.vector.tensor_tensor(picked[0][:, t, cols], window(t, first, count), keep0[:, t, cols], MULT)
@@ -261,22 +277,23 @@ def tile_moe_seb_relu_kernel(
             lead.append(da)
         for n in range(2):
             quantise_da(lead[n], n * P)
-        done = empty(product(0, P, (0,), 0), False)
-        done.update(empty(product(0, P, (2,), 1), False))
+        done = empty(product(0, P, (0,), 7), False)
+        done.update(empty(product(0, P, (2,), 0), False))
         third = product(0, C1, (3,), 2)
         done.update(empty(product(P, P, (0, 2), 3), False))
         done.update(empty(product(0, C1, (1,), 4), False))
         da, view = woven_da("da2", C1, "da0")
-        nc.vector.tensor_tensor(view, by_line(picked[1][:]), by_line(keep1[:]), MULT)
+        nc.vector.tensor_tensor(view, by_line(picked[1][:]), by_line(keep0[:, :, C1:T]), MULT)
         done.update(empty(third, True))
         quantise_da(da, C1)
-        done.update(empty(product(C1, C1, (0, 1), 5), False))
-        done.update(empty(product(C1, C1, (2, 3), 6), False))
+        done.update(empty(product(C1, C1, (2, 3), 5), False))
+        done.update(empty(product(C1, C1, (0,), 6), False))
+        done.update(empty(product(C1, C1, (1,), 1), False))
         send(0, 0, done[0, 0])
-        send(2, 0, done[2, 0], "a1")
+        send(2, 0, done[2, 0], "a0")
         for k in (0, 2):
             send(k, P, done[k, P])
-        send(1, 0, done[1, 0], "da_scales1")
+        send(1, 0, done[1, 0])
         send(3, 0, done[3, 0])
         for k in range(T // P):
             send(k, C1, done[k, C1])

@@ -20,6 +20,8 @@ T = 512
 E1, C1 = 2, 256
 E2, C2 = 4, 128
 PACK = 4
+LINE = 4
+SHARE = 40
 FLOPS = 2 * 2 * T * T * T
 
 
@@ -80,10 +82,10 @@ def tile_moe_seb_relu_kernel(
             nc.sync.dma_start(tile[:], gate2[:, first * C2 : (first + experts) * C2])
             q.extend([tile[:, n * C2 : (n + 1) * C2] for n in range(experts)])
 
-        load_gate2(0, 1)
         load_half(1, 0)
+        load_gate2(0, 1)
         load_half(1, 1)
-        nc.sync.dma_start(g_rows[0:PACK, :], gate1[0].rearrange("(c p) -> c p", p=P))
+        nc.sync.dma_start(g_rows[0 : T // P, :], gate1[0].rearrange("(c p) -> c p", p=P))
         load_half(2, 0)
         load_half(2, 1)
         load_gate2(1, 1)
@@ -116,10 +118,10 @@ def tile_moe_seb_relu_kernel(
 
         dc = [fresh(f"dc{t}", [P, T], F32) for t in range(PACK)]
 
-        def weave(source, woven, t0, on_vector, m0=0):
-            planes = woven.shape[1]
-            src = source[:].rearrange("p j (m t) -> p m j t", t=PACK)[:, :, :, t0 : t0 + planes]
-            copy(on_vector, woven[:].rearrange("p t m j -> p m j t")[:, m0 : m0 + src.shape[1]], src)
+        def weave(f, h, woven, on_vector, t0=0, t1=PACK, m0=0, m1=P // 2):
+            src = halves[f, h][:].rearrange("p j (m t) -> p m j t", t=PACK)
+            dst = woven[:].rearrange("p t m j -> p m j t")[:, h * (P // 2) : (h + 1) * (P // 2)]
+            copy(on_vector, dst[:, m0:m1, :, t0:t1], src[:, m0:m1, :, t0:t1])
 
         def quantise(f, t0, woven):
             width = woven.shape[1] * P
@@ -149,43 +151,41 @@ def tile_moe_seb_relu_kernel(
             copy(on_vector, dc[t][:].indirect(entries(list2, f * C2, values.shape[-1])), values)
 
         sums = [fresh(f"sums{f}", [P, PACK, C2], F32) for f in range(E2)]
-        low = fresh("woven0_low", [P, 2, P, PACK], BF16)
-        high = fresh("woven0_2", [P, 2, P, PACK], BF16)
-        weave(halves[0, 0], low, 0, False)
-        weave(halves[0, 0], high, 2, False)
-        weave(halves[0, 1], low, 0, True, P // 2)
-        weave(halves[0, 1], high, 2, True, P // 2)
-        operands = quantise(0, 0, low[:, 0:1])
+        woven = fresh("woven0", [P, PACK, P, PACK], BF16)
+        weave(0, 0, woven, False)
+        weave(0, 1, woven, True, 0, 2)
+        weave(0, 1, woven, True, 2, PACK)
+        operands = quantise(0, 0, woven[:, 0:1])
         first_acc = bank("acc_first", [P, 1, C2], 7)
-        multiply(0, first_acc, operands[0:1])
-        operands = operands + quantise(0, 1, low[:, 1:2]) + quantise(0, 2, high[:])
-        acc = bank("acc0", [P, PACK - 1, C2], 0)
-        multiply(0, acc, operands[1:])
-        first_sums = fresh("first_sums", [P, 1, C2], F32)
-        gated(0, first_sums[:], first_acc[:])
-        gated(0, sums[0][:, 1:PACK, :], acc[:])
+        multiply(0, first_acc, operands)
+        operands = quantise(0, 1, woven[:, 1:PACK])
+        acc = bank("acc0", [P, 1, C2], 6)
+        waiting = bank("acc0_2", [P, 2, C2], 0)
+        multiply(0, acc, operands[0:1])
+        multiply(0, waiting, operands[1:])
+        gated(0, sums[0][:, 0:1, :], first_acc[:])
+        gated(0, sums[0][:, 1:2, :], acc[:])
         turned = bank("g_turned", [P, P], 5)
         nc.tensor.transpose(turned[:], g_rows[:], identity[:])
-        g_cols = fresh("g_cols", [P, PACK], F32)
-        copy(False, g_cols[:], turned[:, 0:PACK])
-        scatter_dc(0, 0, first_sums[:, 0, :])
-        for t in range(1, PACK):
+        g_cols = fresh("g_cols", [P, T // P], F32)
+        copy(False, g_cols[:], turned[:, 0 : T // P])
+        for t in range(2):
             scatter_dc(t, 0, sums[0][:, t, :])
 
-        waiting = None
         for f in range(1, E2):
             woven = fresh(f"woven{f}", [P, PACK, P, PACK], BF16)
-            for h in range(2):
-                weave(halves[f, h], woven, 0, True, h * (P // 2))
-            if waiting is not None:
-                late = fresh(f"late{f}", [P, 2, C2], F32, f"raw{f}_1")
-                gated(f - 1, late[:], waiting[:])
-                for u in range(2):
-                    if (f, u) != (3, 0):
-                        scatter_dc(2 + u, f - 1, late[:, u, :])
+            if f == 1:
+                weave(f, 0, woven, False, m1=SHARE)
+            weave(f, 0, woven, True, m0=SHARE if f == 1 else 0)
+            weave(f, 1, woven, True)
+            late = fresh(f"late{f}", [P, 2, C2], F32, f"raw{f}_1")
+            gated(f - 1, late[:], waiting[:])
+            for u in range(2):
+                if (f, u) != (E2 - 1, 0):
+                    scatter_dc(2 + u, f - 1, late[:, u, :])
             operands = [quantise(f, t0, woven[:, t0 : t0 + 2]) for t0 in (0, 2)]
-            if f == 3:
-                scatter_dc(2, 2, late[:, 0, :], True)
+            if f == E2 - 1:
+                scatter_dc(2, f - 1, late[:, 0, :], True)
             acc = bank(f"acc{f}_0", [P, 2, C2], 2 * f - 1)
             waiting = bank(f"acc{f}_2", [P, 2, C2], 2 * f)
             multiply(f, acc, operands[0])
@@ -202,15 +202,10 @@ def tile_moe_seb_relu_kernel(
         for t in (2, 3):
             scatter_dc(t, E2 - 1, sums[E2 - 1][:, t, :])
 
-        def make_keep(first, count, tag):
-            kept = fresh(f"keep{first}", [P, PACK, count], F32, tag)
-            gate = g[:, first : first + count].unsqueeze(1).to_broadcast([P, 2, count])
-            for n in range(2):
-                values = a_of[n][:, :, first : first + count]
-                nc.vector.scalar_tensor_tensor(kept[:, 2 * n : 2 * n + 2, :], values, 0.0, gate, IS_GT, MULT)
-            return kept
-
-        keep0 = make_keep(0, T, f"codes{E2 - 1}_2")
+        keep = fresh("keep", [P, PACK, T], F32, f"codes{E2 - 1}_2")
+        gate = g[:].unsqueeze(1).to_broadcast([P, 2, T])
+        for n in range(2):
+            nc.vector.scalar_tensor_tensor(keep[:, 2 * n : 2 * n + 2, :], a_of[n][:], 0.0, gate, IS_GT, MULT)
         picked = [fresh(f"picked{e}", [P, PACK, C1], F32, "a0" if e else None) for e in range(E1)]
 
         def window(t, first, count):
@@ -218,20 +213,22 @@ def tile_moe_seb_relu_kernel(
 
         for t in range(PACK):
             copy(t == 0, picked[1][:, t, :], window(t, C1, C1))
-        for t, first, count in ((0, 0, C1), (1, 0, C1), (2, 0, C1), (3, 0, P), (3, P, P)):
-            cols = slice(first, first + count)
-            nc.vector.tensor_tensor(picked[0][:, t, cols], window(t, first, count), keep0[:, t, cols], MULT)
+        for t in range(PACK):
+            count = P if t == PACK - 1 else C1
+            for first in range(0, C1, count):
+                cols = slice(first, first + count)
+                nc.vector.tensor_tensor(picked[0][:, t, cols], window(t, first, count), keep[:, t, cols], MULT)
 
         codes = [fresh(f"da_codes{e}", [P, C1], U32) for e in range(E1)]
         scales = [fresh(f"da_scales{e}", [P, C1], U8) for e in range(E1)]
         result = {}
 
         def by_line(planes):
-            return planes.rearrange("p t (c i) -> p c t i", i=4)
+            return planes.rearrange("p t (c i) -> p c t i", i=LINE)
 
         def woven_da(name, count, tag=None):
             da = fresh(name, [P, count, PACK], BF16, tag)
-            return da, da[:].rearrange("p (c i) t -> p c t i", i=4)
+            return da, da[:].rearrange("p (c i) t -> p c t i", i=LINE)
 
         def quantise_da(da, first):
             cols = slice(first % C1, first % C1 + da.shape[1])
@@ -268,7 +265,8 @@ def tile_moe_seb_relu_kernel(
                 result[k] = fresh(f"result{k}", [P, T], F32, tag)
             copy(k >= 2, result[k][:].indirect(entries(list1, first, values.shape[1])), values)
             if first == C1:
-                nc.sync.dma_start(out[k * P : (k + 1) * P, :], result[k][:])
+                queue = nc.scalar if k == 1 else nc.sync
+                queue.dma_start(out[k * P : (k + 1) * P, :], result[k][:])
 
         lead = []
         for n in range(2):
@@ -283,7 +281,7 @@ def tile_moe_seb_relu_kernel(
         done.update(empty(product(P, P, (0, 2), 3), False))
         done.update(empty(product(0, C1, (1,), 4), False))
         da, view = woven_da("da2", C1, "da0")
-        nc.vector.tensor_tensor(view, by_line(picked[1][:]), by_line(keep0[:, :, C1:T]), MULT)
+        nc.vector.tensor_tensor(view, by_line(picked[1][:]), by_line(keep[:, :, C1:T]), MULT)
         done.update(empty(third, True))
         quantise_da(da, C1)
         done.update(empty(product(C1, C1, (2, 3), 5), False))

@@ -87,8 +87,8 @@ def tile_moe_seb_relu_kernel(
         load_half(1, 1)
         nc.sync.dma_start(g_rows[0 : T // P, :], gate1[0].rearrange("(c p) -> c p", p=P))
         load_half(2, 0)
-        load_half(2, 1)
         load_gate2(1, 1)
+        load_half(2, 1)
         load_half(3, 0)
         load_half(3, 1)
         load_gate2(2, 2)
@@ -211,8 +211,9 @@ def tile_moe_seb_relu_kernel(
         def window(t, first, count):
             return dc[t][:].indirect(entries(list1, first, count))
 
-        for t in range(PACK):
-            copy(t == 0, picked[1][:, t, :], window(t, C1, C1))
+        for first in (0, P):
+            for t in range(PACK):
+                copy(False, picked[1][:, t, first : first + P], window(t, C1 + first, P))
         for t in range(PACK):
             count = P if t == PACK - 1 else C1
             for first in range(0, C1, count):
@@ -240,7 +241,7 @@ def tile_moe_seb_relu_kernel(
 
         def product(first, count, blocks, number):
             e, cols = first // C1, slice(first % C1, first % C1 + count)
-            acc = bank(f"out_acc{number}", [P, len(blocks), count], number)
+            acc = bank(f"out_acc{first}_{blocks[0]}", [P, len(blocks), count], number)
             for u, k in enumerate(blocks):
                 column = e * T + k * P
                 nc.tensor.matmul_mx(
@@ -256,7 +257,7 @@ def tile_moe_seb_relu_kernel(
 
         def empty(made, on_vector):
             acc, first, blocks, number = made
-            values = fresh(f"out_sums{number}", list(acc.shape), F32)
+            values = fresh(f"out_sums{first}_{blocks[0]}", list(acc.shape), F32)
             copy(on_vector, values[:], acc[:])
             return {(k, first): values[:, u, :] for u, k in enumerate(blocks)}
 
@@ -281,12 +282,15 @@ def tile_moe_seb_relu_kernel(
         done.update(empty(product(P, P, (0, 2), 3), False))
         done.update(empty(product(0, C1, (1,), 4), False))
         da, view = woven_da("da2", C1, "da0")
-        nc.vector.tensor_tensor(view, by_line(picked[1][:]), by_line(keep[:, :, C1:T]), MULT)
+        for first in (0, P):
+            lines = slice(first // LINE, (first + P) // LINE)
+            nc.vector.tensor_tensor(view[:, lines], by_line(picked[1][:])[:, lines], by_line(keep[:, :, C1:T])[:, lines], MULT)
         done.update(empty(third, True))
         quantise_da(da, C1)
-        done.update(empty(product(C1, C1, (2, 3), 5), False))
         done.update(empty(product(C1, C1, (0,), 6), False))
         done.update(empty(product(C1, C1, (1,), 1), False))
+        done.update(empty(product(C1, C1, (2,), 5), True))
+        done.update(empty(product(C1, C1, (3,), 7), True))
         send(0, 0, done[0, 0])
         send(2, 0, done[2, 0], "a0")
         for k in (0, 2):

@@ -277,25 +277,24 @@ def tile_moe_seb_relu_kernel(
         for n in range(2):
             quantise_da(lead[n], n * P)
         done = empty(product(0, P, (0,), 7), False)
-        done.update(empty(product(0, P, (2,), 0), False))
-        third = product(0, C1, (3,), 2)
-        done.update(empty(product(P, P, (0, 2), 3), False))
-        done.update(empty(product(0, C1, (1,), 4), False))
+        done.update(empty(product(0, P, (1,), 0), False))
+        done.update(empty(product(P, P, (0, 1), 3), False))
+        own = [product(0, C1, (k,), number) for k, number in ((2, 2), (3, 4))]
         da, view = woven_da("da2", C1, "da0")
         for first in (0, P):
             lines = slice(first // LINE, (first + P) // LINE)
             nc.vector.tensor_tensor(view[:, lines], by_line(picked[1][:])[:, lines], by_line(keep[:, :, C1:T])[:, lines], MULT)
-        done.update(empty(third, True))
+        done.update(empty(own[0], True))
         quantise_da(da, C1)
+        done.update(empty(own[1], True))
         done.update(empty(product(C1, C1, (0,), 6), False))
         done.update(empty(product(C1, C1, (1,), 1), False))
         done.update(empty(product(C1, C1, (2,), 5), True))
         done.update(empty(product(C1, C1, (3,), 7), True))
-        send(0, 0, done[0, 0])
-        send(2, 0, done[2, 0], "a0")
-        for k in (0, 2):
-            send(k, P, done[k, P])
-        send(1, 0, done[1, 0])
-        send(3, 0, done[3, 0])
+        for first in (0, P):
+            for k in (0, 1):
+                send(k, first, done[k, first])
+        for k in (2, 3):
+            send(k, 0, done[k, 0])
         for k in range(T // P):
             send(k, C1, done[k, C1])

@@ -266,8 +266,7 @@ def tile_moe_seb_relu_kernel(
                 result[k] = fresh(f"result{k}", [P, T], F32, tag)
             copy(k >= 2, result[k][:].indirect(entries(list1, first, values.shape[1])), values)
             if first == C1:
-                queue = nc.scalar if k == 1 else nc.sync
-                queue.dma_start(out[k * P : (k + 1) * P, :], result[k][:])
+                nc.sync.dma_start(out[k * P : (k + 1) * P, :], result[k][:])
 
         lead = []
         for n in range(2):
@@ -286,15 +285,15 @@ def tile_moe_seb_relu_kernel(
             nc.vector.tensor_tensor(view[:, lines], by_line(picked[1][:])[:, lines], by_line(keep[:, :, C1:T])[:, lines], MULT)
         done.update(empty(own[0], True))
         quantise_da(da, C1)
-        done.update(empty(own[1], True))
+        done.update(empty(own[1], False))
         done.update(empty(product(C1, C1, (0,), 6), False))
-        done.update(empty(product(C1, C1, (1,), 1), False))
         done.update(empty(product(C1, C1, (2,), 5), True))
+        done.update(empty(product(C1, C1, (1,), 1), False))
         done.update(empty(product(C1, C1, (3,), 7), True))
         for first in (0, P):
             for k in (0, 1):
                 send(k, first, done[k, first])
         for k in (2, 3):
             send(k, 0, done[k, 0])
-        for k in range(T // P):
+        for k in (0, 2, 1, 3):
             send(k, C1, done[k, C1])

@@ -22,6 +22,8 @@ E2, C2 = 4, 128
 PACK = 4
 LINE = 4
 SHARE = 40
+WINDOW = 704
+CUT = 64
 FLOPS = 2 * 2 * T * T * T
 
 
@@ -51,18 +53,19 @@ def tile_moe_seb_relu_kernel(
 
         list2 = lists.tile([P, T // 16], U16, name="list2")
         list1 = lists.tile([P, T // 16], U16, name="list1")
-        dy_w = fresh("dy_w", [P, T], I32)
-        dy_s = fresh("dy_s", [P, T], U8)
+        dy_w = fresh("dy_w", [P, WINDOW], I32)
+        dy_s = fresh("dy_s", [P, WINDOW], U8)
         w1_w = fresh("w1_w", [P, E1 * 2 * T], U8)
         w1_s = fresh("w1_s", [P, E1 * T], U8)
         nc.gpsimd.memset(dy_s[:].bitcast(I32), 0)
+        nc.vector.memset(dy_w[:, T:WINDOW], 0)
         nc.vector.memset(w1_s[:].bitcast(I32), 0)
         g_rows = fresh("g_rows", [P, P], F32)
         identity = fresh("identity", [P, P], F32)
         nc.vector.memset(g_rows[:], 0.0)
         make_identity(nc, identity[:])
 
-        nc.sync.dma_start(dy_w[:], dy_words[0].rearrange("p t d -> p (t d)").bitcast(I32))
+        nc.sync.dma_start(dy_w[:, 0:T], dy_words[0].rearrange("p t d -> p (t d)").bitcast(I32))
         nc.sync.dma_start(list2[:], offs2)
         q = []
         halves = {}
@@ -74,7 +77,7 @@ def tile_moe_seb_relu_kernel(
 
         load_half(0, 0)
         for r in range(4):
-            nc.sync.dma_start(dy_s[r:P:32, :].bitcast(I32), dy_scales[0, r:16:4, :].bitcast(I32))
+            nc.sync.dma_start(dy_s[r:P:32, 0:T].bitcast(I32), dy_scales[0, r:16:4, :].bitcast(I32))
         load_half(0, 1)
 
         def load_gate2(first, experts):
@@ -84,12 +87,16 @@ def tile_moe_seb_relu_kernel(
 
         load_half(1, 0)
         load_gate2(0, 1)
-        load_half(1, 1)
         nc.sync.dma_start(g_rows[0 : T // P, :], gate1[0].rearrange("(c p) -> c p", p=P))
+        load_half(1, 1)
+        q_again = fresh("q_again", [P, C2], F32)
+        nc.sync.dma_start(q_again[:], gate2[:, 0:C2])
         load_half(2, 0)
         load_gate2(1, 1)
         load_half(2, 1)
         load_half(3, 0)
+        q_early = fresh("q_early", [P, C2], F32)
+        nc.sync.dma_start(q_early[:], gate2[:, 2 * C2 : 3 * C2])
         load_half(3, 1)
         load_gate2(2, 2)
         nc.sync.dma_start(list1[:], offs)
@@ -109,12 +116,8 @@ def tile_moe_seb_relu_kernel(
 
         gq_w = fresh("gq_w", [P, T], U32)
         gq_s = fresh("gq_s", [P, T], U8)
-        for first, count in ((0, C2), (C2, T - C2)):
-            cols = slice(first, first + count)
-            nc.vector.tensor_copy(gq_w[:, cols], dy_w[:].bitcast(U32).indirect(entries(list2, first, count)))
-        for first, count in ((0, C2), (C2, T - C2)):
-            cols = slice(first, first + count)
-            nc.vector.tensor_copy(gq_s[:, cols], dy_s[:].indirect(entries(list2, first, count)))
+        nc.vector.tensor_copy(gq_w[:], dy_w[:].bitcast(U32).indirect(list2[:]))
+        nc.vector.tensor_copy(gq_s[:], dy_s[:].indirect(list2[:]))
 
         dc = [fresh(f"dc{t}", [P, T], F32) for t in range(PACK)]
 
@@ -144,13 +147,14 @@ def tile_moe_seb_relu_kernel(
                     stop=True,
                 )
 
-        def gated(f, place, acc):
-            nc.vector.tensor_tensor(place, acc, q[f].unsqueeze(1).to_broadcast(list(place.shape)), MULT)
+        def gated(f, place, acc, gate=None):
+            gate = q[f] if gate is None else gate
+            nc.vector.tensor_tensor(place, acc, gate.unsqueeze(1).to_broadcast(list(place.shape)), MULT)
 
         def scatter_dc(t, f, values, on_vector=False):
             copy(on_vector, dc[t][:].indirect(entries(list2, f * C2, values.shape[-1])), values)
 
-        sums = [fresh(f"sums{f}", [P, PACK, C2], F32) for f in range(E2)]
+        sums = [fresh(f"sums{f}", [P, PACK if f == E2 - 1 else 2, C2], F32) for f in range(E2)]
         woven = fresh("woven0", [P, PACK, P, PACK], BF16)
         weave(0, 0, woven, False)
         weave(0, 1, woven, True, 0, 2)
@@ -172,35 +176,52 @@ def tile_moe_seb_relu_kernel(
         for t in range(2):
             scatter_dc(t, 0, sums[0][:, t, :])
 
+        middle = fresh("middle", [P, PACK, C2], F32)
         for f in range(1, E2):
+            last = f == E2 - 1
             woven = fresh(f"woven{f}", [P, PACK, P, PACK], BF16)
             if f == 1:
                 weave(f, 0, woven, False, m1=SHARE)
-            weave(f, 0, woven, True, m0=SHARE if f == 1 else 0)
-            weave(f, 1, woven, True)
-            late = fresh(f"late{f}", [P, 2, C2], F32, f"raw{f}_1")
-            gated(f - 1, late[:], waiting[:])
-            for u in range(2):
-                if (f, u) != (E2 - 1, 0):
-                    scatter_dc(2 + u, f - 1, late[:, u, :])
-            operands = [quantise(f, t0, woven[:, t0 : t0 + 2]) for t0 in (0, 2)]
-            if f == E2 - 1:
-                scatter_dc(2, f - 1, late[:, 0, :], True)
-            acc = bank(f"acc{f}_0", [P, 2, C2], 2 * f - 1)
-            waiting = bank(f"acc{f}_2", [P, 2, C2], 2 * f)
-            multiply(f, acc, operands[0])
-            multiply(f, waiting, operands[1])
-            gated(f, sums[f][:, 0:2, :], acc[:])
-            for t in range(2):
-                scatter_dc(t, f, sums[f][:, t, :])
+                weave(f, 0, woven, True, m0=SHARE)
+                weave(f, 1, woven, True)
+                late = fresh("late", [P, 2, C2], F32)
+                gated(0, late[:], waiting[:], q_again[:])
+                for u in range(2):
+                    scatter_dc(2 + u, 0, late[:, u, :])
+            else:
+                weave(f, 0, woven, True)
+            if last:
+                weave(f, 1, woven, True)
+                gated(f - 1, middle[:, 2:PACK, :], waiting[:])
+                scatter_dc(3, f - 1, middle[:, 3, :])
+            elif f == 2:
+                weave(f, 1, woven, True, 0, 2)
+                weave(f, 1, woven, True, 2, PACK)
+            operands = quantise(f, 0, woven[:, 0:2]) + quantise(f, 2, woven[:, 2:PACK])
+            if last:
+                both = middle[:, 1:3, :].rearrange("p u s -> p (u s)")[:, CUT : 2 * C2]
+                copy(True, dc[2][:].indirect(entries(list2, C2 + CUT, 2 * C2 - CUT)), both)
+                acc = bank("acc3", [P, PACK, C2], 4)
+                multiply(f, acc, operands)
+                gated(f, sums[f][:], acc[:])
+                for t in range(PACK):
+                    scatter_dc(t, f, sums[f][:, t, :])
+            else:
+                acc = bank(f"acc{f}_0", [P, 2, C2], f + 1)
+                waiting = bank(f"acc{f}_2", [P, 2, C2], 4 * f - 3)
+                multiply(f, acc, operands[0:2])
+                multiply(f, waiting, operands[2:PACK] if f == 2 else [operands[3], operands[2]])
+                gated(f, sums[f][:], acc[:], q_early[:] if f == 2 else None)
+                for t in range(2):
+                    scatter_dc(t, f, sums[f][:, t, :])
             if f == 1:
-                g = bank("g", [P, T], 1)
+                gated(f, middle[:, 0:2, :], waiting[:])
+                scatter_dc(2, f, middle[:, 1, 0:CUT])
+                scatter_dc(3, f, middle[:, 0, :])
+                g = bank("g", [P, T], 2)
                 for c in range(T // P):
                     column = g_cols[:, c : c + 1].to_broadcast([P, P])
                     nc.tensor.transpose(g[:, c * P : (c + 1) * P], column, identity[:])
-        gated(E2 - 1, sums[E2 - 1][:, 2:PACK, :], waiting[:])
-        for t in (2, 3):
-            scatter_dc(t, E2 - 1, sums[E2 - 1][:, t, :])
 
         keep = fresh("keep", [P, PACK, T], F32, f"codes{E2 - 1}_2")
         gate = g[:].unsqueeze(1).to_broadcast([P, 2, T])
@@ -278,7 +299,7 @@ def tile_moe_seb_relu_kernel(
         done = empty(product(0, P, (0,), 7), False)
         done.update(empty(product(0, P, (1,), 0), False))
         done.update(empty(product(P, P, (0, 1), 3), False))
-        own = [product(0, C1, (k,), number) for k, number in ((2, 2), (3, 4))]
+        own = [product(0, C1, (k,), number) for k, number in ((2, 1), (3, 4))]
         da, view = woven_da("da2", C1, "da0")
         for first in (0, P):
             lines = slice(first // LINE, (first + P) // LINE)
@@ -288,7 +309,7 @@ def tile_moe_seb_relu_kernel(
         done.update(empty(own[1], False))
         done.update(empty(product(C1, C1, (0,), 6), False))
         done.update(empty(product(C1, C1, (2,), 5), True))
-        done.update(empty(product(C1, C1, (1,), 1), False))
+        done.update(empty(product(C1, C1, (1,), 2), False))
         done.update(empty(product(C1, C1, (3,), 7), True))
         for first in (0, P):
             for k in (0, 1):

@@ -23,7 +23,6 @@ PACK = 4
 LINE = 4
 SHARE = 40
 WINDOW = 704
-CUT = 64
 FLOPS = 2 * 2 * T * T * T
 
 
@@ -89,21 +88,19 @@ def tile_moe_seb_relu_kernel(
         load_gate2(0, 1)
         nc.sync.dma_start(g_rows[0 : T // P, :], gate1[0].rearrange("(c p) -> c p", p=P))
         load_half(1, 1)
-        q_again = fresh("q_again", [P, C2], F32)
-        nc.sync.dma_start(q_again[:], gate2[:, 0:C2])
         load_half(2, 0)
         load_gate2(1, 1)
         load_half(2, 1)
         load_half(3, 0)
-        q_early = fresh("q_early", [P, C2], F32)
-        nc.sync.dma_start(q_early[:], gate2[:, 2 * C2 : 3 * C2])
+        load_gate2(2, 1)
         load_half(3, 1)
-        load_gate2(2, 2)
         nc.sync.dma_start(list1[:], offs)
         a_rows = a.rearrange("(p t) s -> p t s", t=PACK)
         a_of = [fresh(f"a{n}", [P, 2, T], F32) for n in range(2)]
         for n in range(2):
             nc.sync.dma_start(a_of[n][:], a_rows[:, 2 * n : 2 * n + 2, :])
+            if n == 0:
+                load_gate2(3, 1)
         nc.sync.dma_start(
             w1_w[:].bitcast(I32).rearrange("p (e c) -> p e c", e=E1),
             w1t_words[:, 0].bitcast(I32).rearrange("e p c -> p e c"),
@@ -154,7 +151,7 @@ def tile_moe_seb_relu_kernel(
         def scatter_dc(t, f, values, on_vector=False):
             copy(on_vector, dc[t][:].indirect(entries(list2, f * C2, values.shape[-1])), values)
 
-        sums = [fresh(f"sums{f}", [P, PACK if f == E2 - 1 else 2, C2], F32) for f in range(E2)]
+        sums = [fresh(f"sums{f}", [P, PACK if f else 2, C2], F32) for f in range(E2)]
         woven = fresh("woven0", [P, PACK, P, PACK], BF16)
         weave(0, 0, woven, False)
         weave(0, 1, woven, True, 0, 2)
@@ -176,7 +173,13 @@ def tile_moe_seb_relu_kernel(
         for t in range(2):
             scatter_dc(t, 0, sums[0][:, t, :])
 
-        middle = fresh("middle", [P, PACK, C2], F32)
+        keep = fresh("keep", [P, PACK, T], F32)
+
+        def make_keep(t0, t1):
+            gate = g[:].unsqueeze(1).to_broadcast([P, t1 - t0, T])
+            planes = a_of[t0 // 2][:, t0 % 2 : t0 % 2 + t1 - t0, :]
+            nc.vector.scalar_tensor_tensor(keep[:, t0:t1, :], planes, 0.0, gate, IS_GT, MULT)
+
         for f in range(1, E2):
             last = f == E2 - 1
             woven = fresh(f"woven{f}", [P, PACK, P, PACK], BF16)
@@ -184,50 +187,31 @@ def tile_moe_seb_relu_kernel(
                 weave(f, 0, woven, False, m1=SHARE)
                 weave(f, 0, woven, True, m0=SHARE)
                 weave(f, 1, woven, True)
-                late = fresh("late", [P, 2, C2], F32)
-                gated(0, late[:], waiting[:], q_again[:])
-                for u in range(2):
-                    scatter_dc(2 + u, 0, late[:, u, :])
+                late = fresh("late", [P, 2, C2], F32, "raw1_1")
+                gated(0, late[:], waiting[:])
+                for t in (2, 3):
+                    scatter_dc(t, 0, late[:, t - 2, :])
             else:
                 weave(f, 0, woven, True)
-            if last:
-                weave(f, 1, woven, True)
-                gated(f - 1, middle[:, 2:PACK, :], waiting[:])
-                scatter_dc(3, f - 1, middle[:, 3, :])
-            elif f == 2:
                 weave(f, 1, woven, True, 0, 2)
                 weave(f, 1, woven, True, 2, PACK)
             operands = quantise(f, 0, woven[:, 0:2]) + quantise(f, 2, woven[:, 2:PACK])
             if last:
-                both = middle[:, 1:3, :].rearrange("p u s -> p (u s)")[:, CUT : 2 * C2]
-                copy(True, dc[2][:].indirect(entries(list2, C2 + CUT, 2 * C2 - CUT)), both)
-                acc = bank("acc3", [P, PACK, C2], 4)
-                multiply(f, acc, operands)
-                gated(f, sums[f][:], acc[:])
-                for t in range(PACK):
-                    scatter_dc(t, f, sums[f][:, t, :])
-            else:
-                acc = bank(f"acc{f}_0", [P, 2, C2], f + 1)
-                waiting = bank(f"acc{f}_2", [P, 2, C2], 4 * f - 3)
-                multiply(f, acc, operands[0:2])
-                multiply(f, waiting, operands[2:PACK] if f == 2 else [operands[3], operands[2]])
-                gated(f, sums[f][:], acc[:], q_early[:] if f == 2 else None)
-                for t in range(2):
-                    scatter_dc(t, f, sums[f][:, t, :])
+                make_keep(0, 2)
+            for t0, count, number in ((0, 2, f + 1), (2, 2, (1, 5, 6)[f - 1])):
+                acc = bank(f"acc{f}_{t0}", [P, count, C2], number)
+                multiply(f, acc, operands[t0 : t0 + count])
+                gated(f, sums[f][:, t0 : t0 + count, :], acc[:])
+            for t in range(PACK):
+                scatter_dc(t, f, sums[f][:, t, :], (f, t) == (E2 - 1, 1))
             if f == 1:
-                gated(f, middle[:, 0:2, :], waiting[:])
-                scatter_dc(2, f, middle[:, 1, 0:CUT])
-                scatter_dc(3, f, middle[:, 0, :])
                 g = bank("g", [P, T], 2)
                 for c in range(T // P):
                     column = g_cols[:, c : c + 1].to_broadcast([P, P])
                     nc.tensor.transpose(g[:, c * P : (c + 1) * P], column, identity[:])
 
-        keep = fresh("keep", [P, PACK, T], F32, f"codes{E2 - 1}_2")
-        gate = g[:].unsqueeze(1).to_broadcast([P, 2, T])
-        for n in range(2):
-            nc.vector.scalar_tensor_tensor(keep[:, 2 * n : 2 * n + 2, :], a_of[n][:], 0.0, gate, IS_GT, MULT)
-        picked = [fresh(f"picked{e}", [P, PACK, C1], F32, "a0" if e else None) for e in range(E1)]
+        make_keep(2, PACK)
+        picked = [fresh(f"picked{e}", [P, PACK, C1], F32, "q3" if e else None) for e in range(E1)]
 
         def window(t, first, count):
             return dc[t][:].indirect(entries(list1, first, count))

@@ -57,7 +57,6 @@ def tile_moe_seb_relu_kernel(
         w1_w = fresh("w1_w", [P, E1 * 2 * T], U8)
         w1_s = fresh("w1_s", [P, E1 * T], U8)
         nc.gpsimd.memset(dy_s[:].bitcast(I32), 0)
-        nc.vector.memset(dy_w[:, T:WINDOW], 0)
         nc.vector.memset(w1_s[:].bitcast(I32), 0)
         g_rows = fresh("g_rows", [P, P], F32)
         identity = fresh("identity", [P, P], F32)

@@ -22,7 +22,6 @@ E2, C2 = 4, 128
 PACK = 4
 LINE = 4
 SHARE = 40
-WINDOW = 704
 FLOPS = 2 * 2 * T * T * T
 
 
@@ -52,8 +51,8 @@ def tile_moe_seb_relu_kernel(
 
         list2 = lists.tile([P, T // 16], U16, name="list2")
         list1 = lists.tile([P, T // 16], U16, name="list1")
-        dy_w = fresh("dy_w", [P, WINDOW], I32)
-        dy_s = fresh("dy_s", [P, WINDOW], U8)
+        dy_w = fresh("dy_w", [P, T], I32)
+        dy_s = fresh("dy_s", [P, T], U8)
         w1_w = fresh("w1_w", [P, E1 * 2 * T], U8)
         w1_s = fresh("w1_s", [P, E1 * T], U8)
         nc.gpsimd.memset(dy_s[:].bitcast(I32), 0)
@@ -63,7 +62,7 @@ def tile_moe_seb_relu_kernel(
         nc.vector.memset(g_rows[:], 0.0)
         make_identity(nc, identity[:])
 
-        nc.sync.dma_start(dy_w[:, 0:T], dy_words[0].rearrange("p t d -> p (t d)").bitcast(I32))
+        nc.sync.dma_start(dy_w[:], dy_words[0].rearrange("p t d -> p (t d)").bitcast(I32))
         nc.sync.dma_start(list2[:], offs2)
         q = []
         halves = {}
@@ -75,7 +74,7 @@ def tile_moe_seb_relu_kernel(
 
         load_half(0, 0)
         for r in range(4):
-            nc.sync.dma_start(dy_s[r:P:32, 0:T].bitcast(I32), dy_scales[0, r:16:4, :].bitcast(I32))
+            nc.sync.dma_start(dy_s[r:P:32, :].bitcast(I32), dy_scales[0, r:16:4, :].bitcast(I32))
         load_half(0, 1)
 
         def load_gate2(first, experts):
@@ -112,8 +111,12 @@ def tile_moe_seb_relu_kernel(
 
         gq_w = fresh("gq_w", [P, T], U32)
         gq_s = fresh("gq_s", [P, T], U8)
-        nc.vector.tensor_copy(gq_w[:], dy_w[:].bitcast(U32).indirect(list2[:]))
-        nc.vector.tensor_copy(gq_s[:], dy_s[:].indirect(list2[:]))
+        for first, count in ((0, C2), (C2, T - C2)):
+            cols = slice(first, first + count)
+            nc.vector.tensor_copy(gq_w[:, cols], dy_w[:].bitcast(U32).indirect(entries(list2, first, count)))
+        for first, count in ((0, C2), (C2, T - C2)):
+            cols = slice(first, first + count)
+            nc.vector.tensor_copy(gq_s[:, cols], dy_s[:].indirect(entries(list2, first, count)))
 
         dc = [fresh(f"dc{t}", [P, T], F32) for t in range(PACK)]
 

@@ -22,6 +22,7 @@ E2, C2 = 4, 128
 PACK = 4
 LINE = 4
 SHARE = 40
+CUT = 96
 FLOPS = 2 * 2 * T * T * T
 
 
@@ -182,6 +183,7 @@ def tile_moe_seb_relu_kernel(
             planes = a_of[t0 // 2][:, t0 % 2 : t0 % 2 + t1 - t0, :]
             nc.vector.scalar_tensor_tensor(keep[:, t0:t1, :], planes, 0.0, gate, IS_GT, MULT)
 
+        border = fresh("border", [P, PACK, C2], F32)
         for f in range(1, E2):
             last = f == E2 - 1
             woven = fresh(f"woven{f}", [P, PACK, P, PACK], BF16)
@@ -202,10 +204,21 @@ def tile_moe_seb_relu_kernel(
                 make_keep(0, 2)
             for t0, count, number in ((0, 2, f + 1), (2, 2, (1, 5, 6)[f - 1])):
                 acc = bank(f"acc{f}_{t0}", [P, count, C2], number)
-                multiply(f, acc, operands[t0 : t0 + count])
-                gated(f, sums[f][:, t0 : t0 + count, :], acc[:])
-            for t in range(PACK):
-                scatter_dc(t, f, sums[f][:, t, :], (f, t) == (E2 - 1, 1))
+                shared = f >= 2 and t0 == 0
+                multiply(f, acc, operands[1::-1] if shared and last else operands[t0 : t0 + count])
+                gated(f, border[:, 2 * f - 4 : 2 * f - 2, :] if shared else sums[f][:, t0 : t0 + count, :], acc[:])
+            if f == 1:
+                for t in range(2):
+                    scatter_dc(t, f, sums[f][:, t, :])
+            elif last:
+                scatter_dc(0, f, border[:, 3, :])
+                both = border[:, 1:3, :].rearrange("p u s -> p (u s)")[:, CUT : 2 * C2]
+                copy(True, dc[1][:].indirect(entries(list2, 2 * C2 + CUT, 2 * C2 - CUT)), both)
+            else:
+                scatter_dc(0, f, border[:, 0, :])
+                scatter_dc(1, f, border[:, 1, 0:CUT])
+            for t in (2, 3):
+                scatter_dc(t, f, sums[f][:, t, :])
             if f == 1:
                 g = bank("g", [P, T], 2)
                 for c in range(T // P):

from contextlib import ExitStack

import concourse.mybir as mybir
from concourse.masks import make_identity

F32 = mybir.dt.float32
BF16 = mybir.dt.bfloat16
I32 = mybir.dt.int32
U32 = mybir.dt.uint32
U16 = mybir.dt.uint16
U8 = mybir.dt.uint8
FP8X4 = mybir.dt.float8_e4m3fn_x4
FP4X4 = mybir.dt.float4_e2m1fn_x4
MULT = mybir.AluOpType.mult
IS_GT = mybir.AluOpType.is_gt
COPY = mybir.ActivationFunctionType.Copy

P = 128
T = 512
E1, C1 = 2, 256
E2, C2 = 4, 128
PACK = 4
LINE = 4
SHARE = 40
CUT = 96
FLOPS = 2 * 2 * T * T * T


def tile_moe_seb_relu_kernel(
    tc, dy_words, dy_scales, w2t, w1t_words, w1t_scales, a, gate1, gate2, offs, offs2, out
):
    nc = tc.nc
    with ExitStack() as ctx:
        lists = ctx.enter_context(tc.tile_pool(name="lists", bufs=1))
        sb = ctx.enter_context(tc.tile_pool(name="sb", bufs=1))
        psum = ctx.enter_context(tc.psum_pool(name="psum", bufs=1))

        def fresh(name, shape, dtype, tag=None):
            return sb.tile(shape, dtype, name=name, tag=tag or name, align_bytes=64)

        def bank(name, shape, number):
            return psum.tile(shape, F32, name=name, tag=f"bank{number}")

        def entries(lst, first, count):
            return lst[:, first // 16 : (first + count) // 16]

        def copy(on_vector, dst, src):
            if on_vector:
                nc.vector.tensor_copy(dst, src)
            else:
                nc.scalar.activation(dst, src, COPY)

        list2 = lists.tile([P, T // 16], U16, name="list2")
        list1 = lists.tile([P, T // 16], U16, name="list1")
        dy_w = fresh("dy_w", [P, T], I32)
        dy_s = fresh("dy_s", [P, T], U8)
        w1_w = fresh("w1_w", [P, E1 * 2 * T], U8)
        w1_s = fresh("w1_s", [P, E1 * T], U8)
        nc.gpsimd.memset(dy_s[:].bitcast(I32), 0)
        nc.vector.memset(w1_s[:].bitcast(I32), 0)
        g_rows = fresh("g_rows", [P, P], F32)
        identity = fresh("identity", [P, P], F32)
        nc.vector.memset(g_rows[:], 0.0)
        make_identity(nc, identity[:])

        nc.sync.dma_start(dy_w[:], dy_words[0].rearrange("p t d -> p (t d)").bitcast(I32))
        nc.sync.dma_start(list2[:], offs2)
        q = []
        halves = {}

        def load_half(f, h):
            halves[f, h] = fresh(f"raw{f}_{h}", [P, PACK, T // 2], F32)
            rows = w2t[f].rearrange("(p j) i -> p j i", j=PACK)
            nc.sync.dma_start(halves[f, h][:], rows[:, :, h * (T // 2) : (h + 1) * (T // 2)])

        load_half(0, 0)
        for r in range(4):
            nc.sync.dma_start(dy_s[r:P:32, :].bitcast(I32), dy_scales[0, r:16:4, :].bitcast(I32))
        load_half(0, 1)

        def load_gate2(first, experts):
            tile = fresh(f"q{first}", [P, experts * C2], F32)
            nc.sync.dma_start(tile[:], gate2[:, first * C2 : (first + experts) * C2])
            q.extend([tile[:, n * C2 : (n + 1) * C2] for n in range(experts)])

        load_half(1, 0)
        load_gate2(0, 1)
        nc.sync.dma_start(g_rows[0 : T // P, :], gate1[0].rearrange("(c p) -> c p", p=P))
        load_half(1, 1)
        load_half(2, 0)
        load_gate2(1, 1)
        load_half(2, 1)
        load_half(3, 0)
        load_gate2(2, 1)
        load_half(3, 1)
        nc.sync.dma_start(list1[:], offs)
        a_rows = a.rearrange("(p t) s -> p t s", t=PACK)
        a_of = [fresh(f"a{n}", [P, 2, T], F32) for n in range(2)]
        for n in range(2):
            nc.sync.dma_start(a_of[n][:], a_rows[:, 2 * n : 2 * n + 2, :])
            if n == 0:
                load_gate2(3, 1)
        nc.sync.dma_start(
            w1_w[:].bitcast(I32).rearrange("p (e c) -> p e c", e=E1),
            w1t_words[:, 0].bitcast(I32).rearrange("e p c -> p e c"),
        )
        for r in range(4):
            nc.sync.dma_start(
                w1_s[r:P:32, :].bitcast(I32).rearrange("p (e c) -> p e c", e=E1),
                w1t_scales[:, 0, r:16:4, :].bitcast(I32).rearrange("e b c -> b e c"),
            )

        gq_w = fresh("gq_w", [P, T], U32)
        gq_s = fresh("gq_s", [P, T], U8)
        for first, count in ((0, C2), (C2, T - C2)):
            cols = slice(first, first + count)
            nc.vector.tensor_copy(gq_w[:, cols], dy_w[:].bitcast(U32).indirect(entries(list2, first, count)))
        for first, count in ((0, C2), (C2, T - C2)):
            cols = slice(first, first + count)
            nc.vector.tensor_copy(gq_s[:, cols], dy_s[:].indirect(entries(list2, first, count)))

        dc = [fresh(f"dc{t}", [P, T], F32) for t in range(PACK)]

        def weave(f, h, woven, on_vector, t0=0, t1=PACK, m0=0, m1=P // 2):
            src = halves[f, h][:].rearrange("p j (m t) -> p m j t", t=PACK)
            dst = woven[:].rearrange("p t m j -> p m j t")[:, h * (P // 2) : (h + 1) * (P // 2)]
            copy(on_vector, dst[:, m0:m1, :, t0:t1], src[:, m0:m1, :, t0:t1])

        def quantise(f, t0, woven):
            width = woven.shape[1] * P
            codes = fresh(f"codes{f}_{t0}", [P, width], U32)
            scales = fresh(f"scales{f}_{t0}", [P, width], U8)
            nc.vector.quantize_mx(
                out=codes[:].bitcast(FP8X4), scales=scales[:], in_=woven.rearrange("p t m j -> p (t m j)")
            )
            return [(codes[:, c : c + P], scales[:, c : c + P]) for c in range(0, width, P)]

        def multiply(f, acc, operands):
            for u, (codes, scales) in enumerate(operands):
                nc.tensor.matmul_mx(
                    out=acc[:, u, :],
                    lhsT=codes.bitcast(FP8X4),
                    lhsT_scale=scales,
                    rhs=gq_w[:, f * C2 : (f + 1) * C2].bitcast(FP8X4),
                    rhs_scale=gq_s[:, f * C2 : (f + 1) * C2],
                    start=True,
                    stop=True,
                )

        def gated(f, place, acc, gate=None):
            gate = q[f] if gate is None else gate
            nc.vector.tensor_tensor(place, acc, gate.unsqueeze(1).to_broadcast(list(place.shape)), MULT)

        def scatter_dc(t, f, values, on_vector=False):
            copy(on_vector, dc[t][:].indirect(entries(list2, f * C2, values.shape[-1])), values)

        sums = [fresh(f"sums{f}", [P, PACK if f else 2, C2], F32) for f in range(E2)]
        woven = fresh("woven0", [P, PACK, P, PACK], BF16)
        weave(0, 0, woven, False)
        weave(0, 1, woven, True, 0, 2)
        weave(0, 1, woven, True, 2, PACK)
        operands = quantise(0, 0, woven[:, 0:1])
        first_acc = bank("acc_first", [P, 1, C2], 7)
        multiply(0, first_acc, operands)
        operands = quantise(0, 1, woven[:, 1:PACK])
        acc = bank("acc0", [P, 1, C2], 6)
        waiting = bank("acc0_2", [P, 2, C2], 0)
        multiply(0, acc, operands[0:1])
        multiply(0, waiting, operands[1:])
        gated(0, sums[0][:, 0:1, :], first_acc[:])
        gated(0, sums[0][:, 1:2, :], acc[:])
        turned = bank("g_turned", [P, P], 5)
        nc.tensor.transpose(turned[:], g_rows[:], identity[:])
        g_cols = fresh("g_cols", [P, T // P], F32)
        copy(False, g_cols[:], turned[:, 0 : T // P])
        for t in range(2):
            scatter_dc(t, 0, sums[0][:, t, :])

        keep = fresh("keep", [P, PACK, T], F32)

        def make_keep(t0, t1):
            gate = g[:].unsqueeze(1).to_broadcast([P, t1 - t0, T])
            planes = a_of[t0 // 2][:, t0 % 2 : t0 % 2 + t1 - t0, :]
            nc.vector.scalar_tensor_tensor(keep[:, t0:t1, :], planes, 0.0, gate, IS_GT, MULT)

        border = fresh("border", [P, PACK, C2], F32)
        for f in range(1, E2):
            last = f == E2 - 1
            woven = fresh(f"woven{f}", [P, PACK, P, PACK], BF16)
            if f == 1:
                weave(f, 0, woven, False, m1=SHARE)
                weave(f, 0, woven, True, m0=SHARE)
                weave(f, 1, woven, True)
                late = fresh("late", [P, 2, C2], F32, "raw1_1")
                gated(0, late[:], waiting[:])
                for t in (2, 3):
                    scatter_dc(t, 0, late[:, t - 2, :])
            else:
                weave(f, 0, woven, True)
                weave(f, 1, woven, True, 0, 2)
                weave(f, 1, woven, True, 2, PACK)
            operands = quantise(f, 0, woven[:, 0:2]) + quantise(f, 2, woven[:, 2:PACK])
            if last:
                make_keep(0, 2)
            for t0, count, number in ((0, 2, f + 1), (2, 2, (1, 5, 6)[f - 1])):
                acc = bank(f"acc{f}_{t0}", [P, count, C2], number)
                shared = f >= 2 and t0 == 0
                multiply(f, acc, operands[1::-1] if shared and last else operands[t0 : t0 + count])
                gated(f, border[:, 2 * f - 4 : 2 * f - 2, :] if shared else sums[f][:, t0 : t0 + count, :], acc[:])
            if f == 1:
                for t in range(2):
                    scatter_dc(t, f, sums[f][:, t, :])
            elif last:
                scatter_dc(0, f, border[:, 3, :])
                both = border[:, 1:3, :].rearrange("p u s -> p (u s)")[:, CUT : 2 * C2]
                copy(True, dc[1][:].indirect(entries(list2, 2 * C2 + CUT, 2 * C2 - CUT)), both)
            else:
                scatter_dc(0, f, border[:, 0, :])
                scatter_dc(1, f, border[:, 1, 0:CUT])
            for t in (2, 3):
                scatter_dc(t, f, sums[f][:, t, :])
            if f == 1:
                g = bank("g", [P, T], 2)
                for c in range(T // P):
                    column = g_cols[:, c : c + 1].to_broadcast([P, P])
                    nc.tensor.transpose(g[:, c * P : (c + 1) * P], column, identity[:])

        make_keep(2, PACK)
        picked = [fresh(f"picked{e}", [P, PACK, C1], F32, "q3" if e else None) for e in range(E1)]

        def window(t, first, count):
            return dc[t][:].indirect(entries(list1, first, count))

        for first in (0, P):
            for t in range(PACK):
                copy(False, picked[1][:, t, first : first + P], window(t, C1 + first, P))
        for t in range(PACK):
            count = P if t == PACK - 1 else C1
            for first in range(0, C1, count):
                cols = slice(first, first + count)
                nc.vector.tensor_tensor(picked[0][:, t, cols], window(t, first, count), keep[:, t, cols], MULT)

        codes = [fresh(f"da_codes{e}", [P, C1], U32) for e in range(E1)]
        scales = [fresh(f"da_scales{e}", [P, C1], U8) for e in range(E1)]
        result = {}

        def by_line(planes):
            return planes.rearrange("p t (c i) -> p c t i", i=LINE)

        def woven_da(name, count, tag=None):
            da = fresh(name, [P, count, PACK], BF16, tag)
            return da, da[:].rearrange("p (c i) t -> p c t i", i=LINE)

        def quantise_da(da, first):
            cols = slice(first % C1, first % C1 + da.shape[1])
            nc.vector.quantize_mx(
                out=codes[first // C1][:, cols].bitcast(FP8X4),
                scales=scales[first // C1][:, cols],
                in_=da[:].rearrange("p s t -> p (s t)"),
            )

        def product(first, count, blocks, number):
            e, cols = first // C1, slice(first % C1, first % C1 + count)
            acc = bank(f"out_acc{first}_{blocks[0]}", [P, len(blocks), count], number)
            for u, k in enumerate(blocks):
                column = e * T + k * P
                nc.tensor.matmul_mx(
                    out=acc[:, u, :],
                    lhsT=w1_w[:, 2 * column : 2 * (column + P)].bitcast(FP4X4),
                    lhsT_scale=w1_s[:, column : column + P],
                    rhs=codes[e][:, cols].bitcast(FP8X4),
                    rhs_scale=scales[e][:, cols],
                    start=True,
                    stop=True,
                )
            return acc, first, blocks, number

        def empty(made, on_vector):
            acc, first, blocks, number = made
            values = fresh(f"out_sums{first}_{blocks[0]}", list(acc.shape), F32)
            copy(on_vector, values[:], acc[:])
            return {(k, first): values[:, u, :] for u, k in enumerate(blocks)}

        def send(k, first, values, tag=None):
            if first == 0:
                result[k] = fresh(f"result{k}", [P, T], F32, tag)
            copy(k >= 2, result[k][:].indirect(entries(list1, first, values.shape[1])), values)
            if first == C1:
                nc.sync.dma_start(out[k * P : (k + 1) * P, :], result[k][:])

        lead = []
        for n in range(2):
            da, view = woven_da(f"da{n}", P)
            nc.vector.tensor_copy(view, by_line(picked[0][:, :, n * P : (n + 1) * P]))
            lead.append(da)
        for n in range(2):
            quantise_da(lead[n], n * P)
        done = empty(product(0, P, (0,), 7), False)
        done.update(empty(product(0, P, (1,), 0), False))
        done.update(empty(product(P, P, (0, 1), 3), False))
        own = [product(0, C1, (k,), number) for k, number in ((2, 1), (3, 4))]
        da, view = woven_da("da2", C1, "da0")
        for first in (0, P):
            lines = slice(first // LINE, (first + P) // LINE)
            nc.vector.tensor_tensor(view[:, lines], by_line(picked[1][:])[:, lines], by_line(keep[:, :, C1:T])[:, lines], MULT)
        done.update(empty(own[0], True))
        quantise_da(da, C1)
        done.update(empty(own[1], False))
        done.update(empty(product(C1, C1, (0,), 6), False))
        done.update(empty(product(C1, C1, (2,), 5), True))
        done.update(empty(product(C1, C1, (1,), 2), False))
        done.update(empty(product(C1, C1, (3,), 7), True))
        for first in (0, P):
            for k in (0, 1):
                send(k, first, done[k, first])
        for k in (2, 3):
            send(k, 0, done[k, 0])
        for k in (0, 2, 1, 3):
            send(k, C1, done[k, C1])
